import numpy as np
import ml_dtypes


def mxq(x, axis, fmt="e4m3"):
    dtype, down = {"e4m3": (ml_dtypes.float8_e4m3fn, 7), "e5m2": (ml_dtypes.float8_e5m2, 14)}[fmt]
    v = np.moveaxis(np.asarray(x, np.float32).astype(ml_dtypes.bfloat16).astype(np.float64), axis, -1)
    blocks = v.reshape(v.shape[:-1] + (-1, 32))
    amax = np.abs(blocks).max(-1, keepdims=True)
    byte = np.maximum(np.where(amax > 0, np.frexp(amax)[1] - 1 + 127, 0) - down, 1)
    scale = np.exp2(byte - 127.0)
    codes = (blocks / scale).astype(np.float32).astype(dtype).astype(np.float64)
    return np.moveaxis((codes * scale).reshape(v.shape), -1, axis)


WIDE = False


def mx_kscale(k):
    if not WIDE:
        return np.ones(k)
    levels = np.array([10, -10, 5, -5, 0])
    if k % 512:
        return np.exp2(np.random.permutation(np.resize(levels, k // 32))).repeat(32)
    a = np.empty((k // 512, 16))
    for p in range(k // 512):
        a[p, :8] = np.random.permutation(np.resize(levels, 8))
        for g in range(8):
            far = levels[np.abs(levels - a[p, g]) >= 10]
            a[p, g + 8] = far[np.random.randint(len(far))]
    return np.exp2(a.ravel()).repeat(32)


def f64(x):
    return np.asarray(x).astype(np.float64)


def striped(idx):
    return np.tile(np.asarray(idx).reshape(-1, 16).T, (8, 1)).astype(np.uint16)


def unstriped(offs):
    return offs[:16].T.reshape(-1).astype(np.int64)


E2M1 = np.array([0.0, 0.5, 1.0, 1.5, 2.0, 3.0, 4.0, 6.0, -0.0, -0.5, -1.0, -1.5, -2.0, -3.0, -4.0, -6.0])


def pack_weight(w, fmt):
    k, n = w.shape
    w = f64(np.asarray(w, np.float32).astype(ml_dtypes.bfloat16)).reshape(k // 32, 32, n)
    amax = np.abs(w).max(1)
    if fmt == "e4m3":
        byte = np.frexp(amax)[1] - 1 + 127 - 7
    else:
        mant, ex = np.frexp(amax / 6.0)
        byte = np.where(mant > 0.5, ex, ex - 1) + 127
    byte = np.clip(np.where(amax > 0, byte, 1), 1, 254)
    scaled = (w * np.exp2(127.0 - byte)[:, None, :]).reshape(k, n).astype(np.float32)
    by_word = np.ascontiguousarray(scaled.reshape(k // 512, 128, 4, n).transpose(0, 1, 3, 2))
    if fmt == "e4m3":
        words = by_word.astype(ml_dtypes.float8_e4m3fn).view(np.uint8)
    else:
        c = by_word.astype(ml_dtypes.float4_e2m1fn).view(np.uint8) & 0xF
        words = (c[..., 0::2] | (c[..., 1::2] << 4)).reshape(k // 512, 128, 2 * n)
    return np.ascontiguousarray(words), np.ascontiguousarray(byte.astype(np.uint8).reshape(k // 512, 16, n))


def unpack_weight(words, scales, fmt):
    g, _, n = scales.shape
    words = np.ascontiguousarray(words).reshape(g, 128, n, -1)
    if fmt == "e4m3":
        vals = words.view(ml_dtypes.float8_e4m3fn).astype(np.float64)
    else:
        nib = np.empty((g, 128, n, 4), np.uint8)
        nib[..., 0::2] = words & 0xF
        nib[..., 1::2] = words >> 4
        vals = E2M1[nib]
    vals = vals * np.repeat(np.exp2(scales.astype(np.float64) - 127.0), 8, axis=1)[..., None]
    return vals.transpose(0, 1, 3, 2).reshape(g * 512, n)


def bf(x):
    return np.asarray(x, np.float32).astype(ml_dtypes.bfloat16)


def planes(Y):
    r, m = Y.shape
    b = f64(bf(Y)).reshape(r // 32, 32, m)
    amax = np.abs(b).max(1)
    byte = np.clip(np.where(amax > 0, np.frexp(amax)[1] - 1 + 127 - 7, 1), 1, 254)
    codes = (b * np.exp2(127.0 - byte)[:, None, :]).reshape(r, m).astype(np.float32).astype(ml_dtypes.float8_e4m3fn).view(np.uint8)
    words = codes.reshape(r // 512, 128, 4, m).transpose(0, 1, 3, 2)
    return np.ascontiguousarray(words), np.ascontiguousarray(byte.astype(np.uint8).reshape(r // 512, 16, m))


D, T, I, Q, E = 512, 2048, 512, 256, 512


def setup_inputs():
    n = np.random.standard_normal
    idx = np.random.permutation(T)[:I]
    fd = mx_kscale(D)
    fi = mx_kscale(I)
    ti = np.ones(T)
    ti[idx] = fi
    keysp = pack_weight(n((D, T)) / fd[:, None], "e2m1")
    return {
        "query": (n((D, Q)) * 0.4 / np.sqrt(D) * fd[:, None]).astype(np.float32),
        "keys_words": keysp[0],
        "keys_scales": keysp[1],
        "c0": (np.random.uniform(0.5, 1.5, (Q, 1))).astype(np.float32),
        "c1": (np.random.uniform(-0.5, 0.7, (Q, 1))).astype(np.float32),
        "c2": (np.random.uniform(-0.5, 0.5, (Q, 1))).astype(np.float32),
        "size": (np.random.uniform(0.5, 2.0, (1, I)) * fi).astype(np.float32),
        "vals": (n((E, T)) / ti).astype(np.float32),
        "offs": striped(idx),
    }


def reference(query, keys_words, keys_scales, c0, c1, c2, size, vals, offs):
    idx = unstriped(offs)
    keysu = unpack_weight(keys_words, keys_scales, "e2m1")
    queryq = mxq(f64(query), 0, "e4m3")
    keysidxg = keysu[:, idx]
    a = queryq.T @ keysidxg
    a1 = np.pad(a, ((0, 0), (1, 0)))[:, :I]
    a2 = np.pad(a, ((0, 0), (2, 0)))[:, :I]
    s = f64(c0) * a + f64(c1) * a1 + f64(c2) * a2
    p = np.exp(s - np.max(s, axis=1, keepdims=True))
    w = p * f64(size) / np.sum(p, axis=1, keepdims=True)
    wt = w.T
    vt = f64(vals)[:, idx].T
    vtq = mxq(vt, 0, "e4m3")
    wtq = mxq(wt, 0, "e4m3")
    o = vtq.T @ wtq
    words, scales = planes(o)
    return o, words, scales

@@ -1,0 +1,212 @@
+from contextlib import ExitStack
+
+import concourse.mybir as mybir
+from concourse.masks import make_identity
+
+D, T, I, Q, E = 512, 2048, 512, 256, 512
+FLOPS = 2 * D * Q * I + 2 * I * E * Q
+
+F32 = mybir.dt.float32
+BF16 = mybir.dt.bfloat16
+I32 = mybir.dt.int32
+U32 = mybir.dt.uint32
+U16 = mybir.dt.uint16
+U8 = mybir.dt.uint8
+FP8X4 = mybir.dt.float8_e4m3fn_x4
+FP4X4 = mybir.dt.float4_e2m1fn_x4
+ALU = mybir.AluOpType
+ACT = mybir.ActivationFunctionType
+
+P = 128
+PACK = 4
+QB = Q // P
+
+
+def tile_attend_multitoken_pl_kernel(tc, query, keys_words, keys_scales, c0, c1, c2, size, vals, offs, out_0, out_1, out_2):
+    nc = tc.nc
+    with ExitStack() as ctx:
+        sb = ctx.enter_context(tc.tile_pool(name="sb", bufs=1))
+        ps = ctx.enter_context(tc.psum_pool(name="ps", bufs=1))
+
+        offsets = sb.tile([P, I // 16], U16, name="offsets")
+        nc.sync.dma_start(offsets[:], offs)
+
+        key_bytes = sb.tile([P, T], U8, name="key_bytes", align_bytes=64)
+        nc.vector.memset(key_bytes[:].bitcast(I32), 0)
+        key_words = sb.tile([P, T], U16, name="key_words", align_bytes=64)
+        nc.sync.dma_start(key_words[:].bitcast(I32), keys_words[0].bitcast(I32))
+        for quad in range(4):
+            nc.sync.dma_start(
+                key_bytes[32 * quad : 32 * quad + 4, :].bitcast(I32),
+                keys_scales[0, 4 * quad : 4 * quad + 4, :].bitcast(I32),
+            )
+        query_raw = sb.tile([P, PACK, Q], F32, name="query_raw", align_bytes=64)
+        nc.sync.dma_start(query_raw[:], query.rearrange("(p t) q -> p t q", t=PACK))
+        vals_rows = vals.rearrange("(m j) t -> j m t", j=PACK)
+        val_pool = [sb.tile([P, T], F32, name="val_pool%d" % j, align_bytes=64) for j in range(PACK)]
+        nc.sync.dma_start(val_pool[0][:], vals_rows[0])
+        factors = []
+        for name, src in (("c0", c0), ("c1", c1), ("c2", c2)):
+            col = sb.tile([P, QB], F32, name="factor_" + name)
+            nc.sync.dma_start(col[:], src.rearrange("(m b) o -> m (b o)", b=QB))
+            factors.append(col)
+        size_cols = sb.tile([P, PACK], F32, name="size_cols")
+        nc.sync.dma_start(size_cols[:], size.rearrange("o (m t) -> (o m) t", t=PACK))
+        for j in range(1, PACK):
+            nc.sync.dma_start(val_pool[j][:], vals_rows[j])
+
+        identity = sb.tile([P, P], F32, name="identity")
+        make_identity(nc, identity[:])
+
+        warm_in = sb.tile([P, 1], F32, name="warm_in")
+        warm_out = sb.tile([P, 1], F32, name="warm_out")
+        nc.vector.memset(warm_in[:], 0.0)
+        nc.scalar.activation(warm_out[:], warm_in[:], ACT.Exp)
+
+        kb_g = sb.tile([P, I], U8, name="kb_g", align_bytes=64)
+        nc.vector.tensor_copy(kb_g[:], key_bytes[:].indirect(offsets[:]))
+        kw_g = sb.tile([P, I], U16, name="kw_g", align_bytes=64)
+        nc.vector.tensor_copy(kw_g[:], key_words[:].indirect(offsets[:]))
+
+        query_bf = sb.tile([P, QB, P, PACK], BF16, name="query_bf", align_bytes=64)
+        nc.scalar.copy(query_bf[:], query_raw[:].rearrange("p t (m b) -> p b m t", b=QB))
+        q_codes = sb.tile([P, Q], U32, name="q_codes", align_bytes=64)
+        q_scales = sb.tile([P, Q], U8, name="q_scales", align_bytes=64)
+        nc.vector.quantize_mx(q_codes[:].bitcast(FP8X4), q_scales[:], query_bf[:].rearrange("p b m t -> p (b m t)"))
+
+        size_ps = ps.tile([P, PACK, P], F32, name="size_ps")
+        for t in range(PACK):
+            nc.tensor.transpose(size_ps[:, t, :], size_cols[:, t : t + 1].to_broadcast([P, P]), identity[:])
+
+        scores = []
+        mixed = []
+        for b in range(QB):
+            cols = slice(b * P, (b + 1) * P)
+            acc = ps.tile([P, I], F32, name="scores%d" % b)
+            nc.tensor.matmul_mx(
+                acc[:],
+                lhsT=q_codes[:, cols].bitcast(FP8X4),
+                lhsT_scale=q_scales[:, cols],
+                rhs=kw_g[:].bitcast(FP4X4),
+                rhs_scale=kb_g[:],
+                start=True,
+                stop=True,
+            )
+            scores.append(acc)
+            s = sb.tile([P, I], F32, name="mixed%d" % b, align_bytes=64)
+            nc.scalar.activation(s[:], acc[:], ACT.Copy, scale=factors[0][:, b : b + 1])
+            mixed.append(s)
+
+        v_codes = [sb.tile([P, P], U32, name="v_codes%d" % j, align_bytes=64) for j in range(PACK)]
+        v_scales = [sb.tile([P, P], U8, name="v_scales%d" % j, align_bytes=64) for j in range(PACK)]
+        v_bf = [sb.tile([P, P, PACK], BF16, name="v_bf%d" % j, align_bytes=64) for j in range(PACK)]
+
+        def gather_and_turn(j):
+            picked = sb.tile([P, I], BF16, name="picked%d" % j, align_bytes=64)
+            nc.vector.tensor_copy(picked[:], val_pool[j][:].indirect(offsets[:]))
+            words = picked[:].bitcast(F32)
+            turned = ps.tile([P, 2, P], F32, name="turned", tag="turned", bufs=2)
+            for u in range(2):
+                nc.tensor.transpose(turned[:, u, :], words[:, u : I // 2 : 2], identity[:])
+            nc.scalar.copy(v_bf[j][:].bitcast(F32), turned[:].rearrange("p u m -> p m u"))
+
+        def quantize_values(j):
+            nc.vector.quantize_mx(v_codes[j][:].bitcast(FP8X4), v_scales[j][:], v_bf[j][:].rearrange("p m t -> p (m t)"))
+
+        gather_and_turn(0)
+        for shift in (1, 2):
+            for b in range(QB):
+                nc.vector.scalar_tensor_tensor(
+                    mixed[b][:, shift:I],
+                    scores[b][:, 0 : I - shift],
+                    factors[shift][:, b : b + 1],
+                    mixed[b][:, shift:I],
+                    ALU.mult,
+                    ALU.add,
+                )
+        probs = []
+        sums = []
+        for b in range(QB):
+            neg_max = sb.tile([P, 1], F32, name="neg_max%d" % b)
+            nc.vector.tensor_reduce(neg_max[:], mixed[b][:], mybir.AxisListType.X, ALU.max, negate=True)
+            prob = sb.tile([P, I], F32, name="prob%d" % b, align_bytes=64)
+            total = sb.tile([P, 1], F32, name="total%d" % b)
+            nc.scalar.activation(prob[:], mixed[b][:], ACT.Exp, bias=neg_max[:], accum_out=total[:])
+            probs.append(prob)
+            sums.append(total)
+        gather_and_turn(1)
+        quantize_values(0)
+
+        w_turned = ps.tile([P, QB, 2, P], F32, name="w_turned")
+        inverses = []
+        for b in range(QB):
+            inverse = sb.tile([P, 1], F32, name="inverse%d" % b)
+            nc.vector.reciprocal(inverse[:], sums[b][:])
+            inverses.append(inverse)
+        for b in range(QB):
+            weights = sb.tile([P, I], BF16, name="weights%d" % b, align_bytes=64)
+            nc.vector.scalar_tensor_tensor(
+                weights[:].rearrange("p (m t) -> p m t", t=PACK),
+                probs[b][:].rearrange("p (m t) -> p m t", t=PACK),
+                inverses[b][:],
+                size_ps[:].rearrange("p t m -> p m t"),
+                ALU.mult,
+                ALU.mult,
+            )
+            words = weights[:].bitcast(F32)
+            for u in range(2):
+                nc.tensor.transpose(w_turned[:, b, u, :], words[:, u : I // 2 : 2], identity[:])
+        w_bf = sb.tile([P, Q, PACK], BF16, name="w_bf", align_bytes=64)
+        nc.scalar.copy(
+            w_bf[:].bitcast(F32).rearrange("p (m b) u -> p m b u", b=QB),
+            w_turned[:].rearrange("p b u m -> p m b u"),
+        )
+        gather_and_turn(2)
+        quantize_values(1)
+        w_codes = sb.tile([P, Q], U32, name="w_codes", align_bytes=64)
+        w_scales = sb.tile([P, Q], U8, name="w_scales", align_bytes=64)
+        nc.vector.quantize_mx(w_codes[:].bitcast(FP8X4), w_scales[:], w_bf[:].rearrange("p q t -> p (q t)"))
+        quantize_values(2)
+        gather_and_turn(3)
+        quantize_values(3)
+
+        result = [ps.tile([P, PACK, P], F32, name="result%d" % h) for h in range(QB)]
+        out_rows = out_0.rearrange("(p j) q -> p j q", j=PACK)
+        early = sb.tile([P, PACK - 1, Q], F32, name="early", align_bytes=64)
+        late = sb.tile([P, Q], F32, name="late", align_bytes=64)
+
+        def multiply(j):
+            for h in range(QB):
+                cols = slice(h * P, (h + 1) * P)
+                nc.tensor.matmul_mx(
+                    result[h][:, j, :],
+                    lhsT=v_codes[j][:].bitcast(FP8X4),
+                    lhsT_scale=v_scales[j][:],
+                    rhs=w_codes[:, cols].bitcast(FP8X4),
+                    rhs_scale=w_scales[:, cols],
+                    start=True,
+                    stop=True,
+                )
+
+        for j in range(PACK - 1):
+            multiply(j)
+        for h in range(QB):
+            nc.scalar.copy(early[:, :, h * P : (h + 1) * P], result[h][:, 0 : PACK - 1, :])
+        nc.sync.dma_start(out_rows[:, 0 : PACK - 1, :], early[:])
+        multiply(PACK - 1)
+
+        out_bf = sb.tile([P, Q, PACK], BF16, name="out_bf", align_bytes=64)
+        nc.vector.tensor_copy(out_bf[:, 0:P, :], result[0][:].rearrange("p j n -> p n j"))
+        nc.scalar.copy(out_bf[:, P:Q, :], result[1][:].rearrange("p j n -> p n j"))
+        o_codes = sb.tile([P, Q], U32, name="o_codes", align_bytes=64)
+        o_scales = sb.tile([P, Q], U8, name="o_scales", align_bytes=64)
+        nc.vector.quantize_mx(o_codes[:].bitcast(FP8X4), o_scales[:], out_bf[:].rearrange("p q j -> p (q j)"))
+        for h in range(QB):
+            nc.scalar.copy(late[:, h * P : (h + 1) * P], result[h][:, PACK - 1, :])
+        nc.sync.dma_start(out_1[0].rearrange("p c r -> p (c r)").bitcast(I32), o_codes[:].bitcast(I32))
+        for quad in range(4):
+            nc.sync.dma_start(
+                out_2[0, 4 * quad : 4 * quad + 4, :].bitcast(I32),
+                o_scales[32 * quad : 32 * quad + 4, :].bitcast(I32),
+            )
+        nc.scalar.dma_start(out_rows[:, PACK - 1, :], late[:])

@@ -31,25 +31,29 @@ def tile_attend_multitoken_pl_kernel(tc, query, keys_words, keys_scales, c0, c1,
         offsets = sb.tile([P, I // 16], U16, name="offsets")
         nc.sync.dma_start(offsets[:], offs)
 
+        factors = [sb.tile([P, QB], F32, name="factor%d" % k, tag="factor%d" % k, align_bytes=64) for k in range(3)]
+
+        def load_factor(k, src, queue):
+            with nc.allow_non_contiguous_dma(reason="one factor a partition and block"):
+                queue.dma_start(factors[k][:], src.rearrange("(b m) o -> m (b o)", b=QB))
+
         key_bytes = sb.tile([P, T], U8, name="key_bytes", align_bytes=64)
         nc.vector.memset(key_bytes[:].bitcast(I32), 0)
         key_words = sb.tile([P, T], U16, name="key_words", align_bytes=64)
         nc.sync.dma_start(key_words[:].bitcast(I32), keys_words[0].bitcast(I32))
+        query_raw = sb.tile([P, PACK, Q], F32, name="query_raw", align_bytes=64)
+        nc.sync.dma_start(query_raw[:], query.rearrange("(p t) q -> p t q", t=PACK))
         for quad in range(4):
             nc.sync.dma_start(
                 key_bytes[32 * quad : 32 * quad + 4, :].bitcast(I32),
                 keys_scales[0, 4 * quad : 4 * quad + 4, :].bitcast(I32),
             )
-        query_raw = sb.tile([P, PACK, Q], F32, name="query_raw", align_bytes=64)
-        nc.sync.dma_start(query_raw[:], query.rearrange("(p t) q -> p t q", t=PACK))
         vals_rows = vals.rearrange("(m j) t -> j m t", j=PACK)
-        val_pool = [sb.tile([P, T], F32, name="val_pool%d" % j, align_bytes=64) for j in range(PACK)]
+        val_pool = [sb.tile([P, T], F32, name="val_pool%d" % j, tag="pool%d" % j, align_bytes=64) for j in range(PACK)]
         nc.sync.dma_start(val_pool[0][:], vals_rows[0])
-        factors = []
-        for name, src in (("c0", c0), ("c1", c1), ("c2", c2)):
-            col = sb.tile([P, QB], F32, name="factor_" + name)
-            nc.sync.dma_start(col[:], src.rearrange("(m b) o -> m (b o)", b=QB))
-            factors.append(col)
+        load_factor(0, c0, nc.sync)
+        load_factor(1, c1, nc.sync)
+        load_factor(2, c2, nc.sync)
         size_cols = sb.tile([P, PACK], F32, name="size_cols")
         nc.sync.dma_start(size_cols[:], size.rearrange("o (m t) -> (o m) t", t=PACK))
         for j in range(1, PACK):
@@ -58,21 +62,16 @@ def tile_attend_multitoken_pl_kernel(tc, query, keys_words, keys_scales, c0, c1,
         identity = sb.tile([P, P], F32, name="identity")
         make_identity(nc, identity[:])
 
-        warm_in = sb.tile([P, 1], F32, name="warm_in")
-        warm_out = sb.tile([P, 1], F32, name="warm_out")
-        nc.vector.memset(warm_in[:], 0.0)
-        nc.scalar.activation(warm_out[:], warm_in[:], ACT.Exp)
-
-        kb_g = sb.tile([P, I], U8, name="kb_g", align_bytes=64)
-        nc.vector.tensor_copy(kb_g[:], key_bytes[:].indirect(offsets[:]))
         kw_g = sb.tile([P, I], U16, name="kw_g", align_bytes=64)
         nc.vector.tensor_copy(kw_g[:], key_words[:].indirect(offsets[:]))
+        kb_g = sb.tile([P, I], U8, name="kb_g", align_bytes=64)
+        nc.vector.tensor_copy(kb_g[:], key_bytes[:].indirect(offsets[:]))
 
-        query_bf = sb.tile([P, QB, P, PACK], BF16, name="query_bf", align_bytes=64)
-        nc.scalar.copy(query_bf[:], query_raw[:].rearrange("p t (m b) -> p b m t", b=QB))
         q_codes = sb.tile([P, Q], U32, name="q_codes", align_bytes=64)
         q_scales = sb.tile([P, Q], U8, name="q_scales", align_bytes=64)
-        nc.vector.quantize_mx(q_codes[:].bitcast(FP8X4), q_scales[:], query_bf[:].rearrange("p b m t -> p (b m t)"))
+        query_bf = sb.tile([P, Q, PACK], BF16, name="query_bf", align_bytes=64)
+        nc.scalar.activation(query_bf[:], query_raw[:].rearrange("p t q -> p q t"), ACT.Copy)
+        nc.vector.quantize_mx(q_codes[:].bitcast(FP8X4), q_scales[:], query_bf[:].rearrange("p q t -> p (q t)"))
 
         size_ps = ps.tile([P, PACK, P], F32, name="size_ps")
         for t in range(PACK):
@@ -82,7 +81,7 @@ def tile_attend_multitoken_pl_kernel(tc, query, keys_words, keys_scales, c0, c1,
         mixed = []
         for b in range(QB):
             cols = slice(b * P, (b + 1) * P)
-            acc = ps.tile([P, I], F32, name="scores%d" % b)
+            acc = ps.tile([P, I], F32, name="scores%d" % b, tag="scores%d" % b)
             nc.tensor.matmul_mx(
                 acc[:],
                 lhsT=q_codes[:, cols].bitcast(FP8X4),
@@ -93,25 +92,22 @@ def tile_attend_multitoken_pl_kernel(tc, query, keys_words, keys_scales, c0, c1,
                 stop=True,
             )
             scores.append(acc)
-            s = sb.tile([P, I], F32, name="mixed%d" % b, align_bytes=64)
+            s = sb.tile([P, I], F32, name="mixed%d" % b, tag="mixed%d" % b, align_bytes=64)
             nc.scalar.activation(s[:], acc[:], ACT.Copy, scale=factors[0][:, b : b + 1])
             mixed.append(s)
 
-        v_codes = [sb.tile([P, P], U32, name="v_codes%d" % j, align_bytes=64) for j in range(PACK)]
-        v_scales = [sb.tile([P, P], U8, name="v_scales%d" % j, align_bytes=64) for j in range(PACK)]
-        v_bf = [sb.tile([P, P, PACK], BF16, name="v_bf%d" % j, align_bytes=64) for j in range(PACK)]
+        stage_a = sb.tile([P, (Q + 2 * P) * PACK], BF16, name="stage_a", align_bytes=64)
+        stage_b = [sb.tile([P, P * PACK], BF16, name="stage_b%d" % j, align_bytes=64) for j in range(2)]
+        v_bf = [stage_a[:, (Q + j * P) * PACK : (Q + (j + 1) * P) * PACK] for j in range(2)] + [t[:] for t in stage_b]
 
         def gather_and_turn(j):
             picked = sb.tile([P, I], BF16, name="picked%d" % j, align_bytes=64)
             nc.vector.tensor_copy(picked[:], val_pool[j][:].indirect(offsets[:]))
             words = picked[:].bitcast(F32)
-            turned = ps.tile([P, 2, P], F32, name="turned", tag="turned", bufs=2)
+            turned = ps.tile([P, 2, P], F32, name="turned", tag="turned", bufs=3)
             for u in range(2):
                 nc.tensor.transpose(turned[:, u, :], words[:, u : I // 2 : 2], identity[:])
-            nc.scalar.copy(v_bf[j][:].bitcast(F32), turned[:].rearrange("p u m -> p m u"))
-
-        def quantize_values(j):
-            nc.vector.quantize_mx(v_codes[j][:].bitcast(FP8X4), v_scales[j][:], v_bf[j][:].rearrange("p m t -> p (m t)"))
+            nc.scalar.copy(v_bf[j].bitcast(F32).rearrange("p (m u) -> p m u", u=2), turned[:].rearrange("p u m -> p m u"))
 
         gather_and_turn(0)
         for shift in (1, 2):
@@ -125,75 +121,77 @@ def tile_attend_multitoken_pl_kernel(tc, query, keys_words, keys_scales, c0, c1,
                     ALU.add,
                 )
         probs = []
-        sums = []
+        sums = sb.tile([P, QB], F32, name="sums")
         for b in range(QB):
             neg_max = sb.tile([P, 1], F32, name="neg_max%d" % b)
             nc.vector.tensor_reduce(neg_max[:], mixed[b][:], mybir.AxisListType.X, ALU.max, negate=True)
             prob = sb.tile([P, I], F32, name="prob%d" % b, align_bytes=64)
-            total = sb.tile([P, 1], F32, name="total%d" % b)
-            nc.scalar.activation(prob[:], mixed[b][:], ACT.Exp, bias=neg_max[:], accum_out=total[:])
+            nc.scalar.activation(prob[:], mixed[b][:], ACT.Exp, bias=neg_max[:], accum_out=sums[:, b : b + 1])
             probs.append(prob)
-            sums.append(total)
         gather_and_turn(1)
-        quantize_values(0)
 
-        w_turned = ps.tile([P, QB, 2, P], F32, name="w_turned")
-        inverses = []
+        inverses = sb.tile([P, QB], F32, name="inverses")
+        nc.vector.reciprocal(inverses[:], sums[:])
+        weights = sb.tile([P, QB, I], BF16, name="weights", tag="pool1", align_bytes=64)
         for b in range(QB):
-            inverse = sb.tile([P, 1], F32, name="inverse%d" % b)
-            nc.vector.reciprocal(inverse[:], sums[b][:])
-            inverses.append(inverse)
-        for b in range(QB):
-            weights = sb.tile([P, I], BF16, name="weights%d" % b, align_bytes=64)
             nc.vector.scalar_tensor_tensor(
-                weights[:].rearrange("p (m t) -> p m t", t=PACK),
+                weights[:, b, :].rearrange("p (m t) -> p m t", t=PACK),
                 probs[b][:].rearrange("p (m t) -> p m t", t=PACK),
-                inverses[b][:],
+                inverses[:, b : b + 1],
                 size_ps[:].rearrange("p t m -> p m t"),
                 ALU.mult,
                 ALU.mult,
             )
-            words = weights[:].bitcast(F32)
+            words = weights[:, b, :].bitcast(F32)
+            w_turned = ps.tile([P, 2, P], F32, name="w_turned", tag="scores%d" % b)
             for u in range(2):
-                nc.tensor.transpose(w_turned[:, b, u, :], words[:, u : I // 2 : 2], identity[:])
-        w_bf = sb.tile([P, Q, PACK], BF16, name="w_bf", align_bytes=64)
-        nc.scalar.copy(
-            w_bf[:].bitcast(F32).rearrange("p (m b) u -> p m b u", b=QB),
-            w_turned[:].rearrange("p b u m -> p m b u"),
-        )
+                nc.tensor.transpose(w_turned[:, u, :], words[:, u : I // 2 : 2], identity[:])
+            nc.scalar.copy(
+                stage_a[:, b * P * PACK : (b + 1) * P * PACK].bitcast(F32).rearrange("p (m u) -> p m u", u=2),
+                w_turned[:].rearrange("p u m -> p m u"),
+            )
         gather_and_turn(2)
-        quantize_values(1)
-        w_codes = sb.tile([P, Q], U32, name="w_codes", align_bytes=64)
-        w_scales = sb.tile([P, Q], U8, name="w_scales", align_bytes=64)
-        nc.vector.quantize_mx(w_codes[:].bitcast(FP8X4), w_scales[:], w_bf[:].rearrange("p q t -> p (q t)"))
-        quantize_values(2)
+        codes_a = sb.tile([P, Q + 2 * P], U32, name="codes_a", tag="pool2", align_bytes=64)
+        scales_a = sb.tile([P, Q + 2 * P], U8, name="scales_a", align_bytes=64)
+        nc.vector.quantize_mx(codes_a[:].bitcast(FP8X4), scales_a[:], stage_a[:])
         gather_and_turn(3)
-        quantize_values(3)
+        codes_2 = sb.tile([P, P], U32, name="codes_2", tag="pool3", align_bytes=64)
+        scales_2 = sb.tile([P, P], U8, name="scales_2", align_bytes=64)
+        nc.vector.quantize_mx(codes_2[:].bitcast(FP8X4), scales_2[:], v_bf[2])
+        codes_3 = sb.tile([P, P], U32, name="codes_3", align_bytes=64)
+        scales_3 = sb.tile([P, P], U8, name="scales_3", align_bytes=64)
+        nc.vector.quantize_mx(codes_3[:].bitcast(FP8X4), scales_3[:], v_bf[3])
+        v_codes = [codes_a[:, Q : Q + P], codes_a[:, Q + P : Q + 2 * P], codes_2[:], codes_3[:]]
+        v_scales = [scales_a[:, Q : Q + P], scales_a[:, Q + P : Q + 2 * P], scales_2[:], scales_3[:]]
 
         result = [ps.tile([P, PACK, P], F32, name="result%d" % h) for h in range(QB)]
         out_rows = out_0.rearrange("(p j) q -> p j q", j=PACK)
-        early = sb.tile([P, PACK - 1, Q], F32, name="early", align_bytes=64)
-        late = sb.tile([P, Q], F32, name="late", align_bytes=64)
+        out_sb = [sb.tile([P, n, Q], F32, name="out_sb%d" % k, align_bytes=64) for k, n in enumerate((2, 1, 1))]
 
         def multiply(j):
             for h in range(QB):
                 cols = slice(h * P, (h + 1) * P)
                 nc.tensor.matmul_mx(
                     result[h][:, j, :],
-                    lhsT=v_codes[j][:].bitcast(FP8X4),
-                    lhsT_scale=v_scales[j][:],
-                    rhs=w_codes[:, cols].bitcast(FP8X4),
-                    rhs_scale=w_scales[:, cols],
+                    lhsT=v_codes[j].bitcast(FP8X4),
+                    lhsT_scale=v_scales[j],
+                    rhs=codes_a[:, cols].bitcast(FP8X4),
+                    rhs_scale=scales_a[:, cols],
                     start=True,
                     stop=True,
                 )
 
-        for j in range(PACK - 1):
-            multiply(j)
-        for h in range(QB):
-            nc.scalar.copy(early[:, :, h * P : (h + 1) * P], result[h][:, 0 : PACK - 1, :])
-        nc.sync.dma_start(out_rows[:, 0 : PACK - 1, :], early[:])
-        multiply(PACK - 1)
+        def store_rows(k, first, end, queue):
+            for h in range(QB):
+                nc.scalar.copy(out_sb[k][:, :, h * P : (h + 1) * P], result[h][:, first:end, :])
+            queue.dma_start(out_rows[:, first:end, :], out_sb[k][:])
+
+        multiply(0)
+        multiply(1)
+        store_rows(0, 0, 2, nc.sync)
+        multiply(2)
+        store_rows(1, 2, 3, nc.sync)
+        multiply(3)
 
         out_bf = sb.tile([P, Q, PACK], BF16, name="out_bf", align_bytes=64)
         nc.vector.tensor_copy(out_bf[:, 0:P, :], result[0][:].rearrange("p j n -> p n j"))
@@ -201,12 +199,11 @@ def tile_attend_multitoken_pl_kernel(tc, query, keys_words, keys_scales, c0, c1,
         o_codes = sb.tile([P, Q], U32, name="o_codes", align_bytes=64)
         o_scales = sb.tile([P, Q], U8, name="o_scales", align_bytes=64)
         nc.vector.quantize_mx(o_codes[:].bitcast(FP8X4), o_scales[:], out_bf[:].rearrange("p q j -> p (q j)"))
-        for h in range(QB):
-            nc.scalar.copy(late[:, h * P : (h + 1) * P], result[h][:, PACK - 1, :])
+        store_rows(2, 3, 4, nc.scalar)
         nc.sync.dma_start(out_1[0].rearrange("p c r -> p (c r)").bitcast(I32), o_codes[:].bitcast(I32))
         for quad in range(4):
-            nc.sync.dma_start(
+            queue = nc.sync if quad < 3 else nc.scalar
+            queue.dma_start(
                 out_2[0, 4 * quad : 4 * quad + 4, :].bitcast(I32),
                 o_scales[32 * quad : 32 * quad + 4, :].bitcast(I32),
             )
-        nc.scalar.dma_start(out_rows[:, PACK - 1, :], late[:])

@@ -19,7 +19,23 @@ ACT = mybir.ActivationFunctionType
 
 P = 128
 PACK = 4
-QB = Q // P
+PAIRS = PACK // 2
+BLOCKS = Q // P
+TAPS = 3
+QUADRANTS = 4
+TURN_BANKS = 3
+
+
+def block_cols(b):
+    return slice(b * P, (b + 1) * P)
+
+
+def scale_partitions(quadrant):
+    return slice(32 * quadrant, 32 * quadrant + 4)
+
+
+def scale_rows(quadrant):
+    return slice(4 * quadrant, 4 * quadrant + 4)
 
 
 def tile_attend_multitoken_pl_kernel(tc, query, keys_words, keys_scales, c0, c1, c2, size, vals, offs, out_0, out_1, out_2):
@@ -31,29 +47,24 @@ def tile_attend_multitoken_pl_kernel(tc, query, keys_words, keys_scales, c0, c1,
         offsets = sb.tile([P, I // 16], U16, name="offsets")
         nc.sync.dma_start(offsets[:], offs)
 
-        factors = [sb.tile([P, QB], F32, name="factor%d" % k, tag="factor%d" % k, align_bytes=64) for k in range(3)]
-
-        def load_factor(k, src, queue):
-            with nc.allow_non_contiguous_dma(reason="one factor a partition and block"):
-                queue.dma_start(factors[k][:], src.rearrange("(b m) o -> m (b o)", b=QB))
-
         key_bytes = sb.tile([P, T], U8, name="key_bytes", align_bytes=64)
         nc.vector.memset(key_bytes[:].bitcast(I32), 0)
         key_words = sb.tile([P, T], U16, name="key_words", align_bytes=64)
         nc.sync.dma_start(key_words[:].bitcast(I32), keys_words[0].bitcast(I32))
         query_raw = sb.tile([P, PACK, Q], F32, name="query_raw", align_bytes=64)
         nc.sync.dma_start(query_raw[:], query.rearrange("(p t) q -> p t q", t=PACK))
-        for quad in range(4):
+        for quadrant in range(QUADRANTS):
             nc.sync.dma_start(
-                key_bytes[32 * quad : 32 * quad + 4, :].bitcast(I32),
-                keys_scales[0, 4 * quad : 4 * quad + 4, :].bitcast(I32),
+                key_bytes[scale_partitions(quadrant), :].bitcast(I32),
+                keys_scales[0, scale_rows(quadrant), :].bitcast(I32),
             )
         vals_rows = vals.rearrange("(m j) t -> j m t", j=PACK)
         val_pool = [sb.tile([P, T], F32, name="val_pool%d" % j, tag="pool%d" % j, align_bytes=64) for j in range(PACK)]
         nc.sync.dma_start(val_pool[0][:], vals_rows[0])
-        load_factor(0, c0, nc.sync)
-        load_factor(1, c1, nc.sync)
-        load_factor(2, c2, nc.sync)
+        factors = [sb.tile([P, BLOCKS], F32, name="factor%d" % k, align_bytes=64) for k in range(TAPS)]
+        for factor, source in zip(factors, (c0, c1, c2)):
+            with nc.allow_non_contiguous_dma(reason="one factor a partition and block"):
+                nc.sync.dma_start(factor[:], source.rearrange("(b m) o -> m (b o)", b=BLOCKS))
         size_cols = sb.tile([P, PACK], F32, name="size_cols")
         nc.sync.dma_start(size_cols[:], size.rearrange("o (m t) -> (o m) t", t=PACK))
         for j in range(1, PACK):
@@ -62,10 +73,10 @@ def tile_attend_multitoken_pl_kernel(tc, query, keys_words, keys_scales, c0, c1,
         identity = sb.tile([P, P], F32, name="identity")
         make_identity(nc, identity[:])
 
-        kw_g = sb.tile([P, I], U16, name="kw_g", align_bytes=64)
-        nc.vector.tensor_copy(kw_g[:], key_words[:].indirect(offsets[:]))
-        kb_g = sb.tile([P, I], U8, name="kb_g", align_bytes=64)
-        nc.vector.tensor_copy(kb_g[:], key_bytes[:].indirect(offsets[:]))
+        listed_words = sb.tile([P, I], U16, name="listed_words", align_bytes=64)
+        nc.vector.tensor_copy(listed_words[:], key_words[:].indirect(offsets[:]))
+        listed_bytes = sb.tile([P, I], U8, name="listed_bytes", align_bytes=64)
+        nc.vector.tensor_copy(listed_bytes[:], key_bytes[:].indirect(offsets[:]))
 
         q_codes = sb.tile([P, Q], U32, name="q_codes", align_bytes=64)
         q_scales = sb.tile([P, Q], U8, name="q_scales", align_bytes=64)
@@ -79,61 +90,66 @@ def tile_attend_multitoken_pl_kernel(tc, query, keys_words, keys_scales, c0, c1,
 
         scores = []
         mixed = []
-        for b in range(QB):
-            cols = slice(b * P, (b + 1) * P)
-            acc = ps.tile([P, I], F32, name="scores%d" % b, tag="scores%d" % b)
+        for b in range(BLOCKS):
+            score = ps.tile([P, I], F32, name="score%d" % b, tag="block%d" % b)
             nc.tensor.matmul_mx(
-                acc[:],
-                lhsT=q_codes[:, cols].bitcast(FP8X4),
-                lhsT_scale=q_scales[:, cols],
-                rhs=kw_g[:].bitcast(FP4X4),
-                rhs_scale=kb_g[:],
+                score[:],
+                lhsT=q_codes[:, block_cols(b)].bitcast(FP8X4),
+                lhsT_scale=q_scales[:, block_cols(b)],
+                rhs=listed_words[:].bitcast(FP4X4),
+                rhs_scale=listed_bytes[:],
                 start=True,
                 stop=True,
             )
-            scores.append(acc)
-            s = sb.tile([P, I], F32, name="mixed%d" % b, tag="mixed%d" % b, align_bytes=64)
-            nc.scalar.activation(s[:], acc[:], ACT.Copy, scale=factors[0][:, b : b + 1])
-            mixed.append(s)
+            scores.append(score)
+            mix = sb.tile([P, I], F32, name="mixed%d" % b, align_bytes=64)
+            nc.scalar.activation(mix[:], score[:], ACT.Copy, scale=factors[0][:, b : b + 1])
+            mixed.append(mix)
 
-        stage_a = sb.tile([P, (Q + 2 * P) * PACK], BF16, name="stage_a", align_bytes=64)
-        stage_b = [sb.tile([P, P * PACK], BF16, name="stage_b%d" % j, align_bytes=64) for j in range(2)]
-        v_bf = [stage_a[:, (Q + j * P) * PACK : (Q + (j + 1) * P) * PACK] for j in range(2)] + [t[:] for t in stage_b]
+        joint_bf = sb.tile([P, (Q + 2 * P) * PACK], BF16, name="joint_bf", align_bytes=64)
+        later_bf = [sb.tile([P, P * PACK], BF16, name="later_bf%d" % j, align_bytes=64) for j in range(2, PACK)]
+        weights_bf = [joint_bf[:, b * P * PACK : (b + 1) * P * PACK] for b in range(BLOCKS)]
+        values_bf = [joint_bf[:, (Q + j * P) * PACK : (Q + (j + 1) * P) * PACK] for j in range(2)]
+        values_bf = values_bf + [tile[:] for tile in later_bf]
 
-        def gather_and_turn(j):
+        def turn(rows_bf, bank, target):
+            words = rows_bf.bitcast(F32)
+            for u in range(PAIRS):
+                nc.tensor.transpose(bank[:, u, :], words[:, u : I // 2 : PAIRS], identity[:])
+            nc.scalar.copy(target.bitcast(F32).rearrange("p (m u) -> p m u", u=PAIRS), bank[:].rearrange("p u m -> p m u"))
+
+        def gather_values(j):
             picked = sb.tile([P, I], BF16, name="picked%d" % j, align_bytes=64)
             nc.vector.tensor_copy(picked[:], val_pool[j][:].indirect(offsets[:]))
-            words = picked[:].bitcast(F32)
-            turned = ps.tile([P, 2, P], F32, name="turned", tag="turned", bufs=3)
-            for u in range(2):
-                nc.tensor.transpose(turned[:, u, :], words[:, u : I // 2 : 2], identity[:])
-            nc.scalar.copy(v_bf[j].bitcast(F32).rearrange("p (m u) -> p m u", u=2), turned[:].rearrange("p u m -> p m u"))
+            bank = ps.tile([P, PAIRS, P], F32, name="turned", tag="turned", bufs=TURN_BANKS)
+            turn(picked[:], bank, values_bf[j])
 
-        gather_and_turn(0)
-        for shift in (1, 2):
-            for b in range(QB):
+        gather_values(0)
+
+        for tap in range(1, TAPS):
+            for b in range(BLOCKS):
                 nc.vector.scalar_tensor_tensor(
-                    mixed[b][:, shift:I],
-                    scores[b][:, 0 : I - shift],
-                    factors[shift][:, b : b + 1],
-                    mixed[b][:, shift:I],
+                    mixed[b][:, tap:I],
+                    scores[b][:, 0 : I - tap],
+                    factors[tap][:, b : b + 1],
+                    mixed[b][:, tap:I],
                     ALU.mult,
                     ALU.add,
                 )
         probs = []
-        sums = sb.tile([P, QB], F32, name="sums")
-        for b in range(QB):
+        sums = sb.tile([P, BLOCKS], F32, name="sums")
+        for b in range(BLOCKS):
             neg_max = sb.tile([P, 1], F32, name="neg_max%d" % b)
             nc.vector.tensor_reduce(neg_max[:], mixed[b][:], mybir.AxisListType.X, ALU.max, negate=True)
             prob = sb.tile([P, I], F32, name="prob%d" % b, align_bytes=64)
             nc.scalar.activation(prob[:], mixed[b][:], ACT.Exp, bias=neg_max[:], accum_out=sums[:, b : b + 1])
             probs.append(prob)
-        gather_and_turn(1)
 
-        inverses = sb.tile([P, QB], F32, name="inverses")
+        gather_values(1)
+        inverses = sb.tile([P, BLOCKS], F32, name="inverses")
         nc.vector.reciprocal(inverses[:], sums[:])
-        weights = sb.tile([P, QB, I], BF16, name="weights", tag="pool1", align_bytes=64)
-        for b in range(QB):
+        weights = sb.tile([P, BLOCKS, I], BF16, name="weights", tag="pool1", align_bytes=64)
+        for b in range(BLOCKS):
             nc.vector.scalar_tensor_tensor(
                 weights[:, b, :].rearrange("p (m t) -> p m t", t=PACK),
                 probs[b][:].rearrange("p (m t) -> p m t", t=PACK),
@@ -142,68 +158,70 @@ def tile_attend_multitoken_pl_kernel(tc, query, keys_words, keys_scales, c0, c1,
                 ALU.mult,
                 ALU.mult,
             )
-            words = weights[:, b, :].bitcast(F32)
-            w_turned = ps.tile([P, 2, P], F32, name="w_turned", tag="scores%d" % b)
-            for u in range(2):
-                nc.tensor.transpose(w_turned[:, u, :], words[:, u : I // 2 : 2], identity[:])
-            nc.scalar.copy(
-                stage_a[:, b * P * PACK : (b + 1) * P * PACK].bitcast(F32).rearrange("p (m u) -> p m u", u=2),
-                w_turned[:].rearrange("p u m -> p m u"),
-            )
-        gather_and_turn(2)
-        codes_a = sb.tile([P, Q + 2 * P], U32, name="codes_a", tag="pool2", align_bytes=64)
-        scales_a = sb.tile([P, Q + 2 * P], U8, name="scales_a", align_bytes=64)
-        nc.vector.quantize_mx(codes_a[:].bitcast(FP8X4), scales_a[:], stage_a[:])
-        gather_and_turn(3)
-        codes_2 = sb.tile([P, P], U32, name="codes_2", tag="pool3", align_bytes=64)
-        scales_2 = sb.tile([P, P], U8, name="scales_2", align_bytes=64)
-        nc.vector.quantize_mx(codes_2[:].bitcast(FP8X4), scales_2[:], v_bf[2])
-        codes_3 = sb.tile([P, P], U32, name="codes_3", align_bytes=64)
-        scales_3 = sb.tile([P, P], U8, name="scales_3", align_bytes=64)
-        nc.vector.quantize_mx(codes_3[:].bitcast(FP8X4), scales_3[:], v_bf[3])
-        v_codes = [codes_a[:, Q : Q + P], codes_a[:, Q + P : Q + 2 * P], codes_2[:], codes_3[:]]
-        v_scales = [scales_a[:, Q : Q + P], scales_a[:, Q + P : Q + 2 * P], scales_2[:], scales_3[:]]
+            bank = ps.tile([P, PAIRS, P], F32, name="weights_turned", tag="block%d" % b)
+            turn(weights[:, b, :], bank, weights_bf[b])
 
-        result = [ps.tile([P, PACK, P], F32, name="result%d" % h) for h in range(QB)]
+        gather_values(2)
+        joint_codes = sb.tile([P, Q + 2 * P], U32, name="joint_codes", tag="pool2", align_bytes=64)
+        joint_scales = sb.tile([P, Q + 2 * P], U8, name="joint_scales", align_bytes=64)
+        nc.vector.quantize_mx(joint_codes[:].bitcast(FP8X4), joint_scales[:], joint_bf[:])
+        v_codes = [joint_codes[:, Q + j * P : Q + (j + 1) * P] for j in range(2)]
+        v_scales = [joint_scales[:, Q + j * P : Q + (j + 1) * P] for j in range(2)]
+
+        gather_values(3)
+        for j, tag in ((2, "pool3"), (3, "last_codes")):
+            codes = sb.tile([P, P], U32, name="codes%d" % j, tag=tag, align_bytes=64)
+            scales = sb.tile([P, P], U8, name="scales%d" % j, align_bytes=64)
+            nc.vector.quantize_mx(codes[:].bitcast(FP8X4), scales[:], values_bf[j])
+            v_codes.append(codes[:])
+            v_scales.append(scales[:])
+
+        result = [ps.tile([P, PACK, P], F32, name="result%d" % b) for b in range(BLOCKS)]
         out_rows = out_0.rearrange("(p j) q -> p j q", j=PACK)
-        out_sb = [sb.tile([P, n, Q], F32, name="out_sb%d" % k, align_bytes=64) for k, n in enumerate((2, 1, 1))]
 
         def multiply(j):
-            for h in range(QB):
-                cols = slice(h * P, (h + 1) * P)
+            for b in range(BLOCKS):
                 nc.tensor.matmul_mx(
-                    result[h][:, j, :],
+                    result[b][:, j, :],
                     lhsT=v_codes[j].bitcast(FP8X4),
                     lhsT_scale=v_scales[j],
-                    rhs=codes_a[:, cols].bitcast(FP8X4),
-                    rhs_scale=scales_a[:, cols],
+                    rhs=joint_codes[:, block_cols(b)].bitcast(FP8X4),
+                    rhs_scale=joint_scales[:, block_cols(b)],
                     start=True,
                     stop=True,
                 )
 
-        def store_rows(k, first, end, queue):
-            for h in range(QB):
-                nc.scalar.copy(out_sb[k][:, :, h * P : (h + 1) * P], result[h][:, first:end, :])
-            queue.dma_start(out_rows[:, first:end, :], out_sb[k][:])
+        for first, end in ((0, 2), (2, 3)):
+            for j in range(first, end):
+                multiply(j)
+            early_rows = sb.tile([P, end - first, Q], F32, name="early_rows%d" % first, align_bytes=64)
+            for b in range(BLOCKS):
+                nc.scalar.copy(early_rows[:, :, block_cols(b)], result[b][:, first:end, :])
+            nc.sync.dma_start(out_rows[:, first:end, :], early_rows[:])
+        last = PACK - 1
+        multiply(last)
 
-        multiply(0)
-        multiply(1)
-        store_rows(0, 0, 2, nc.sync)
-        multiply(2)
-        store_rows(1, 2, 3, nc.sync)
-        multiply(3)
-
+        copies = (nc.vector.tensor_copy, nc.scalar.copy)
         out_bf = sb.tile([P, Q, PACK], BF16, name="out_bf", align_bytes=64)
-        nc.vector.tensor_copy(out_bf[:, 0:P, :], result[0][:].rearrange("p j n -> p n j"))
-        nc.scalar.copy(out_bf[:, P:Q, :], result[1][:].rearrange("p j n -> p n j"))
-        o_codes = sb.tile([P, Q], U32, name="o_codes", align_bytes=64)
-        o_scales = sb.tile([P, Q], U8, name="o_scales", align_bytes=64)
-        nc.vector.quantize_mx(o_codes[:].bitcast(FP8X4), o_scales[:], out_bf[:].rearrange("p q j -> p (q j)"))
-        store_rows(2, 3, 4, nc.scalar)
-        nc.sync.dma_start(out_1[0].rearrange("p c r -> p (c r)").bitcast(I32), o_codes[:].bitcast(I32))
-        for quad in range(4):
-            queue = nc.sync if quad < 3 else nc.scalar
+        for b in range(BLOCKS):
+            copies[b](out_bf[:, block_cols(b), :], result[b][:].rearrange("p j n -> p n j"))
+        last_rows = sb.tile([P, 1, Q], F32, name="last_rows", align_bytes=64)
+        for b in range(BLOCKS):
+            copies[b](last_rows[:, :, block_cols(b)], result[b][:, last:PACK, :])
+        nc.scalar.dma_start(out_rows[:, last:PACK, :], last_rows[:])
+
+        out_codes = sb.tile([P, Q], U32, name="out_codes", align_bytes=64)
+        out_scales = sb.tile([P, Q], U8, name="out_scales", align_bytes=64)
+        for b in range(BLOCKS):
+            nc.vector.quantize_mx(
+                out_codes[:, block_cols(b)].bitcast(FP8X4),
+                out_scales[:, block_cols(b)],
+                out_bf[:, block_cols(b), :].rearrange("p q j -> p (q j)"),
+            )
+        nc.sync.dma_start(out_1[0].rearrange("p c r -> p (c r)").bitcast(I32), out_codes[:].bitcast(I32))
+        for quadrant in range(QUADRANTS):
+            queue = nc.sync if quadrant < QUADRANTS // 2 else nc.scalar
             queue.dma_start(
-                out_2[0, 4 * quad : 4 * quad + 4, :].bitcast(I32),
-                o_scales[32 * quad : 32 * quad + 4, :].bitcast(I32),
+                out_2[0, scale_rows(quadrant), :].bitcast(I32),
+                out_scales[scale_partitions(quadrant), :].bitcast(I32),
             )

@@ -53,40 +53,47 @@ def tile_attend_multitoken_pl_kernel(tc, query, keys_words, keys_scales, c0, c1,
         nc.sync.dma_start(key_words[:].bitcast(I32), keys_words[0].bitcast(I32))
         query_raw = sb.tile([P, PACK, Q], F32, name="query_raw", align_bytes=64)
         nc.sync.dma_start(query_raw[:], query.rearrange("(p t) q -> p t q", t=PACK))
-        for quadrant in range(QUADRANTS):
+        for r in range(PACK):
             nc.sync.dma_start(
-                key_bytes[scale_partitions(quadrant), :].bitcast(I32),
-                keys_scales[0, scale_rows(quadrant), :].bitcast(I32),
+                key_bytes[r : P : 32, :].bitcast(I32),
+                keys_scales[0].rearrange("(g r) t -> r g t", r=PACK)[r].bitcast(I32),
             )
         vals_rows = vals.rearrange("(m j) t -> j m t", j=PACK)
-        val_pool = [sb.tile([P, T], F32, name="val_pool%d" % j, tag="pool%d" % j, align_bytes=64) for j in range(PACK)]
+        val_pool = {j: sb.tile([P, T], F32, name="val_pool%d" % j, tag="pool%d" % j, align_bytes=64) for j in (0, 2, 3)}
+        halves = [sb.tile([P, T // 2], F32, name="half%d" % h, align_bytes=64) for h in range(2)]
+        first_rows = sb.tile([P, P], F32, name="first_rows", tag="first", align_bytes=64)
+        later_rows = sb.tile([P, P], F32, name="later_rows", align_bytes=64)
+        nc.gpsimd.memset(first_rows[:], 0.0)
+        nc.gpsimd.memset(later_rows[:], 0.0)
+        nc.sync.dma_start(first_rows[0:BLOCKS, :], c0.rearrange("(b m) o -> b (m o)", b=BLOCKS))
         nc.sync.dma_start(val_pool[0][:], vals_rows[0])
-        factors = [sb.tile([P, BLOCKS], F32, name="factor%d" % k, align_bytes=64) for k in range(TAPS)]
-        for factor, source in zip(factors, (c0, c1, c2)):
-            with nc.allow_non_contiguous_dma(reason="one factor a partition and block"):
-                nc.sync.dma_start(factor[:], source.rearrange("(b m) o -> m (b o)", b=BLOCKS))
+        for k, source in enumerate((c1, c2)):
+            nc.sync.dma_start(later_rows[k * BLOCKS : (k + 1) * BLOCKS, :], source.rearrange("(b m) o -> b (m o)", b=BLOCKS))
+        for h in range(2):
+            nc.sync.dma_start(halves[h][:], vals_rows[1][:, h * T // 2 : (h + 1) * T // 2])
         size_cols = sb.tile([P, PACK], F32, name="size_cols")
         nc.sync.dma_start(size_cols[:], size.rearrange("o (m t) -> (o m) t", t=PACK))
-        for j in range(1, PACK):
+        for j in (2, 3):
             nc.sync.dma_start(val_pool[j][:], vals_rows[j])
 
         identity = sb.tile([P, P], F32, name="identity")
         make_identity(nc, identity[:])
+
+        first_ps = ps.tile([P, P], F32, name="first_ps", tag="block0")
+        nc.tensor.transpose(first_ps[:], first_rows[:], identity[:])
+        first_cols = sb.tile([P, BLOCKS], F32, name="first_cols", align_bytes=64)
+        nc.scalar.copy(first_cols[:], first_ps[:, 0:BLOCKS])
 
         listed_words = sb.tile([P, I], U16, name="listed_words", align_bytes=64)
         nc.vector.tensor_copy(listed_words[:], key_words[:].indirect(offsets[:]))
         listed_bytes = sb.tile([P, I], U8, name="listed_bytes", align_bytes=64)
         nc.vector.tensor_copy(listed_bytes[:], key_bytes[:].indirect(offsets[:]))
 
-        q_codes = sb.tile([P, Q], U32, name="q_codes", align_bytes=64)
+        q_codes = sb.tile([P, Q], U32, name="q_codes", tag="first", align_bytes=64)
         q_scales = sb.tile([P, Q], U8, name="q_scales", align_bytes=64)
         query_bf = sb.tile([P, Q, PACK], BF16, name="query_bf", align_bytes=64)
         nc.scalar.activation(query_bf[:], query_raw[:].rearrange("p t q -> p q t"), ACT.Copy)
         nc.vector.quantize_mx(q_codes[:].bitcast(FP8X4), q_scales[:], query_bf[:].rearrange("p q t -> p (q t)"))
-
-        size_ps = ps.tile([P, PACK, P], F32, name="size_ps")
-        for t in range(PACK):
-            nc.tensor.transpose(size_ps[:, t, :], size_cols[:, t : t + 1].to_broadcast([P, P]), identity[:])
 
         scores = []
         mixed = []
@@ -102,29 +109,40 @@ def tile_attend_multitoken_pl_kernel(tc, query, keys_words, keys_scales, c0, c1,
                 stop=True,
             )
             scores.append(score)
-            mix = sb.tile([P, I], F32, name="mixed%d" % b, align_bytes=64)
-            nc.scalar.activation(mix[:], score[:], ACT.Copy, scale=factors[0][:, b : b + 1])
+            mix = sb.tile([P, I], F32, name="mixed%d" % b, tag="mixed%d" % b, align_bytes=64)
+            nc.scalar.activation(mix[:], score[:], ACT.Copy, scale=first_cols[:, b : b + 1])
             mixed.append(mix)
 
-        joint_bf = sb.tile([P, (Q + 2 * P) * PACK], BF16, name="joint_bf", align_bytes=64)
-        later_bf = [sb.tile([P, P * PACK], BF16, name="later_bf%d" % j, align_bytes=64) for j in range(2, PACK)]
-        weights_bf = [joint_bf[:, b * P * PACK : (b + 1) * P * PACK] for b in range(BLOCKS)]
-        values_bf = [joint_bf[:, (Q + j * P) * PACK : (Q + (j + 1) * P) * PACK] for j in range(2)]
-        values_bf = values_bf + [tile[:] for tile in later_bf]
+        later_ps = ps.tile([P, P], F32, name="later_ps", tag="turn0")
+        nc.tensor.transpose(later_ps[:], later_rows[:], identity[:])
+        factors = [first_cols, later_ps[:, 0:BLOCKS], later_ps[:, BLOCKS : 2 * BLOCKS]]
 
-        def turn(rows_bf, bank, target):
+        joint_bf = sb.tile([P, (Q + 2 * P) * PACK], BF16, name="joint_bf", align_bytes=64)
+        later_bf = {j: sb.tile([P, P * PACK], BF16, name="later_bf%d" % j, align_bytes=64) for j in (1, 3)}
+        weights_bf = [joint_bf[:, b * P * PACK : (b + 1) * P * PACK] for b in range(BLOCKS)]
+        values_bf = {j: joint_bf[:, (Q + n * P) * PACK : (Q + (n + 1) * P) * PACK] for n, j in enumerate((0, 2))}
+        values_bf.update({j: later_bf[j][:] for j in (1, 3)})
+
+        def turn(rows_bf, tag, target):
+            bank = ps.tile([P, PAIRS, P], F32, name="turned", tag=tag)
             words = rows_bf.bitcast(F32)
             for u in range(PAIRS):
                 nc.tensor.transpose(bank[:, u, :], words[:, u : I // 2 : PAIRS], identity[:])
             nc.scalar.copy(target.bitcast(F32).rearrange("p (m u) -> p m u", u=PAIRS), bank[:].rearrange("p u m -> p m u"))
 
-        def gather_values(j):
-            picked = sb.tile([P, I], BF16, name="picked%d" % j, align_bytes=64)
+        def gather_values(j, tag):
+            picked = sb.tile([P, I], BF16, name="picked%d" % j, tag=tag, align_bytes=64)
             nc.vector.tensor_copy(picked[:], val_pool[j][:].indirect(offsets[:]))
-            bank = ps.tile([P, PAIRS, P], F32, name="turned", tag="turned", bufs=TURN_BANKS)
-            turn(picked[:], bank, values_bf[j])
+            return picked
 
-        gather_values(0)
+        picked0 = gather_values(0, "picked0")
+        pool_bf = sb.tile([P, T], BF16, name="pool_bf", align_bytes=64)
+        for h in range(2):
+            nc.scalar.activation(pool_bf[:, h * T // 2 : (h + 1) * T // 2], halves[h][:], ACT.Copy)
+
+        size_ps = ps.tile([P, PACK, P], F32, name="size_ps")
+        for t in range(PACK):
+            nc.tensor.transpose(size_ps[:, t, :], size_cols[:, t : t + 1].to_broadcast([P, P]), identity[:])
 
         for tap in range(1, TAPS):
             for b in range(BLOCKS):
@@ -137,49 +155,52 @@ def tile_attend_multitoken_pl_kernel(tc, query, keys_words, keys_scales, c0, c1,
                     ALU.add,
                 )
         probs = []
-        sums = sb.tile([P, BLOCKS], F32, name="sums")
+        minus_one = sb.tile([P, 1], F32, name="minus_one")
+        nc.gpsimd.memset(minus_one[:], -1.0)
+        inverses = []
         for b in range(BLOCKS):
             neg_max = sb.tile([P, 1], F32, name="neg_max%d" % b)
             nc.vector.tensor_reduce(neg_max[:], mixed[b][:], mybir.AxisListType.X, ALU.max, negate=True)
-            prob = sb.tile([P, I], F32, name="prob%d" % b, align_bytes=64)
-            nc.scalar.activation(prob[:], mixed[b][:], ACT.Exp, bias=neg_max[:], accum_out=sums[:, b : b + 1])
+            row_sum = sb.tile([P, 1], F32, name="row_sum%d" % b)
+            prob = sb.tile([P, I], F32, name="prob%d" % b, tag="prob%d" % b, align_bytes=64)
+            nc.scalar.activation(prob[:], mixed[b][:], ACT.Exp, bias=neg_max[:], accum_out=row_sum[:])
+            inverse = sb.tile([P, 1], F32, name="inverse%d" % b)
+            nc.gpsimd.tensor_tensor(inverse[:], row_sum[:], minus_one[:], ALU.pow)
+            inverses.append(inverse)
             probs.append(prob)
+        turn(picked0[:], "turn0", values_bf[0])
 
-        gather_values(1)
-        inverses = sb.tile([P, BLOCKS], F32, name="inverses")
-        nc.vector.reciprocal(inverses[:], sums[:])
-        weights = sb.tile([P, BLOCKS, I], BF16, name="weights", tag="pool1", align_bytes=64)
+        picked2 = gather_values(2, "picked2")
+        picked1 = sb.tile([P, I], BF16, name="picked1", tag="mixed1", align_bytes=64)
+        nc.scalar.activation(picked1[:], pool_bf[:].indirect(offsets[:]), ACT.Copy)
+        turn(picked2[:], "turn1", values_bf[2])
+
+        weights = sb.tile([P, BLOCKS, I], BF16, name="weights", tag="pool2", align_bytes=64)
         for b in range(BLOCKS):
             nc.vector.scalar_tensor_tensor(
                 weights[:, b, :].rearrange("p (m t) -> p m t", t=PACK),
                 probs[b][:].rearrange("p (m t) -> p m t", t=PACK),
-                inverses[:, b : b + 1],
+                inverses[b][:],
                 size_ps[:].rearrange("p t m -> p m t"),
                 ALU.mult,
                 ALU.mult,
             )
-            bank = ps.tile([P, PAIRS, P], F32, name="weights_turned", tag="block%d" % b)
-            turn(weights[:, b, :], bank, weights_bf[b])
+            turn(weights[:, b, :], "block%d" % b, weights_bf[b])
+        picked3 = gather_values(3, "prob0")
+        turn(picked1[:], "block0", values_bf[1])
+        turn(picked3[:], "turn2", values_bf[3])
 
-        gather_values(2)
-        joint_codes = sb.tile([P, Q + 2 * P], U32, name="joint_codes", tag="pool2", align_bytes=64)
-        joint_scales = sb.tile([P, Q + 2 * P], U8, name="joint_scales", align_bytes=64)
-        nc.vector.quantize_mx(joint_codes[:].bitcast(FP8X4), joint_scales[:], joint_bf[:])
-        v_codes = [joint_codes[:, Q + j * P : Q + (j + 1) * P] for j in range(2)]
-        v_scales = [joint_scales[:, Q + j * P : Q + (j + 1) * P] for j in range(2)]
-
-        gather_values(3)
-        for j, tag in ((2, "pool3"), (3, "last_codes")):
-            codes = sb.tile([P, P], U32, name="codes%d" % j, tag=tag, align_bytes=64)
-            scales = sb.tile([P, P], U8, name="scales%d" % j, align_bytes=64)
-            nc.vector.quantize_mx(codes[:].bitcast(FP8X4), scales[:], values_bf[j])
-            v_codes.append(codes[:])
-            v_scales.append(scales[:])
+        joint_codes = sb.tile([P, Q + PACK * P], U32, name="joint_codes", tag="pool3", align_bytes=64)
+        joint_scales = sb.tile([P, Q + PACK * P], U8, name="joint_scales", align_bytes=64)
+        nc.vector.quantize_mx(joint_codes[:, 0 : Q + 2 * P].bitcast(FP8X4), joint_scales[:, 0 : Q + 2 * P], joint_bf[:])
+        v_codes = {j: joint_codes[:, Q + n * P : Q + (n + 1) * P] for n, j in enumerate((0, 2, 1, 3))}
+        v_scales = {j: joint_scales[:, Q + n * P : Q + (n + 1) * P] for n, j in enumerate((0, 2, 1, 3))}
+        for j in (1, 3):
+            nc.vector.quantize_mx(v_codes[j].bitcast(FP8X4), v_scales[j], values_bf[j])
 
         result = [ps.tile([P, PACK, P], F32, name="result%d" % b) for b in range(BLOCKS)]
         out_rows = out_0.rearrange("(p j) q -> p j q", j=PACK)
-
-        def multiply(j):
+        for j in (0, 2, 1, 3):
             for b in range(BLOCKS):
                 nc.tensor.matmul_mx(
                     result[b][:, j, :],
@@ -191,24 +212,18 @@ def tile_attend_multitoken_pl_kernel(tc, query, keys_words, keys_scales, c0, c1,
                     stop=True,
                 )
 
-        for first, end in ((0, 2), (2, 3)):
-            for j in range(first, end):
-                multiply(j)
-            early_rows = sb.tile([P, end - first, Q], F32, name="early_rows%d" % first, align_bytes=64)
-            for b in range(BLOCKS):
-                nc.scalar.copy(early_rows[:, :, block_cols(b)], result[b][:, first:end, :])
-            nc.sync.dma_start(out_rows[:, first:end, :], early_rows[:])
-        last = PACK - 1
-        multiply(last)
-
         copies = (nc.vector.tensor_copy, nc.scalar.copy)
         out_bf = sb.tile([P, Q, PACK], BF16, name="out_bf", align_bytes=64)
         for b in range(BLOCKS):
             copies[b](out_bf[:, block_cols(b), :], result[b][:].rearrange("p j n -> p n j"))
-        last_rows = sb.tile([P, 1, Q], F32, name="last_rows", align_bytes=64)
+        low_rows = sb.tile([P, PAIRS, Q], F32, name="low_rows", align_bytes=64)
+        high_rows = sb.tile([P, PAIRS, Q], F32, name="high_rows", align_bytes=64)
         for b in range(BLOCKS):
-            copies[b](last_rows[:, :, block_cols(b)], result[b][:, last:PACK, :])
-        nc.scalar.dma_start(out_rows[:, last:PACK, :], last_rows[:])
+            copies[b](low_rows[:, :, block_cols(b)], result[b][:, 0:PAIRS, :])
+        nc.sync.dma_start(out_rows[:, 0:PAIRS, :], low_rows[:])
+        for b in (1, 0):
+            nc.scalar.copy(high_rows[:, :, block_cols(b)], result[b][:, PAIRS:PACK, :])
+        nc.scalar.dma_start(out_rows[:, PAIRS:PACK, :], high_rows[:])
 
         out_codes = sb.tile([P, Q], U32, name="out_codes", align_bytes=64)
         out_scales = sb.tile([P, Q], U8, name="out_scales", align_bytes=64)

@@ -71,10 +71,10 @@ def tile_attend_multitoken_pl_kernel(tc, query, keys_words, keys_scales, c0, c1,
             nc.sync.dma_start(later_rows[k * BLOCKS : (k + 1) * BLOCKS, :], source.rearrange("(b m) o -> b (m o)", b=BLOCKS))
         for h in range(2):
             nc.sync.dma_start(halves[h][:], vals_rows[1][:, h * T // 2 : (h + 1) * T // 2])
+        nc.sync.dma_start(val_pool[2][:], vals_rows[2])
         size_cols = sb.tile([P, PACK], F32, name="size_cols")
         nc.sync.dma_start(size_cols[:], size.rearrange("o (m t) -> (o m) t", t=PACK))
-        for j in (2, 3):
-            nc.sync.dma_start(val_pool[j][:], vals_rows[j])
+        nc.sync.dma_start(val_pool[3][:], vals_rows[3])
 
         identity = sb.tile([P, P], F32, name="identity")
         make_identity(nc, identity[:])
@@ -92,8 +92,17 @@ def tile_attend_multitoken_pl_kernel(tc, query, keys_words, keys_scales, c0, c1,
         q_codes = sb.tile([P, Q], U32, name="q_codes", tag="first", align_bytes=64)
         q_scales = sb.tile([P, Q], U8, name="q_scales", align_bytes=64)
         query_bf = sb.tile([P, Q, PACK], BF16, name="query_bf", align_bytes=64)
-        nc.scalar.activation(query_bf[:], query_raw[:].rearrange("p t q -> p q t"), ACT.Copy)
-        nc.vector.quantize_mx(q_codes[:].bitcast(FP8X4), q_scales[:], query_bf[:].rearrange("p q t -> p (q t)"))
+        for b in range(BLOCKS):
+            nc.scalar.activation(
+                query_bf[:, block_cols(b), :].rearrange("p (c i) t -> p c t i", i=PACK),
+                query_raw[:, :, block_cols(b)].rearrange("p t (c i) -> p c t i", i=PACK),
+                ACT.Copy,
+            )
+            nc.vector.quantize_mx(
+                q_codes[:, block_cols(b)].bitcast(FP8X4),
+                q_scales[:, block_cols(b)],
+                query_bf[:, block_cols(b), :].rearrange("p q t -> p (q t)"),
+            )
 
         scores = []
         mixed = []
@@ -117,18 +126,19 @@ def tile_attend_multitoken_pl_kernel(tc, query, keys_words, keys_scales, c0, c1,
         nc.tensor.transpose(later_ps[:], later_rows[:], identity[:])
         factors = [first_cols, later_ps[:, 0:BLOCKS], later_ps[:, BLOCKS : 2 * BLOCKS]]
 
-        joint_bf = sb.tile([P, (Q + 2 * P) * PACK], BF16, name="joint_bf", align_bytes=64)
-        later_bf = {j: sb.tile([P, P * PACK], BF16, name="later_bf%d" % j, align_bytes=64) for j in (1, 3)}
-        weights_bf = [joint_bf[:, b * P * PACK : (b + 1) * P * PACK] for b in range(BLOCKS)]
-        values_bf = {j: joint_bf[:, (Q + n * P) * PACK : (Q + (n + 1) * P) * PACK] for n, j in enumerate((0, 2))}
-        values_bf.update({j: later_bf[j][:] for j in (1, 3)})
-
-        def turn(rows_bf, tag, target):
-            bank = ps.tile([P, PAIRS, P], F32, name="turned", tag=tag)
-            words = rows_bf.bitcast(F32)
-            for u in range(PAIRS):
-                nc.tensor.transpose(bank[:, u, :], words[:, u : I // 2 : PAIRS], identity[:])
-            nc.scalar.copy(target.bitcast(F32).rearrange("p (m u) -> p m u", u=PAIRS), bank[:].rearrange("p u m -> p m u"))
+        def turn(sources, tag):
+            count = len(sources)
+            bank = ps.tile([P, count, PAIRS, P], F32, name="turned", tag=tag)
+            for n, rows_bf in enumerate(sources):
+                words = rows_bf.bitcast(F32)
+                for u in range(PAIRS):
+                    nc.tensor.transpose(bank[:, n, u, :], words[:, u : I // 2 : PAIRS], identity[:])
+            target = sb.tile([P, count * P * PACK], BF16, name="turned_bf", tag="bf_" + tag, align_bytes=64)
+            nc.scalar.copy(
+                target[:].bitcast(F32).rearrange("p (n m u) -> p n m u", n=count, u=PAIRS),
+                bank[:].rearrange("p n u m -> p n m u"),
+            )
+            return target
 
         def gather_values(j, tag):
             picked = sb.tile([P, I], BF16, name="picked%d" % j, tag=tag, align_bytes=64)
@@ -168,14 +178,13 @@ def tile_attend_multitoken_pl_kernel(tc, query, keys_words, keys_scales, c0, c1,
             nc.gpsimd.tensor_tensor(inverse[:], row_sum[:], minus_one[:], ALU.pow)
             inverses.append(inverse)
             probs.append(prob)
-        turn(picked0[:], "turn0", values_bf[0])
+        turned = [turn([picked0[:]], "turn0")]
 
         picked2 = gather_values(2, "picked2")
         picked1 = sb.tile([P, I], BF16, name="picked1", tag="mixed1", align_bytes=64)
         nc.scalar.activation(picked1[:], pool_bf[:].indirect(offsets[:]), ACT.Copy)
-        turn(picked2[:], "turn1", values_bf[2])
 
-        weights = sb.tile([P, BLOCKS, I], BF16, name="weights", tag="pool2", align_bytes=64)
+        weights = sb.tile([P, BLOCKS, I], BF16, name="weights", align_bytes=64)
         for b in range(BLOCKS):
             nc.vector.scalar_tensor_tensor(
                 weights[:, b, :].rearrange("p (m t) -> p m t", t=PACK),
@@ -185,32 +194,32 @@ def tile_attend_multitoken_pl_kernel(tc, query, keys_words, keys_scales, c0, c1,
                 ALU.mult,
                 ALU.mult,
             )
-            turn(weights[:, b, :], "block%d" % b, weights_bf[b])
+            turned.append(turn([weights[:, b, :], (picked2, picked1)[b][:]], "block%d" % b))
         picked3 = gather_values(3, "prob0")
-        turn(picked1[:], "block0", values_bf[1])
-        turn(picked3[:], "turn2", values_bf[3])
+        turned.append(turn([picked3[:]], "turn1"))
 
         joint_codes = sb.tile([P, Q + PACK * P], U32, name="joint_codes", tag="pool3", align_bytes=64)
         joint_scales = sb.tile([P, Q + PACK * P], U8, name="joint_scales", align_bytes=64)
-        nc.vector.quantize_mx(joint_codes[:, 0 : Q + 2 * P].bitcast(FP8X4), joint_scales[:, 0 : Q + 2 * P], joint_bf[:])
-        v_codes = {j: joint_codes[:, Q + n * P : Q + (n + 1) * P] for n, j in enumerate((0, 2, 1, 3))}
-        v_scales = {j: joint_scales[:, Q + n * P : Q + (n + 1) * P] for n, j in enumerate((0, 2, 1, 3))}
-        for j in (1, 3):
-            nc.vector.quantize_mx(v_codes[j].bitcast(FP8X4), v_scales[j], values_bf[j])
+        start = 0
+        for target, count in zip(turned, (1, 2, 2, 1)):
+            cols = slice(start * P, (start + count) * P)
+            nc.vector.quantize_mx(joint_codes[:, cols].bitcast(FP8X4), joint_scales[:, cols], target[:])
+            start = start + count
+        weight_cols = [block_cols(1), block_cols(3)]
+        value_cols = [block_cols(0), block_cols(4), block_cols(2), block_cols(5)]
 
         result = [ps.tile([P, PACK, P], F32, name="result%d" % b) for b in range(BLOCKS)]
         out_rows = out_0.rearrange("(p j) q -> p j q", j=PACK)
-        for j in (0, 2, 1, 3):
-            for b in range(BLOCKS):
-                nc.tensor.matmul_mx(
-                    result[b][:, j, :],
-                    lhsT=v_codes[j].bitcast(FP8X4),
-                    lhsT_scale=v_scales[j],
-                    rhs=joint_codes[:, block_cols(b)].bitcast(FP8X4),
-                    rhs_scale=joint_scales[:, block_cols(b)],
-                    start=True,
-                    stop=True,
-                )
+        for j, b in ((0, 0), (2, 0), (1, 0), (0, 1), (1, 1), (2, 1), (3, 0), (3, 1)):
+            nc.tensor.matmul_mx(
+                result[b][:, j, :],
+                lhsT=joint_codes[:, value_cols[j]].bitcast(FP8X4),
+                lhsT_scale=joint_scales[:, value_cols[j]],
+                rhs=joint_codes[:, weight_cols[b]].bitcast(FP8X4),
+                rhs_scale=joint_scales[:, weight_cols[b]],
+                start=True,
+                stop=True,
+            )
 
         copies = (nc.vector.tensor_copy, nc.scalar.copy)
         out_bf = sb.tile([P, Q, PACK], BF16, name="out_bf", align_bytes=64)

@@ -70,8 +70,8 @@ def tile_attend_multitoken_pl_kernel(tc, query, keys_words, keys_scales, c0, c1,
         for k, source in enumerate((c1, c2)):
             nc.sync.dma_start(later_rows[k * BLOCKS : (k + 1) * BLOCKS, :], source.rearrange("(b m) o -> b (m o)", b=BLOCKS))
         for h in range(2):
-            nc.sync.dma_start(halves[h][:], vals_rows[1][:, h * T // 2 : (h + 1) * T // 2])
-        nc.sync.dma_start(val_pool[2][:], vals_rows[2])
+            nc.sync.dma_start(halves[h][:], vals_rows[2][:, h * T // 2 : (h + 1) * T // 2])
+        nc.sync.dma_start(val_pool[2][:], vals_rows[1])
         size_cols = sb.tile([P, PACK], F32, name="size_cols")
         nc.sync.dma_start(size_cols[:], size.rearrange("o (m t) -> (o m) t", t=PACK))
         nc.sync.dma_start(val_pool[3][:], vals_rows[3])
@@ -150,7 +150,7 @@ def tile_attend_multitoken_pl_kernel(tc, query, keys_words, keys_scales, c0, c1,
         for h in range(2):
             nc.scalar.activation(pool_bf[:, h * T // 2 : (h + 1) * T // 2], halves[h][:], ACT.Copy)
 
-        size_ps = ps.tile([P, PACK, P], F32, name="size_ps")
+        size_ps = ps.tile([P, PACK, P], F32, name="size_ps", tag="size")
         for t in range(PACK):
             nc.tensor.transpose(size_ps[:, t, :], size_cols[:, t : t + 1].to_broadcast([P, P]), identity[:])
 
@@ -206,13 +206,14 @@ def tile_attend_multitoken_pl_kernel(tc, query, keys_words, keys_scales, c0, c1,
             nc.vector.quantize_mx(joint_codes[:, cols].bitcast(FP8X4), joint_scales[:, cols], target[:])
             start = start + count
         weight_cols = [block_cols(1), block_cols(3)]
-        value_cols = [block_cols(0), block_cols(4), block_cols(2), block_cols(5)]
+        value_cols = [block_cols(0), block_cols(2), block_cols(4), block_cols(5)]
 
-        result = [ps.tile([P, PACK, P], F32, name="result%d" % b) for b in range(BLOCKS)]
+        bank_tags = (("result0", "result1"), ("turn0", "size"))
+        result = [[ps.tile([P, PAIRS, P], F32, name="result", tag=bank_tags[u][b]) for b in range(BLOCKS)] for u in range(PAIRS)]
         out_rows = out_0.rearrange("(p j) q -> p j q", j=PACK)
-        for j, b in ((0, 0), (2, 0), (1, 0), (0, 1), (1, 1), (2, 1), (3, 0), (3, 1)):
+        for j, b in ((0, 0), (1, 0), (0, 1), (1, 1), (2, 0), (2, 1), (3, 0), (3, 1)):
             nc.tensor.matmul_mx(
-                result[b][:, j, :],
+                result[j // 2][b][:, j % 2, :],
                 lhsT=joint_codes[:, value_cols[j]].bitcast(FP8X4),
                 lhsT_scale=joint_scales[:, value_cols[j]],
                 rhs=joint_codes[:, weight_cols[b]].bitcast(FP8X4),
@@ -223,16 +224,22 @@ def tile_attend_multitoken_pl_kernel(tc, query, keys_words, keys_scales, c0, c1,
 
         copies = (nc.vector.tensor_copy, nc.scalar.copy)
         out_bf = sb.tile([P, Q, PACK], BF16, name="out_bf", align_bytes=64)
-        for b in range(BLOCKS):
-            copies[b](out_bf[:, block_cols(b), :], result[b][:].rearrange("p j n -> p n j"))
-        low_rows = sb.tile([P, PAIRS, Q], F32, name="low_rows", align_bytes=64)
-        high_rows = sb.tile([P, PAIRS, Q], F32, name="high_rows", align_bytes=64)
-        for b in range(BLOCKS):
-            copies[b](low_rows[:, :, block_cols(b)], result[b][:, 0:PAIRS, :])
-        nc.sync.dma_start(out_rows[:, 0:PAIRS, :], low_rows[:])
-        for b in (1, 0):
-            nc.scalar.copy(high_rows[:, :, block_cols(b)], result[b][:, PAIRS:PACK, :])
-        nc.scalar.dma_start(out_rows[:, PAIRS:PACK, :], high_rows[:])
+        rows = [sb.tile([P, PAIRS, Q], F32, name="rows%d" % u, align_bytes=64) for u in range(PAIRS)]
+
+        def copy_rows(u):
+            for b in range(BLOCKS):
+                copies[b](rows[u][:, :, block_cols(b)], result[u][b][:])
+
+        def copy_places(u):
+            for b in range(BLOCKS):
+                copies[b](out_bf[:, block_cols(b), 2 * u : 2 * u + 2], result[u][b][:].rearrange("p j n -> p n j"))
+
+        copy_rows(0)
+        nc.sync.dma_start(out_rows[:, 0:PAIRS, :], rows[0][:])
+        copy_places(0)
+        copy_places(1)
+        copy_rows(1)
+        nc.scalar.dma_start(out_rows[:, PAIRS:PACK, :], rows[1][:])
 
         out_codes = sb.tile([P, Q], U32, name="out_codes", align_bytes=64)
         out_scales = sb.tile([P, Q], U8, name="out_scales", align_bytes=64)

@@ -60,20 +60,21 @@ def tile_attend_multitoken_pl_kernel(tc, query, keys_words, keys_scales, c0, c1,
             )
         vals_rows = vals.rearrange("(m j) t -> j m t", j=PACK)
         val_pool = {j: sb.tile([P, T], F32, name="val_pool%d" % j, tag="pool%d" % j, align_bytes=64) for j in (0, 2, 3)}
-        halves = [sb.tile([P, T // 2], F32, name="half%d" % h, align_bytes=64) for h in range(2)]
+        parts = (slice(0, T // 2), slice(T // 2, T))
+        halves = [sb.tile([P, part.stop - part.start], F32, name="part%d" % h, tag="part%d" % h, align_bytes=64) for h, part in enumerate(parts)]
         first_rows = sb.tile([P, P], F32, name="first_rows", tag="first", align_bytes=64)
         later_rows = sb.tile([P, P], F32, name="later_rows", align_bytes=64)
-        nc.gpsimd.memset(first_rows[:], 0.0)
-        nc.gpsimd.memset(later_rows[:], 0.0)
+        size_rows = sb.tile([P, P], F32, name="size_rows", align_bytes=64)
+        for rows in (first_rows, later_rows, size_rows):
+            nc.gpsimd.memset(rows[:], 0.0)
         nc.sync.dma_start(first_rows[0:BLOCKS, :], c0.rearrange("(b m) o -> b (m o)", b=BLOCKS))
         nc.sync.dma_start(val_pool[0][:], vals_rows[0])
         for k, source in enumerate((c1, c2)):
             nc.sync.dma_start(later_rows[k * BLOCKS : (k + 1) * BLOCKS, :], source.rearrange("(b m) o -> b (m o)", b=BLOCKS))
+        nc.sync.dma_start(size_rows[0:PACK, :], size.rearrange("o (r m) -> (o r) m", r=PACK))
         for h in range(2):
-            nc.sync.dma_start(halves[h][:], vals_rows[2][:, h * T // 2 : (h + 1) * T // 2])
+            nc.sync.dma_start(halves[h][:], vals_rows[2][:, parts[h]])
         nc.sync.dma_start(val_pool[2][:], vals_rows[1])
-        size_cols = sb.tile([P, PACK], F32, name="size_cols")
-        nc.sync.dma_start(size_cols[:], size.rearrange("o (m t) -> (o m) t", t=PACK))
         nc.sync.dma_start(val_pool[3][:], vals_rows[3])
 
         identity = sb.tile([P, P], F32, name="identity")
@@ -125,17 +126,22 @@ def tile_attend_multitoken_pl_kernel(tc, query, keys_words, keys_scales, c0, c1,
         later_ps = ps.tile([P, P], F32, name="later_ps", tag="turn0")
         nc.tensor.transpose(later_ps[:], later_rows[:], identity[:])
         factors = [first_cols, later_ps[:, 0:BLOCKS], later_ps[:, BLOCKS : 2 * BLOCKS]]
+        size_turned = ps.tile([P, P], F32, name="size_turned", tag="result0")
+        nc.tensor.transpose(size_turned[:], size_rows[:], identity[:])
+        size_cols = sb.tile([P, PACK], F32, name="size_cols", align_bytes=64)
+        nc.scalar.copy(size_cols[:], size_turned[:, 0:PACK])
 
-        def turn(sources, tag):
+        def turn(sources, tag, target=None):
             count = len(sources)
             bank = ps.tile([P, count, PAIRS, P], F32, name="turned", tag=tag)
             for n, rows_bf in enumerate(sources):
                 words = rows_bf.bitcast(F32)
                 for u in range(PAIRS):
                     nc.tensor.transpose(bank[:, n, u, :], words[:, u : I // 2 : PAIRS], identity[:])
-            target = sb.tile([P, count * P * PACK], BF16, name="turned_bf", tag="bf_" + tag, align_bytes=64)
+            if target is None:
+                target = sb.tile([P, count * P * PACK], BF16, name="turned_bf", tag="bf_" + tag, align_bytes=64)[:]
             nc.scalar.copy(
-                target[:].bitcast(F32).rearrange("p (n m u) -> p n m u", n=count, u=PAIRS),
+                target.bitcast(F32).rearrange("p (n m u) -> p n m u", n=count, u=PAIRS),
                 bank[:].rearrange("p n u m -> p n m u"),
             )
             return target
@@ -148,7 +154,7 @@ def tile_attend_multitoken_pl_kernel(tc, query, keys_words, keys_scales, c0, c1,
         picked0 = gather_values(0, "picked0")
         pool_bf = sb.tile([P, T], BF16, name="pool_bf", align_bytes=64)
         for h in range(2):
-            nc.scalar.activation(pool_bf[:, h * T // 2 : (h + 1) * T // 2], halves[h][:], ACT.Copy)
+            nc.scalar.activation(pool_bf[:, parts[h]], halves[h][:], ACT.Copy)
 
         size_ps = ps.tile([P, PACK, P], F32, name="size_ps", tag="size")
         for t in range(PACK):
@@ -168,33 +174,35 @@ def tile_attend_multitoken_pl_kernel(tc, query, keys_words, keys_scales, c0, c1,
         minus_one = sb.tile([P, 1], F32, name="minus_one")
         nc.gpsimd.memset(minus_one[:], -1.0)
         inverses = []
+        after_cast = sb.tile([P, I // 2 + 32], F32, name="after_cast", tag="part1", align_bytes=64)
         for b in range(BLOCKS):
             neg_max = sb.tile([P, 1], F32, name="neg_max%d" % b)
             nc.vector.tensor_reduce(neg_max[:], mixed[b][:], mybir.AxisListType.X, ALU.max, negate=True)
-            row_sum = sb.tile([P, 1], F32, name="row_sum%d" % b)
+            row_sum = after_cast[:, I // 2 + 16 * b : I // 2 + 16 * b + 1]
             prob = sb.tile([P, I], F32, name="prob%d" % b, tag="prob%d" % b, align_bytes=64)
-            nc.scalar.activation(prob[:], mixed[b][:], ACT.Exp, bias=neg_max[:], accum_out=row_sum[:])
+            nc.scalar.activation(prob[:], mixed[b][:], ACT.Exp, bias=neg_max[:], accum_out=row_sum)
             inverse = sb.tile([P, 1], F32, name="inverse%d" % b)
-            nc.gpsimd.tensor_tensor(inverse[:], row_sum[:], minus_one[:], ALU.pow)
+            nc.gpsimd.tensor_tensor(inverse[:], row_sum, minus_one[:], ALU.pow)
             inverses.append(inverse)
             probs.append(prob)
-        turned = [turn([picked0[:]], "turn0")]
 
+        turned = [turn([picked0[:]], "turn0", after_cast[:, 0 : I // 2].bitcast(BF16))]
         picked2 = gather_values(2, "picked2")
         picked1 = sb.tile([P, I], BF16, name="picked1", tag="mixed1", align_bytes=64)
         nc.scalar.activation(picked1[:], pool_bf[:].indirect(offsets[:]), ACT.Copy)
 
-        weights = sb.tile([P, BLOCKS, I], BF16, name="weights", align_bytes=64)
+        weights_tile = sb.tile([P, BLOCKS, I], BF16, name="weights", tag="pool2", align_bytes=64)
+        weights = [weights_tile[:, b, :] for b in range(BLOCKS)]
         for b in range(BLOCKS):
             nc.vector.scalar_tensor_tensor(
-                weights[:, b, :].rearrange("p (m t) -> p m t", t=PACK),
-                probs[b][:].rearrange("p (m t) -> p m t", t=PACK),
+                weights[b],
+                probs[b][:],
                 inverses[b][:],
-                size_ps[:].rearrange("p t m -> p m t"),
+                size_ps[:].rearrange("p r m -> p (r m)"),
                 ALU.mult,
                 ALU.mult,
             )
-            turned.append(turn([weights[:, b, :], (picked2, picked1)[b][:]], "block%d" % b))
+            turned.append(turn([weights[b], (picked2, picked1)[b][:]], "block%d" % b))
         picked3 = gather_values(3, "prob0")
         turned.append(turn([picked3[:]], "turn1"))
 
@@ -203,7 +211,7 @@ def tile_attend_multitoken_pl_kernel(tc, query, keys_words, keys_scales, c0, c1,
         start = 0
         for target, count in zip(turned, (1, 2, 2, 1)):
             cols = slice(start * P, (start + count) * P)
-            nc.vector.quantize_mx(joint_codes[:, cols].bitcast(FP8X4), joint_scales[:, cols], target[:])
+            nc.vector.quantize_mx(joint_codes[:, cols].bitcast(FP8X4), joint_scales[:, cols], target)
             start = start + count
         weight_cols = [block_cols(1), block_cols(3)]
         value_cols = [block_cols(0), block_cols(2), block_cols(4), block_cols(5)]

@@ -23,6 +23,7 @@ PAIRS = PACK // 2
 BLOCKS = Q // P
 TAPS = 3
 QUADRANTS = 4
+EARLY = 128
 TURN_BANKS = 3
 
 
@@ -119,8 +120,9 @@ def tile_attend_multitoken_pl_kernel(tc, query, keys_words, keys_scales, c0, c1,
                 stop=True,
             )
             scores.append(score)
-            mix = sb.tile([P, I], F32, name="mixed%d" % b, tag="mixed%d" % b, align_bytes=64)
-            nc.scalar.activation(mix[:], score[:], ACT.Copy, scale=first_cols[:, b : b + 1])
+            room = sb.tile([P, EARLY // 2 + I], F32, name="mixed%d" % b, align_bytes=64)
+            mix = room[:, EARLY // 2 : EARLY // 2 + I]
+            nc.scalar.activation(mix, score[:], ACT.Copy, scale=first_cols[:, b : b + 1])
             mixed.append(mix)
 
         later_ps = ps.tile([P, P], F32, name="later_ps", tag="turn0")
@@ -156,6 +158,8 @@ def tile_attend_multitoken_pl_kernel(tc, query, keys_words, keys_scales, c0, c1,
         for h in range(2):
             nc.scalar.activation(pool_bf[:, parts[h]], halves[h][:], ACT.Copy)
 
+        picked1 = room[:, 0 : I // 2].bitcast(BF16)
+        nc.scalar.activation(picked1[:, 0:EARLY], pool_bf[:].indirect(offsets[:, 0 : EARLY // 16]), ACT.Copy)
         size_ps = ps.tile([P, PACK, P], F32, name="size_ps", tag="size")
         for t in range(PACK):
             nc.tensor.transpose(size_ps[:, t, :], size_cols[:, t : t + 1].to_broadcast([P, P]), identity[:])
@@ -177,19 +181,21 @@ def tile_attend_multitoken_pl_kernel(tc, query, keys_words, keys_scales, c0, c1,
         after_cast = sb.tile([P, I // 2 + 32], F32, name="after_cast", tag="part1", align_bytes=64)
         for b in range(BLOCKS):
             neg_max = sb.tile([P, 1], F32, name="neg_max%d" % b)
-            nc.vector.tensor_reduce(neg_max[:], mixed[b][:], mybir.AxisListType.X, ALU.max, negate=True)
+            nc.vector.tensor_reduce(neg_max[:], mixed[b], mybir.AxisListType.X, ALU.max, negate=True)
             row_sum = after_cast[:, I // 2 + 16 * b : I // 2 + 16 * b + 1]
             prob = sb.tile([P, I], F32, name="prob%d" % b, tag="prob%d" % b, align_bytes=64)
-            nc.scalar.activation(prob[:], mixed[b][:], ACT.Exp, bias=neg_max[:], accum_out=row_sum)
+            nc.scalar.activation(prob[:], mixed[b], ACT.Exp, bias=neg_max[:], accum_out=row_sum)
             inverse = sb.tile([P, 1], F32, name="inverse%d" % b)
             nc.gpsimd.tensor_tensor(inverse[:], row_sum, minus_one[:], ALU.pow)
             inverses.append(inverse)
             probs.append(prob)
 
         turned = [turn([picked0[:]], "turn0", after_cast[:, 0 : I // 2].bitcast(BF16))]
+        first_codes = sb.tile([P, P], U32, name="first_codes", align_bytes=64)
+        first_scales = sb.tile([P, P], U8, name="first_scales", align_bytes=64)
+        nc.vector.quantize_mx(first_codes[:].bitcast(FP8X4), first_scales[:], turned[0])
         picked2 = gather_values(2, "picked2")
-        picked1 = sb.tile([P, I], BF16, name="picked1", tag="mixed1", align_bytes=64)
-        nc.scalar.activation(picked1[:], pool_bf[:].indirect(offsets[:]), ACT.Copy)
+        nc.scalar.activation(picked1[:, EARLY:I], pool_bf[:].indirect(offsets[:, EARLY // 16 : I // 16]), ACT.Copy)
 
         weights_tile = sb.tile([P, BLOCKS, I], BF16, name="weights", tag="pool2", align_bytes=64)
         weights = [weights_tile[:, b, :] for b in range(BLOCKS)]
@@ -202,19 +208,20 @@ def tile_attend_multitoken_pl_kernel(tc, query, keys_words, keys_scales, c0, c1,
                 ALU.mult,
                 ALU.mult,
             )
-            turned.append(turn([weights[b], (picked2, picked1)[b][:]], "block%d" % b))
+            turned.append(turn([weights[b], (picked2[:], picked1)[b]], "block%d" % b))
         picked3 = gather_values(3, "prob0")
         turned.append(turn([picked3[:]], "turn1"))
 
-        joint_codes = sb.tile([P, Q + PACK * P], U32, name="joint_codes", tag="pool3", align_bytes=64)
-        joint_scales = sb.tile([P, Q + PACK * P], U8, name="joint_scales", align_bytes=64)
+        joint_codes = sb.tile([P, 5 * P], U32, name="joint_codes", tag="pool3", align_bytes=64)
+        joint_scales = sb.tile([P, 5 * P], U8, name="joint_scales", align_bytes=64)
         start = 0
-        for target, count in zip(turned, (1, 2, 2, 1)):
+        for target, count in zip(turned[1:], (2, 2, 1)):
             cols = slice(start * P, (start + count) * P)
             nc.vector.quantize_mx(joint_codes[:, cols].bitcast(FP8X4), joint_scales[:, cols], target)
             start = start + count
-        weight_cols = [block_cols(1), block_cols(3)]
-        value_cols = [block_cols(0), block_cols(2), block_cols(4), block_cols(5)]
+        weight_cols = [block_cols(0), block_cols(2)]
+        value_codes = [first_codes[:]] + [joint_codes[:, block_cols(n)] for n in (1, 3, 4)]
+        value_scales = [first_scales[:]] + [joint_scales[:, block_cols(n)] for n in (1, 3, 4)]
 
         bank_tags = (("result0", "result1"), ("turn0", "size"))
         result = [[ps.tile([P, PAIRS, P], F32, name="result", tag=bank_tags[u][b]) for b in range(BLOCKS)] for u in range(PAIRS)]
@@ -222,8 +229,8 @@ def tile_attend_multitoken_pl_kernel(tc, query, keys_words, keys_scales, c0, c1,
         for j, b in ((0, 0), (1, 0), (0, 1), (1, 1), (2, 0), (2, 1), (3, 0), (3, 1)):
             nc.tensor.matmul_mx(
                 result[j // 2][b][:, j % 2, :],
-                lhsT=joint_codes[:, value_cols[j]].bitcast(FP8X4),
-                lhsT_scale=joint_scales[:, value_cols[j]],
+                lhsT=value_codes[j].bitcast(FP8X4),
+                lhsT_scale=value_scales[j],
                 rhs=joint_codes[:, weight_cols[b]].bitcast(FP8X4),
                 rhs_scale=joint_scales[:, weight_cols[b]],
                 start=True,

@@ -178,11 +178,11 @@ def tile_attend_multitoken_pl_kernel(tc, query, keys_words, keys_scales, c0, c1,
         minus_one = sb.tile([P, 1], F32, name="minus_one")
         nc.gpsimd.memset(minus_one[:], -1.0)
         inverses = []
-        after_cast = sb.tile([P, I // 2 + 32], F32, name="after_cast", tag="part1", align_bytes=64)
+        after_cast = sb.tile([P, I + 32], F32, name="after_cast", tag="part1", align_bytes=64)
         for b in range(BLOCKS):
             neg_max = sb.tile([P, 1], F32, name="neg_max%d" % b)
             nc.vector.tensor_reduce(neg_max[:], mixed[b], mybir.AxisListType.X, ALU.max, negate=True)
-            row_sum = after_cast[:, I // 2 + 16 * b : I // 2 + 16 * b + 1]
+            row_sum = after_cast[:, I + 16 * b : I + 16 * b + 1]
             prob = sb.tile([P, I], F32, name="prob%d" % b, tag="prob%d" % b, align_bytes=64)
             nc.scalar.activation(prob[:], mixed[b], ACT.Exp, bias=neg_max[:], accum_out=row_sum)
             inverse = sb.tile([P, 1], F32, name="inverse%d" % b)
@@ -190,13 +190,12 @@ def tile_attend_multitoken_pl_kernel(tc, query, keys_words, keys_scales, c0, c1,
             inverses.append(inverse)
             probs.append(prob)
 
-        turned = [turn([picked0[:]], "turn0", after_cast[:, 0 : I // 2].bitcast(BF16))]
-        first_codes = sb.tile([P, P], U32, name="first_codes", align_bytes=64)
-        first_scales = sb.tile([P, P], U8, name="first_scales", align_bytes=64)
-        nc.vector.quantize_mx(first_codes[:].bitcast(FP8X4), first_scales[:], turned[0])
+        turn([picked0[:]], "turn0", after_cast[:, 0 : I // 2].bitcast(BF16))
+        turned = [after_cast[:, 0:I].bitcast(BF16)]
         picked2 = gather_values(2, "picked2")
         nc.scalar.activation(picked1[:, EARLY:I], pool_bf[:].indirect(offsets[:, EARLY // 16 : I // 16]), ACT.Copy)
 
+        middle = turn([picked2[:], picked1], "turn2")
         weights_tile = sb.tile([P, BLOCKS, I], BF16, name="weights", tag="pool2", align_bytes=64)
         weights = [weights_tile[:, b, :] for b in range(BLOCKS)]
         for b in range(BLOCKS):
@@ -208,25 +207,25 @@ def tile_attend_multitoken_pl_kernel(tc, query, keys_words, keys_scales, c0, c1,
                 ALU.mult,
                 ALU.mult,
             )
-            turned.append(turn([weights[b], (picked2[:], picked1)[b]], "block%d" % b))
+            turned.append(turn([weights[b]], "block%d" % b, (after_cast[:, I // 2 : I].bitcast(BF16), None)[b]))
         picked3 = gather_values(3, "prob0")
         turned.append(turn([picked3[:]], "turn1"))
 
-        joint_codes = sb.tile([P, 5 * P], U32, name="joint_codes", tag="pool3", align_bytes=64)
-        joint_scales = sb.tile([P, 5 * P], U8, name="joint_scales", align_bytes=64)
+        joint_codes = sb.tile([P, 6 * P], U32, name="joint_codes", tag="pool3", align_bytes=64)
+        joint_scales = sb.tile([P, 6 * P], U8, name="joint_scales", align_bytes=64)
         start = 0
-        for target, count in zip(turned[1:], (2, 2, 1)):
+        for target, count in zip((turned[0], middle, turned[2], turned[3]), (2, 2, 1, 1)):
             cols = slice(start * P, (start + count) * P)
             nc.vector.quantize_mx(joint_codes[:, cols].bitcast(FP8X4), joint_scales[:, cols], target)
             start = start + count
-        weight_cols = [block_cols(0), block_cols(2)]
-        value_codes = [first_codes[:]] + [joint_codes[:, block_cols(n)] for n in (1, 3, 4)]
-        value_scales = [first_scales[:]] + [joint_scales[:, block_cols(n)] for n in (1, 3, 4)]
+        weight_cols = [block_cols(1), block_cols(4)]
+        value_codes = [joint_codes[:, block_cols(n)] for n in (0, 2, 3, 5)]
+        value_scales = [joint_scales[:, block_cols(n)] for n in (0, 2, 3, 5)]
 
         bank_tags = (("result0", "result1"), ("turn0", "size"))
         result = [[ps.tile([P, PAIRS, P], F32, name="result", tag=bank_tags[u][b]) for b in range(BLOCKS)] for u in range(PAIRS)]
         out_rows = out_0.rearrange("(p j) q -> p j q", j=PACK)
-        for j, b in ((0, 0), (1, 0), (0, 1), (1, 1), (2, 0), (2, 1), (3, 0), (3, 1)):
+        for j, b in ((0, 0), (1, 0), (0, 1), (1, 1), (2, 0), (3, 0), (2, 1), (3, 1)):
             nc.tensor.matmul_mx(
                 result[j // 2][b][:, j % 2, :],
                 lhsT=value_codes[j].bitcast(FP8X4),
@@ -237,7 +236,7 @@ def tile_attend_multitoken_pl_kernel(tc, query, keys_words, keys_scales, c0, c1,
                 stop=True,
             )
 
-        copies = (nc.vector.tensor_copy, nc.scalar.copy)
+        copies = (nc.scalar.copy, nc.vector.tensor_copy)
         out_bf = sb.tile([P, Q, PACK], BF16, name="out_bf", align_bytes=64)
         rows = [sb.tile([P, PAIRS, Q], F32, name="rows%d" % u, align_bytes=64) for u in range(PAIRS)]
 

@@ -24,6 +24,7 @@ BLOCKS = Q // P
 TAPS = 3
 QUADRANTS = 4
 EARLY = 128
+FIRST_AT, LATER_AT, SIZE_AT = 4, 8, 12
 TURN_BANKS = 3
 
 
@@ -52,13 +53,13 @@ def tile_attend_multitoken_pl_kernel(tc, query, keys_words, keys_scales, c0, c1,
         nc.vector.memset(key_bytes[:].bitcast(I32), 0)
         key_words = sb.tile([P, T], U16, name="key_words", align_bytes=64)
         nc.sync.dma_start(key_words[:].bitcast(I32), keys_words[0].bitcast(I32))
-        query_raw = sb.tile([P, PACK, Q], F32, name="query_raw", align_bytes=64)
-        nc.sync.dma_start(query_raw[:], query.rearrange("(p t) q -> p t q", t=PACK))
         for r in range(PACK):
             nc.sync.dma_start(
                 key_bytes[r : P : 32, :].bitcast(I32),
                 keys_scales[0].rearrange("(g r) t -> r g t", r=PACK)[r].bitcast(I32),
             )
+        query_raw = sb.tile([P, PACK, Q], F32, name="query_raw", align_bytes=64)
+        nc.sync.dma_start(query_raw[:], query.rearrange("(p t) q -> p t q", t=PACK))
         vals_rows = vals.rearrange("(m j) t -> j m t", j=PACK)
         val_pool = {j: sb.tile([P, T], F32, name="val_pool%d" % j, tag="pool%d" % j, align_bytes=64) for j in (0, 2, 3)}
         parts = (slice(0, T // 2), slice(T // 2, T))
@@ -68,14 +69,14 @@ def tile_attend_multitoken_pl_kernel(tc, query, keys_words, keys_scales, c0, c1,
         size_rows = sb.tile([P, P], F32, name="size_rows", align_bytes=64)
         for rows in (first_rows, later_rows, size_rows):
             nc.gpsimd.memset(rows[:], 0.0)
-        nc.sync.dma_start(first_rows[0:BLOCKS, :], c0.rearrange("(b m) o -> b (m o)", b=BLOCKS))
+        nc.sync.dma_start(first_rows[FIRST_AT : FIRST_AT + BLOCKS, :], c0.rearrange("(b m) o -> b (m o)", b=BLOCKS))
         nc.sync.dma_start(val_pool[0][:], vals_rows[0])
         for k, source in enumerate((c1, c2)):
-            nc.sync.dma_start(later_rows[k * BLOCKS : (k + 1) * BLOCKS, :], source.rearrange("(b m) o -> b (m o)", b=BLOCKS))
-        nc.sync.dma_start(size_rows[0:PACK, :], size.rearrange("o (r m) -> (o r) m", r=PACK))
+            nc.sync.dma_start(later_rows[LATER_AT + k * BLOCKS : LATER_AT + (k + 1) * BLOCKS, :], source.rearrange("(b m) o -> b (m o)", b=BLOCKS))
+        nc.sync.dma_start(size_rows[SIZE_AT : SIZE_AT + PACK, :], size.rearrange("o (r m) -> (o r) m", r=PACK))
         for h in range(2):
-            nc.sync.dma_start(halves[h][:], vals_rows[2][:, parts[h]])
-        nc.sync.dma_start(val_pool[2][:], vals_rows[1])
+            nc.sync.dma_start(halves[h][:], vals_rows[1][:, parts[h]])
+        nc.sync.dma_start(val_pool[2][:], vals_rows[2])
         nc.sync.dma_start(val_pool[3][:], vals_rows[3])
 
         identity = sb.tile([P, P], F32, name="identity")
@@ -84,7 +85,7 @@ def tile_attend_multitoken_pl_kernel(tc, query, keys_words, keys_scales, c0, c1,
         first_ps = ps.tile([P, P], F32, name="first_ps", tag="block0")
         nc.tensor.transpose(first_ps[:], first_rows[:], identity[:])
         first_cols = sb.tile([P, BLOCKS], F32, name="first_cols", align_bytes=64)
-        nc.scalar.copy(first_cols[:], first_ps[:, 0:BLOCKS])
+        nc.scalar.copy(first_cols[:], first_ps[:, FIRST_AT : FIRST_AT + BLOCKS])
 
         listed_words = sb.tile([P, I], U16, name="listed_words", align_bytes=64)
         nc.vector.tensor_copy(listed_words[:], key_words[:].indirect(offsets[:]))
@@ -127,11 +128,11 @@ def tile_attend_multitoken_pl_kernel(tc, query, keys_words, keys_scales, c0, c1,
 
         later_ps = ps.tile([P, P], F32, name="later_ps", tag="turn0")
         nc.tensor.transpose(later_ps[:], later_rows[:], identity[:])
-        factors = [first_cols, later_ps[:, 0:BLOCKS], later_ps[:, BLOCKS : 2 * BLOCKS]]
+        factors = [first_cols, later_ps[:, LATER_AT : LATER_AT + BLOCKS], later_ps[:, LATER_AT + BLOCKS : LATER_AT + 2 * BLOCKS]]
         size_turned = ps.tile([P, P], F32, name="size_turned", tag="result0")
         nc.tensor.transpose(size_turned[:], size_rows[:], identity[:])
         size_cols = sb.tile([P, PACK], F32, name="size_cols", align_bytes=64)
-        nc.scalar.copy(size_cols[:], size_turned[:, 0:PACK])
+        nc.scalar.copy(size_cols[:], size_turned[:, SIZE_AT : SIZE_AT + PACK])
 
         def turn(sources, tag, target=None):
             count = len(sources)
@@ -195,9 +196,10 @@ def tile_attend_multitoken_pl_kernel(tc, query, keys_words, keys_scales, c0, c1,
         picked2 = gather_values(2, "picked2")
         nc.scalar.activation(picked1[:, EARLY:I], pool_bf[:].indirect(offsets[:, EARLY // 16 : I // 16]), ACT.Copy)
 
-        middle = turn([picked2[:], picked1], "turn2")
-        weights_tile = sb.tile([P, BLOCKS, I], BF16, name="weights", tag="pool2", align_bytes=64)
-        weights = [weights_tile[:, b, :] for b in range(BLOCKS)]
+        trio = sb.tile([P, 3 * I], BF16, name="trio", align_bytes=64)
+        turn([picked2[:], picked1], "turn2", trio[:, 0 : 2 * I])
+        weights_tile = sb.tile([P, I], BF16, name="weights", align_bytes=64)
+        weights = [room[:, EARLY // 2 + I // 2 : EARLY // 2 + I].bitcast(BF16), weights_tile[:]]
         for b in range(BLOCKS):
             nc.vector.scalar_tensor_tensor(
                 weights[b],
@@ -207,20 +209,20 @@ def tile_attend_multitoken_pl_kernel(tc, query, keys_words, keys_scales, c0, c1,
                 ALU.mult,
                 ALU.mult,
             )
-            turned.append(turn([weights[b]], "block%d" % b, (after_cast[:, I // 2 : I].bitcast(BF16), None)[b]))
+            turned.append(turn([weights[b]], "block%d" % b, (after_cast[:, I // 2 : I].bitcast(BF16), trio[:, 2 * I : 3 * I])[b]))
         picked3 = gather_values(3, "prob0")
         turned.append(turn([picked3[:]], "turn1"))
 
         joint_codes = sb.tile([P, 6 * P], U32, name="joint_codes", tag="pool3", align_bytes=64)
         joint_scales = sb.tile([P, 6 * P], U8, name="joint_scales", align_bytes=64)
         start = 0
-        for target, count in zip((turned[0], middle, turned[2], turned[3]), (2, 2, 1, 1)):
+        for target, count in zip((turned[0], trio[:, I : 3 * I], trio[:, 0:I], turned[3]), (2, 2, 1, 1)):
             cols = slice(start * P, (start + count) * P)
             nc.vector.quantize_mx(joint_codes[:, cols].bitcast(FP8X4), joint_scales[:, cols], target)
             start = start + count
-        weight_cols = [block_cols(1), block_cols(4)]
-        value_codes = [joint_codes[:, block_cols(n)] for n in (0, 2, 3, 5)]
-        value_scales = [joint_scales[:, block_cols(n)] for n in (0, 2, 3, 5)]
+        weight_cols = [block_cols(1), block_cols(3)]
+        value_codes = [joint_codes[:, block_cols(n)] for n in (0, 2, 4, 5)]
+        value_scales = [joint_scales[:, block_cols(n)] for n in (0, 2, 4, 5)]
 
         bank_tags = (("result0", "result1"), ("turn0", "size"))
         result = [[ps.tile([P, PAIRS, P], F32, name="result", tag=bank_tags[u][b]) for b in range(BLOCKS)] for u in range(PAIRS)]

@@ -75,8 +75,8 @@ def tile_attend_multitoken_pl_kernel(tc, query, keys_words, keys_scales, c0, c1,
             nc.sync.dma_start(later_rows[LATER_AT + k * BLOCKS : LATER_AT + (k + 1) * BLOCKS, :], source.rearrange("(b m) o -> b (m o)", b=BLOCKS))
         nc.sync.dma_start(size_rows[SIZE_AT : SIZE_AT + PACK, :], size.rearrange("o (r m) -> (o r) m", r=PACK))
         for h in range(2):
-            nc.sync.dma_start(halves[h][:], vals_rows[1][:, parts[h]])
-        nc.sync.dma_start(val_pool[2][:], vals_rows[2])
+            nc.sync.dma_start(halves[h][:], vals_rows[2][:, parts[h]])
+        nc.sync.dma_start(val_pool[2][:], vals_rows[1])
         nc.sync.dma_start(val_pool[3][:], vals_rows[3])
 
         identity = sb.tile([P, P], F32, name="identity")
@@ -134,20 +134,14 @@ def tile_attend_multitoken_pl_kernel(tc, query, keys_words, keys_scales, c0, c1,
         size_cols = sb.tile([P, PACK], F32, name="size_cols", align_bytes=64)
         nc.scalar.copy(size_cols[:], size_turned[:, SIZE_AT : SIZE_AT + PACK])
 
-        def turn(sources, tag, target=None):
+        def turn(sources, tag, target):
             count = len(sources)
             bank = ps.tile([P, count, PAIRS, P], F32, name="turned", tag=tag)
             for n, rows_bf in enumerate(sources):
                 words = rows_bf.bitcast(F32)
                 for u in range(PAIRS):
                     nc.tensor.transpose(bank[:, n, u, :], words[:, u : I // 2 : PAIRS], identity[:])
-            if target is None:
-                target = sb.tile([P, count * P * PACK], BF16, name="turned_bf", tag="bf_" + tag, align_bytes=64)[:]
-            nc.scalar.copy(
-                target.bitcast(F32).rearrange("p (n m u) -> p n m u", n=count, u=PAIRS),
-                bank[:].rearrange("p n u m -> p n m u"),
-            )
-            return target
+            nc.scalar.copy(target, bank[:].rearrange("p n u m -> p n m u"))
 
         def gather_values(j, tag):
             picked = sb.tile([P, I], BF16, name="picked%d" % j, tag=tag, align_bytes=64)
@@ -179,11 +173,11 @@ def tile_attend_multitoken_pl_kernel(tc, query, keys_words, keys_scales, c0, c1,
         minus_one = sb.tile([P, 1], F32, name="minus_one")
         nc.gpsimd.memset(minus_one[:], -1.0)
         inverses = []
-        after_cast = sb.tile([P, I + 32], F32, name="after_cast", tag="part1", align_bytes=64)
+        after_cast = sb.tile([P, 32], F32, name="after_cast", tag="part1", align_bytes=64)
         for b in range(BLOCKS):
             neg_max = sb.tile([P, 1], F32, name="neg_max%d" % b)
             nc.vector.tensor_reduce(neg_max[:], mixed[b], mybir.AxisListType.X, ALU.max, negate=True)
-            row_sum = after_cast[:, I + 16 * b : I + 16 * b + 1]
+            row_sum = after_cast[:, 16 * b : 16 * b + 1]
             prob = sb.tile([P, I], F32, name="prob%d" % b, tag="prob%d" % b, align_bytes=64)
             nc.scalar.activation(prob[:], mixed[b], ACT.Exp, bias=neg_max[:], accum_out=row_sum)
             inverse = sb.tile([P, 1], F32, name="inverse%d" % b)
@@ -191,13 +185,12 @@ def tile_attend_multitoken_pl_kernel(tc, query, keys_words, keys_scales, c0, c1,
             inverses.append(inverse)
             probs.append(prob)
 
-        turn([picked0[:]], "turn0", after_cast[:, 0 : I // 2].bitcast(BF16))
-        turned = [after_cast[:, 0:I].bitcast(BF16)]
         picked2 = gather_values(2, "picked2")
         nc.scalar.activation(picked1[:, EARLY:I], pool_bf[:].indirect(offsets[:, EARLY // 16 : I // 16]), ACT.Copy)
 
-        trio = sb.tile([P, 3 * I], BF16, name="trio", align_bytes=64)
-        turn([picked2[:], picked1], "turn2", trio[:, 0 : 2 * I])
+        quad = sb.tile([P, 2 * I], F32, name="quad", align_bytes=64)
+        quad_parts = quad[:].rearrange("p (n k m u) -> p k n m u", n=BLOCKS, k=2, u=PAIRS)
+        turn([picked0[:], picked2[:]], "turn0", quad_parts[:, 0])
         weights_tile = sb.tile([P, I], BF16, name="weights", align_bytes=64)
         weights = [room[:, EARLY // 2 + I // 2 : EARLY // 2 + I].bitcast(BF16), weights_tile[:]]
         for b in range(BLOCKS):
@@ -209,25 +202,28 @@ def tile_attend_multitoken_pl_kernel(tc, query, keys_words, keys_scales, c0, c1,
                 ALU.mult,
                 ALU.mult,
             )
-            turned.append(turn([weights[b]], "block%d" % b, (after_cast[:, I // 2 : I].bitcast(BF16), trio[:, 2 * I : 3 * I])[b]))
+            turn([weights[b]], "block%d" % b, quad_parts[:, 1, b : b + 1])
         picked3 = gather_values(3, "prob0")
-        turned.append(turn([picked3[:]], "turn1"))
+        last = [sb.tile([P, 1, P, PAIRS], F32, name="last%d" % n, align_bytes=64) for n in range(2)]
+        turn([picked1], "size", last[0][:])
+        turn([picked3[:]], "turn1", last[1][:])
+        flat = [part[:].rearrange("p n m u -> p (n m u)") for part in last]
 
         joint_codes = sb.tile([P, 6 * P], U32, name="joint_codes", tag="pool3", align_bytes=64)
         joint_scales = sb.tile([P, 6 * P], U8, name="joint_scales", align_bytes=64)
         start = 0
-        for target, count in zip((turned[0], trio[:, I : 3 * I], trio[:, 0:I], turned[3]), (2, 2, 1, 1)):
+        for target, count in zip((quad[:, 0:I], quad[:, I : 2 * I], flat[0], flat[1]), (2, 2, 1, 1)):
             cols = slice(start * P, (start + count) * P)
-            nc.vector.quantize_mx(joint_codes[:, cols].bitcast(FP8X4), joint_scales[:, cols], target)
+            nc.vector.quantize_mx(joint_codes[:, cols].bitcast(FP8X4), joint_scales[:, cols], target.bitcast(BF16))
             start = start + count
         weight_cols = [block_cols(1), block_cols(3)]
         value_codes = [joint_codes[:, block_cols(n)] for n in (0, 2, 4, 5)]
         value_scales = [joint_scales[:, block_cols(n)] for n in (0, 2, 4, 5)]
 
-        bank_tags = (("result0", "result1"), ("turn0", "size"))
+        bank_tags = (("result0", "result1"), ("turn0", "turn2"))
         result = [[ps.tile([P, PAIRS, P], F32, name="result", tag=bank_tags[u][b]) for b in range(BLOCKS)] for u in range(PAIRS)]
         out_rows = out_0.rearrange("(p j) q -> p j q", j=PACK)
-        for j, b in ((0, 0), (1, 0), (0, 1), (1, 1), (2, 0), (3, 0), (2, 1), (3, 1)):
+        for j, b in ((0, 0), (1, 0), (0, 1), (1, 1), (2, 0), (2, 1), (3, 0), (3, 1)):
             nc.tensor.matmul_mx(
                 result[j // 2][b][:, j % 2, :],
                 lhsT=value_codes[j].bitcast(FP8X4),
@@ -253,9 +249,9 @@ def tile_attend_multitoken_pl_kernel(tc, query, keys_words, keys_scales, c0, c1,
         copy_rows(0)
         nc.sync.dma_start(out_rows[:, 0:PAIRS, :], rows[0][:])
         copy_places(0)
-        copy_places(1)
         copy_rows(1)
-        nc.scalar.dma_start(out_rows[:, PAIRS:PACK, :], rows[1][:])
+        nc.sync.dma_start(out_rows[:, PAIRS:PACK, :], rows[1][:])
+        copy_places(1)
 
         out_codes = sb.tile([P, Q], U32, name="out_codes", align_bytes=64)
         out_scales = sb.tile([P, Q], U8, name="out_scales", align_bytes=64)
@@ -267,7 +263,7 @@ def tile_attend_multitoken_pl_kernel(tc, query, keys_words, keys_scales, c0, c1,
             )
         nc.sync.dma_start(out_1[0].rearrange("p c r -> p (c r)").bitcast(I32), out_codes[:].bitcast(I32))
         for quadrant in range(QUADRANTS):
-            queue = nc.sync if quadrant < QUADRANTS // 2 else nc.scalar
+            queue = nc.sync if quadrant < 1 else nc.scalar
             queue.dma_start(
                 out_2[0, scale_rows(quadrant), :].bitcast(I32),
                 out_scales[scale_partitions(quadrant), :].bitcast(I32),

@@ -23,7 +23,7 @@ PAIRS = PACK // 2
 BLOCKS = Q // P
 TAPS = 3
 QUADRANTS = 4
-EARLY = 128
+EARLY = 64
 FIRST_AT, LATER_AT, SIZE_AT = 4, 8, 12
 TURN_BANKS = 3
 
@@ -153,6 +153,8 @@ def tile_attend_multitoken_pl_kernel(tc, query, keys_words, keys_scales, c0, c1,
         for h in range(2):
             nc.scalar.activation(pool_bf[:, parts[h]], halves[h][:], ACT.Copy)
 
+        after_cast = sb.tile([P, I // 2 + 16], F32, name="after_cast", tag="part1", align_bytes=64)
+        turn([picked0[:]], "result0", after_cast[:, 0 : I // 2].rearrange("p (n m u) -> p n m u", n=1, u=PAIRS))
         picked1 = room[:, 0 : I // 2].bitcast(BF16)
         nc.scalar.activation(picked1[:, 0:EARLY], pool_bf[:].indirect(offsets[:, 0 : EARLY // 16]), ACT.Copy)
         size_ps = ps.tile([P, PACK, P], F32, name="size_ps", tag="size")
@@ -173,11 +175,10 @@ def tile_attend_multitoken_pl_kernel(tc, query, keys_words, keys_scales, c0, c1,
         minus_one = sb.tile([P, 1], F32, name="minus_one")
         nc.gpsimd.memset(minus_one[:], -1.0)
         inverses = []
-        after_cast = sb.tile([P, 32], F32, name="after_cast", tag="part1", align_bytes=64)
         for b in range(BLOCKS):
             neg_max = sb.tile([P, 1], F32, name="neg_max%d" % b)
             nc.vector.tensor_reduce(neg_max[:], mixed[b], mybir.AxisListType.X, ALU.max, negate=True)
-            row_sum = after_cast[:, 16 * b : 16 * b + 1]
+            row_sum = after_cast[:, I // 2 + b : I // 2 + b + 1]
             prob = sb.tile([P, I], F32, name="prob%d" % b, tag="prob%d" % b, align_bytes=64)
             nc.scalar.activation(prob[:], mixed[b], ACT.Exp, bias=neg_max[:], accum_out=row_sum)
             inverse = sb.tile([P, 1], F32, name="inverse%d" % b)
@@ -185,12 +186,20 @@ def tile_attend_multitoken_pl_kernel(tc, query, keys_words, keys_scales, c0, c1,
             inverses.append(inverse)
             probs.append(prob)
 
-        picked2 = gather_values(2, "picked2")
+        first_codes = sb.tile([P, P], U32, name="first_codes", align_bytes=64)
+        first_scales = sb.tile([P, P], U8, name="first_scales", align_bytes=64)
+        nc.vector.quantize_mx(first_codes[:].bitcast(FP8X4), first_scales[:], after_cast[:, 0 : I // 2].bitcast(BF16))
+        picked2 = sb.tile([P, I], BF16, name="picked2", align_bytes=64)
+        for h in range(2):
+            nc.vector.tensor_copy(
+                picked2[:, h * I // 2 : (h + 1) * I // 2],
+                val_pool[2][:].indirect(offsets[:, h * I // 32 : (h + 1) * I // 32]),
+            )
         nc.scalar.activation(picked1[:, EARLY:I], pool_bf[:].indirect(offsets[:, EARLY // 16 : I // 16]), ACT.Copy)
 
-        quad = sb.tile([P, 2 * I], F32, name="quad", align_bytes=64)
-        quad_parts = quad[:].rearrange("p (n k m u) -> p k n m u", n=BLOCKS, k=2, u=PAIRS)
-        turn([picked0[:], picked2[:]], "turn0", quad_parts[:, 0])
+        quad = sb.tile([P, 3 * I // 2], F32, name="quad", align_bytes=64)
+        quad_parts = quad[:].rearrange("p (n m u) -> p n m u", n=3, u=PAIRS)
+        turn([picked2[:]], "turn0", quad_parts[:, 1:2])
         weights_tile = sb.tile([P, I], BF16, name="weights", align_bytes=64)
         weights = [room[:, EARLY // 2 + I // 2 : EARLY // 2 + I].bitcast(BF16), weights_tile[:]]
         for b in range(BLOCKS):
@@ -202,23 +211,23 @@ def tile_attend_multitoken_pl_kernel(tc, query, keys_words, keys_scales, c0, c1,
                 ALU.mult,
                 ALU.mult,
             )
-            turn([weights[b]], "block%d" % b, quad_parts[:, 1, b : b + 1])
+            turn([weights[b]], "block%d" % b, quad_parts[:, 2 * b : 2 * b + 1])
         picked3 = gather_values(3, "prob0")
         last = [sb.tile([P, 1, P, PAIRS], F32, name="last%d" % n, align_bytes=64) for n in range(2)]
         turn([picked1], "size", last[0][:])
         turn([picked3[:]], "turn1", last[1][:])
         flat = [part[:].rearrange("p n m u -> p (n m u)") for part in last]
 
-        joint_codes = sb.tile([P, 6 * P], U32, name="joint_codes", tag="pool3", align_bytes=64)
-        joint_scales = sb.tile([P, 6 * P], U8, name="joint_scales", align_bytes=64)
+        joint_codes = sb.tile([P, 5 * P], U32, name="joint_codes", tag="pool3", align_bytes=64)
+        joint_scales = sb.tile([P, 5 * P], U8, name="joint_scales", align_bytes=64)
         start = 0
-        for target, count in zip((quad[:, 0:I], quad[:, I : 2 * I], flat[0], flat[1]), (2, 2, 1, 1)):
+        for target, count in zip((quad[:, 0 : I // 2], quad[:, I // 2 : 3 * I // 2], flat[0], flat[1]), (1, 2, 1, 1)):
             cols = slice(start * P, (start + count) * P)
             nc.vector.quantize_mx(joint_codes[:, cols].bitcast(FP8X4), joint_scales[:, cols], target.bitcast(BF16))
             start = start + count
-        weight_cols = [block_cols(1), block_cols(3)]
-        value_codes = [joint_codes[:, block_cols(n)] for n in (0, 2, 4, 5)]
-        value_scales = [joint_scales[:, block_cols(n)] for n in (0, 2, 4, 5)]
+        weight_cols = [block_cols(0), block_cols(2)]
+        value_codes = [first_codes[:]] + [joint_codes[:, block_cols(n)] for n in (1, 3, 4)]
+        value_scales = [first_scales[:]] + [joint_scales[:, block_cols(n)] for n in (1, 3, 4)]
 
         bank_tags = (("result0", "result1"), ("turn0", "turn2"))
         result = [[ps.tile([P, PAIRS, P], F32, name="result", tag=bank_tags[u][b]) for b in range(BLOCKS)] for u in range(PAIRS)]

@@ -22,10 +22,17 @@ PACK = 4
 PAIRS = PACK // 2
 BLOCKS = Q // P
 TAPS = 3
-QUADRANTS = 4
+QUADRANT = 32
+QUADRANTS = P // QUADRANT
+SCALE_ROWS = 4
+PER_COLUMN = 16
+WORDS = I // 2
+SIZE_ROWS = I // P
+SUMS_ROOM = 16
+HALVES = 2
 EARLY = 64
 FIRST_AT, LATER_AT, SIZE_AT = 4, 8, 12
-TURN_BANKS = 3
+SYNC_SCALE_STORES = 1
 
 
 def block_cols(b):
@@ -33,11 +40,11 @@ def block_cols(b):
 
 
 def scale_partitions(quadrant):
-    return slice(32 * quadrant, 32 * quadrant + 4)
+    return slice(QUADRANT * quadrant, QUADRANT * quadrant + SCALE_ROWS)
 
 
 def scale_rows(quadrant):
-    return slice(4 * quadrant, 4 * quadrant + 4)
+    return slice(SCALE_ROWS * quadrant, SCALE_ROWS * (quadrant + 1))
 
 
 def tile_attend_multitoken_pl_kernel(tc, query, keys_words, keys_scales, c0, c1, c2, size, vals, offs, out_0, out_1, out_2):
@@ -46,37 +53,40 @@ def tile_attend_multitoken_pl_kernel(tc, query, keys_words, keys_scales, c0, c1,
         sb = ctx.enter_context(tc.tile_pool(name="sb", bufs=1))
         ps = ctx.enter_context(tc.psum_pool(name="ps", bufs=1))
 
-        offsets = sb.tile([P, I // 16], U16, name="offsets")
+        offsets = sb.tile([P, I // PER_COLUMN], U16, name="offsets")
         nc.sync.dma_start(offsets[:], offs)
 
         key_bytes = sb.tile([P, T], U8, name="key_bytes", align_bytes=64)
         nc.vector.memset(key_bytes[:].bitcast(I32), 0)
         key_words = sb.tile([P, T], U16, name="key_words", align_bytes=64)
         nc.sync.dma_start(key_words[:].bitcast(I32), keys_words[0].bitcast(I32))
-        for r in range(PACK):
+        for r in range(SCALE_ROWS):
             nc.sync.dma_start(
-                key_bytes[r : P : 32, :].bitcast(I32),
-                keys_scales[0].rearrange("(g r) t -> r g t", r=PACK)[r].bitcast(I32),
+                key_bytes[r:P:QUADRANT, :].bitcast(I32),
+                keys_scales[0].rearrange("(g r) t -> r g t", r=SCALE_ROWS)[r].bitcast(I32),
             )
         query_raw = sb.tile([P, PACK, Q], F32, name="query_raw", align_bytes=64)
         nc.sync.dma_start(query_raw[:], query.rearrange("(p t) q -> p t q", t=PACK))
+
         vals_rows = vals.rearrange("(m j) t -> j m t", j=PACK)
-        val_pool = {j: sb.tile([P, T], F32, name="val_pool%d" % j, tag="pool%d" % j, align_bytes=64) for j in (0, 2, 3)}
-        parts = (slice(0, T // 2), slice(T // 2, T))
-        halves = [sb.tile([P, part.stop - part.start], F32, name="part%d" % h, tag="part%d" % h, align_bytes=64) for h, part in enumerate(parts)]
+        val_pool = {j: sb.tile([P, T], F32, name="val_pool%d" % j, tag="pool%d" % j, align_bytes=64) for j in (0, 1, 3)}
+        parts = [slice(h * T // HALVES, (h + 1) * T // HALVES) for h in range(HALVES)]
+        halves = [sb.tile([P, T // HALVES], F32, name="half%d" % h, tag="half%d" % h, align_bytes=64) for h in range(HALVES)]
+
         first_rows = sb.tile([P, P], F32, name="first_rows", tag="first", align_bytes=64)
         later_rows = sb.tile([P, P], F32, name="later_rows", align_bytes=64)
         size_rows = sb.tile([P, P], F32, name="size_rows", align_bytes=64)
-        for rows in (first_rows, later_rows, size_rows):
-            nc.gpsimd.memset(rows[:], 0.0)
+        for zeroed in (first_rows, later_rows, size_rows):
+            nc.gpsimd.memset(zeroed[:], 0.0)
         nc.sync.dma_start(first_rows[FIRST_AT : FIRST_AT + BLOCKS, :], c0.rearrange("(b m) o -> b (m o)", b=BLOCKS))
         nc.sync.dma_start(val_pool[0][:], vals_rows[0])
         for k, source in enumerate((c1, c2)):
-            nc.sync.dma_start(later_rows[LATER_AT + k * BLOCKS : LATER_AT + (k + 1) * BLOCKS, :], source.rearrange("(b m) o -> b (m o)", b=BLOCKS))
-        nc.sync.dma_start(size_rows[SIZE_AT : SIZE_AT + PACK, :], size.rearrange("o (r m) -> (o r) m", r=PACK))
-        for h in range(2):
+            row = LATER_AT + k * BLOCKS
+            nc.sync.dma_start(later_rows[row : row + BLOCKS, :], source.rearrange("(b m) o -> b (m o)", b=BLOCKS))
+        nc.sync.dma_start(size_rows[SIZE_AT : SIZE_AT + SIZE_ROWS, :], size.rearrange("o (r m) -> (o r) m", r=SIZE_ROWS))
+        for h in range(HALVES):
             nc.sync.dma_start(halves[h][:], vals_rows[2][:, parts[h]])
-        nc.sync.dma_start(val_pool[2][:], vals_rows[1])
+        nc.sync.dma_start(val_pool[1][:], vals_rows[1])
         nc.sync.dma_start(val_pool[3][:], vals_rows[3])
 
         identity = sb.tile([P, P], F32, name="identity")
@@ -108,6 +118,7 @@ def tile_attend_multitoken_pl_kernel(tc, query, keys_words, keys_scales, c0, c1,
             )
 
         scores = []
+        rooms = []
         mixed = []
         for b in range(BLOCKS):
             score = ps.tile([P, I], F32, name="score%d" % b, tag="block%d" % b)
@@ -121,87 +132,78 @@ def tile_attend_multitoken_pl_kernel(tc, query, keys_words, keys_scales, c0, c1,
                 stop=True,
             )
             scores.append(score)
-            room = sb.tile([P, EARLY // 2 + I], F32, name="mixed%d" % b, align_bytes=64)
-            mix = room[:, EARLY // 2 : EARLY // 2 + I]
-            nc.scalar.activation(mix, score[:], ACT.Copy, scale=first_cols[:, b : b + 1])
-            mixed.append(mix)
+            room = sb.tile([P, EARLY // 2 + I], F32, name="room%d" % b, align_bytes=64)
+            rooms.append(room)
+            mixed.append(room[:, EARLY // 2 : EARLY // 2 + I])
+            nc.scalar.activation(mixed[b], score[:], ACT.Copy, scale=first_cols[:, b : b + 1])
 
-        later_ps = ps.tile([P, P], F32, name="later_ps", tag="turn0")
+        later_ps = ps.tile([P, P], F32, name="later_ps", tag="later")
         nc.tensor.transpose(later_ps[:], later_rows[:], identity[:])
-        factors = [first_cols, later_ps[:, LATER_AT : LATER_AT + BLOCKS], later_ps[:, LATER_AT + BLOCKS : LATER_AT + 2 * BLOCKS]]
-        size_turned = ps.tile([P, P], F32, name="size_turned", tag="result0")
+        size_turned = ps.tile([P, P], F32, name="size_turned", tag="small")
         nc.tensor.transpose(size_turned[:], size_rows[:], identity[:])
-        size_cols = sb.tile([P, PACK], F32, name="size_cols", align_bytes=64)
-        nc.scalar.copy(size_cols[:], size_turned[:, SIZE_AT : SIZE_AT + PACK])
+        size_cols = sb.tile([P, SIZE_ROWS], F32, name="size_cols", align_bytes=64)
+        nc.scalar.copy(size_cols[:], size_turned[:, SIZE_AT : SIZE_AT + SIZE_ROWS])
 
-        def turn(sources, tag, target):
-            count = len(sources)
-            bank = ps.tile([P, count, PAIRS, P], F32, name="turned", tag=tag)
-            for n, rows_bf in enumerate(sources):
-                words = rows_bf.bitcast(F32)
-                for u in range(PAIRS):
-                    nc.tensor.transpose(bank[:, n, u, :], words[:, u : I // 2 : PAIRS], identity[:])
-            nc.scalar.copy(target, bank[:].rearrange("p n u m -> p n m u"))
+        def turn(rows_bf, tag, target):
+            bank = ps.tile([P, PAIRS, P], F32, name="turned", tag=tag)
+            words = rows_bf.bitcast(F32)
+            for u in range(PAIRS):
+                nc.tensor.transpose(bank[:, u, :], words[:, u:WORDS:PAIRS], identity[:])
+            nc.scalar.copy(target.rearrange("p (m u) -> p m u", u=PAIRS), bank[:].rearrange("p u m -> p m u"))
 
-        def gather_values(j, tag):
-            picked = sb.tile([P, I], BF16, name="picked%d" % j, tag=tag, align_bytes=64)
-            nc.vector.tensor_copy(picked[:], val_pool[j][:].indirect(offsets[:]))
-            return picked
+        def listed(window, begin, end):
+            return window[:].indirect(offsets[:, begin // PER_COLUMN : end // PER_COLUMN])
 
-        picked0 = gather_values(0, "picked0")
+        picked0 = sb.tile([P, I], BF16, name="picked0", align_bytes=64)
+        nc.vector.tensor_copy(picked0[:], listed(val_pool[0], 0, I))
         pool_bf = sb.tile([P, T], BF16, name="pool_bf", align_bytes=64)
-        for h in range(2):
+        for h in range(HALVES):
             nc.scalar.activation(pool_bf[:, parts[h]], halves[h][:], ACT.Copy)
 
-        after_cast = sb.tile([P, I // 2 + 16], F32, name="after_cast", tag="part1", align_bytes=64)
-        turn([picked0[:]], "result0", after_cast[:, 0 : I // 2].rearrange("p (n m u) -> p n m u", n=1, u=PAIRS))
-        picked1 = room[:, 0 : I // 2].bitcast(BF16)
-        nc.scalar.activation(picked1[:, 0:EARLY], pool_bf[:].indirect(offsets[:, 0 : EARLY // 16]), ACT.Copy)
-        size_ps = ps.tile([P, PACK, P], F32, name="size_ps", tag="size")
-        for t in range(PACK):
-            nc.tensor.transpose(size_ps[:, t, :], size_cols[:, t : t + 1].to_broadcast([P, P]), identity[:])
+        after_cast = sb.tile([P, WORDS + SUMS_ROOM], F32, name="after_cast", tag="half1", align_bytes=64)
+        turned0 = after_cast[:, 0:WORDS]
+        turn(picked0[:], "small", turned0)
+        picked2 = rooms[1][:, 0:WORDS].bitcast(BF16)
+        nc.scalar.activation(picked2[:, 0:EARLY], listed(pool_bf, 0, EARLY), ACT.Copy)
+        size_ps = ps.tile([P, SIZE_ROWS, P], F32, name="size_ps", tag="size")
+        for r in range(SIZE_ROWS):
+            nc.tensor.transpose(size_ps[:, r, :], size_cols[:, r : r + 1].to_broadcast([P, P]), identity[:])
 
         for tap in range(1, TAPS):
             for b in range(BLOCKS):
+                column = LATER_AT + (tap - 1) * BLOCKS + b
                 nc.vector.scalar_tensor_tensor(
                     mixed[b][:, tap:I],
                     scores[b][:, 0 : I - tap],
-                    factors[tap][:, b : b + 1],
+                    later_ps[:, column : column + 1],
                     mixed[b][:, tap:I],
                     ALU.mult,
                     ALU.add,
                 )
         probs = []
-        minus_one = sb.tile([P, 1], F32, name="minus_one")
-        nc.gpsimd.memset(minus_one[:], -1.0)
-        inverses = []
+        inverses = [sb.tile([P, 1], F32, name="inverse%d" % b) for b in range(BLOCKS)]
         for b in range(BLOCKS):
             neg_max = sb.tile([P, 1], F32, name="neg_max%d" % b)
             nc.vector.tensor_reduce(neg_max[:], mixed[b], mybir.AxisListType.X, ALU.max, negate=True)
-            row_sum = after_cast[:, I // 2 + b : I // 2 + b + 1]
+            row_sum = after_cast[:, WORDS + b : WORDS + b + 1]
             prob = sb.tile([P, I], F32, name="prob%d" % b, tag="prob%d" % b, align_bytes=64)
             nc.scalar.activation(prob[:], mixed[b], ACT.Exp, bias=neg_max[:], accum_out=row_sum)
-            inverse = sb.tile([P, 1], F32, name="inverse%d" % b)
-            nc.gpsimd.tensor_tensor(inverse[:], row_sum, minus_one[:], ALU.pow)
-            inverses.append(inverse)
             probs.append(prob)
 
-        first_codes = sb.tile([P, P], U32, name="first_codes", align_bytes=64)
-        first_scales = sb.tile([P, P], U8, name="first_scales", align_bytes=64)
-        nc.vector.quantize_mx(first_codes[:].bitcast(FP8X4), first_scales[:], after_cast[:, 0 : I // 2].bitcast(BF16))
-        picked2 = sb.tile([P, I], BF16, name="picked2", align_bytes=64)
-        for h in range(2):
-            nc.vector.tensor_copy(
-                picked2[:, h * I // 2 : (h + 1) * I // 2],
-                val_pool[2][:].indirect(offsets[:, h * I // 32 : (h + 1) * I // 32]),
-            )
-        nc.scalar.activation(picked1[:, EARLY:I], pool_bf[:].indirect(offsets[:, EARLY // 16 : I // 16]), ACT.Copy)
+        codes0 = sb.tile([P, P], U32, name="codes0", align_bytes=64)
+        scales0 = sb.tile([P, P], U8, name="scales0", align_bytes=64)
+        nc.vector.quantize_mx(codes0[:].bitcast(FP8X4), scales0[:], turned0.bitcast(BF16))
+        picked1 = sb.tile([P, I], BF16, name="picked1", align_bytes=64)
+        for h in range(HALVES):
+            begin, end = h * I // HALVES, (h + 1) * I // HALVES
+            nc.vector.tensor_copy(picked1[:, begin:end], listed(val_pool[1], begin, end))
+            nc.vector.reciprocal(inverses[h][:], after_cast[:, WORDS + h : WORDS + h + 1])
+        nc.scalar.activation(picked2[:, EARLY:I], listed(pool_bf, EARLY, I), ACT.Copy)
 
-        quad = sb.tile([P, 3 * I // 2], F32, name="quad", align_bytes=64)
-        quad_parts = quad[:].rearrange("p (n m u) -> p n m u", n=3, u=PAIRS)
-        turn([picked2[:]], "turn0", quad_parts[:, 1:2])
-        weights_tile = sb.tile([P, I], BF16, name="weights", align_bytes=64)
-        weights = [room[:, EARLY // 2 + I // 2 : EARLY // 2 + I].bitcast(BF16), weights_tile[:]]
+        trio = sb.tile([P, 3 * WORDS], F32, name="trio", align_bytes=64)
+        turn(picked1[:], "later", trio[:, WORDS : 2 * WORDS])
+        weights1 = sb.tile([P, I], BF16, name="weights1", align_bytes=64)
+        weights = [rooms[1][:, EARLY // 2 + WORDS : EARLY // 2 + I].bitcast(BF16), weights1[:]]
         for b in range(BLOCKS):
             nc.vector.scalar_tensor_tensor(
                 weights[b],
@@ -211,30 +213,33 @@ def tile_attend_multitoken_pl_kernel(tc, query, keys_words, keys_scales, c0, c1,
                 ALU.mult,
                 ALU.mult,
             )
-            turn([weights[b]], "block%d" % b, quad_parts[:, 2 * b : 2 * b + 1])
-        picked3 = gather_values(3, "prob0")
-        last = [sb.tile([P, 1, P, PAIRS], F32, name="last%d" % n, align_bytes=64) for n in range(2)]
-        turn([picked1], "size", last[0][:])
-        turn([picked3[:]], "turn1", last[1][:])
-        flat = [part[:].rearrange("p n m u -> p (n m u)") for part in last]
+            turn(weights[b], "block%d" % b, trio[:, 2 * b * WORDS : (2 * b + 1) * WORDS])
+        picked3 = sb.tile([P, I], BF16, name="picked3", tag="prob0", align_bytes=64)
+        nc.vector.tensor_copy(picked3[:], listed(val_pool[3], 0, I))
+        turned2 = sb.tile([P, WORDS], F32, name="turned2", align_bytes=64)
+        turned3 = sb.tile([P, WORDS], F32, name="turned3", align_bytes=64)
+        turn(picked2, "size", turned2[:])
+        turn(picked3[:], "last", turned3[:])
 
-        joint_codes = sb.tile([P, 5 * P], U32, name="joint_codes", tag="pool3", align_bytes=64)
-        joint_scales = sb.tile([P, 5 * P], U8, name="joint_scales", align_bytes=64)
-        start = 0
-        for target, count in zip((quad[:, 0 : I // 2], quad[:, I // 2 : 3 * I // 2], flat[0], flat[1]), (1, 2, 1, 1)):
-            cols = slice(start * P, (start + count) * P)
-            nc.vector.quantize_mx(joint_codes[:, cols].bitcast(FP8X4), joint_scales[:, cols], target.bitcast(BF16))
-            start = start + count
+        sources = (trio[:, 0:WORDS], trio[:, WORDS : 3 * WORDS], turned2[:], turned3[:])
+        widths = (1, 2, 1, 1)
+        joint_codes = sb.tile([P, sum(widths) * P], U32, name="joint_codes", tag="pool3", align_bytes=64)
+        joint_scales = sb.tile([P, sum(widths) * P], U8, name="joint_scales", align_bytes=64)
+        for n, source in enumerate(sources):
+            cols = slice(sum(widths[:n]) * P, sum(widths[: n + 1]) * P)
+            nc.vector.quantize_mx(joint_codes[:, cols].bitcast(FP8X4), joint_scales[:, cols], source.bitcast(BF16))
         weight_cols = [block_cols(0), block_cols(2)]
-        value_codes = [first_codes[:]] + [joint_codes[:, block_cols(n)] for n in (1, 3, 4)]
-        value_scales = [first_scales[:]] + [joint_scales[:, block_cols(n)] for n in (1, 3, 4)]
+        value_cols = [block_cols(1), block_cols(3), block_cols(4)]
+        value_codes = [codes0[:]] + [joint_codes[:, cols] for cols in value_cols]
+        value_scales = [scales0[:]] + [joint_scales[:, cols] for cols in value_cols]
 
-        bank_tags = (("result0", "result1"), ("turn0", "turn2"))
+        bank_tags = (("small", "result1"), ("later", "result3"))
         result = [[ps.tile([P, PAIRS, P], F32, name="result", tag=bank_tags[u][b]) for b in range(BLOCKS)] for u in range(PAIRS)]
-        out_rows = out_0.rearrange("(p j) q -> p j q", j=PACK)
-        for j, b in ((0, 0), (1, 0), (0, 1), (1, 1), (2, 0), (2, 1), (3, 0), (3, 1)):
+        first_pair = [(j, b) for b in range(BLOCKS) for j in range(PAIRS)]
+        second_pair = [(j, b) for j in range(PAIRS, PACK) for b in range(BLOCKS)]
+        for j, b in first_pair + second_pair:
             nc.tensor.matmul_mx(
-                result[j // 2][b][:, j % 2, :],
+                result[j // PAIRS][b][:, j % PAIRS, :],
                 lhsT=value_codes[j].bitcast(FP8X4),
                 lhsT_scale=value_scales[j],
                 rhs=joint_codes[:, weight_cols[b]].bitcast(FP8X4),
@@ -244,23 +249,16 @@ def tile_attend_multitoken_pl_kernel(tc, query, keys_words, keys_scales, c0, c1,
             )
 
         copies = (nc.scalar.copy, nc.vector.tensor_copy)
+        out_rows = out_0.rearrange("(p j) q -> p j q", j=PACK)
         out_bf = sb.tile([P, Q, PACK], BF16, name="out_bf", align_bytes=64)
         rows = [sb.tile([P, PAIRS, Q], F32, name="rows%d" % u, align_bytes=64) for u in range(PAIRS)]
-
-        def copy_rows(u):
+        for u in range(PAIRS):
+            places = slice(PAIRS * u, PAIRS * (u + 1))
             for b in range(BLOCKS):
                 copies[b](rows[u][:, :, block_cols(b)], result[u][b][:])
-
-        def copy_places(u):
+            nc.sync.dma_start(out_rows[:, places, :], rows[u][:])
             for b in range(BLOCKS):
-                copies[b](out_bf[:, block_cols(b), 2 * u : 2 * u + 2], result[u][b][:].rearrange("p j n -> p n j"))
-
-        copy_rows(0)
-        nc.sync.dma_start(out_rows[:, 0:PAIRS, :], rows[0][:])
-        copy_places(0)
-        copy_rows(1)
-        nc.sync.dma_start(out_rows[:, PAIRS:PACK, :], rows[1][:])
-        copy_places(1)
+                copies[b](out_bf[:, block_cols(b), places], result[u][b][:].rearrange("p j n -> p n j"))
 
         out_codes = sb.tile([P, Q], U32, name="out_codes", align_bytes=64)
         out_scales = sb.tile([P, Q], U8, name="out_scales", align_bytes=64)
@@ -272,7 +270,7 @@ def tile_attend_multitoken_pl_kernel(tc, query, keys_words, keys_scales, c0, c1,
             )
         nc.sync.dma_start(out_1[0].rearrange("p c r -> p (c r)").bitcast(I32), out_codes[:].bitcast(I32))
         for quadrant in range(QUADRANTS):
-            queue = nc.sync if quadrant < 1 else nc.scalar
+            queue = nc.sync if quadrant < SYNC_SCALE_STORES else nc.scalar
             queue.dma_start(
                 out_2[0, scale_rows(quadrant), :].bitcast(I32),
                 out_scales[scale_partitions(quadrant), :].bitcast(I32),

@@ -31,6 +31,7 @@ SIZE_ROWS = I // P
 SUMS_ROOM = 16
 HALVES = 2
 EARLY = 64
+POOL_BYTES = 4 * T
 FIRST_AT, LATER_AT, SIZE_AT = 4, 8, 12
 SYNC_SCALE_STORES = 1
 
@@ -51,6 +52,7 @@ def tile_attend_multitoken_pl_kernel(tc, query, keys_words, keys_scales, c0, c1,
     nc = tc.nc
     with ExitStack() as ctx:
         sb = ctx.enter_context(tc.tile_pool(name="sb", bufs=1))
+        shared = ctx.enter_context(tc.tile_pool(name="shared", bufs=1))
         ps = ctx.enter_context(tc.psum_pool(name="ps", bufs=1))
 
         offsets = sb.tile([P, I // PER_COLUMN], U16, name="offsets")
@@ -69,9 +71,7 @@ def tile_attend_multitoken_pl_kernel(tc, query, keys_words, keys_scales, c0, c1,
         nc.sync.dma_start(query_raw[:], query.rearrange("(p t) q -> p t q", t=PACK))
 
         vals_rows = vals.rearrange("(m j) t -> j m t", j=PACK)
-        val_pool = {j: sb.tile([P, T], F32, name="val_pool%d" % j, tag="pool%d" % j, align_bytes=64) for j in (0, 1, 3)}
-        parts = [slice(h * T // HALVES, (h + 1) * T // HALVES) for h in range(HALVES)]
-        halves = [sb.tile([P, T // HALVES], F32, name="half%d" % h, tag="half%d" % h, align_bytes=64) for h in range(HALVES)]
+        val_pool = [shared.tile([P, T], F32, name="val_pool%d" % j, offset=j * POOL_BYTES, align_bytes=64) for j in range(PACK)]
 
         first_rows = sb.tile([P, P], F32, name="first_rows", tag="first", align_bytes=64)
         later_rows = sb.tile([P, P], F32, name="later_rows", align_bytes=64)
@@ -84,10 +84,8 @@ def tile_attend_multitoken_pl_kernel(tc, query, keys_words, keys_scales, c0, c1,
             row = LATER_AT + k * BLOCKS
             nc.sync.dma_start(later_rows[row : row + BLOCKS, :], source.rearrange("(b m) o -> b (m o)", b=BLOCKS))
         nc.sync.dma_start(size_rows[SIZE_AT : SIZE_AT + SIZE_ROWS, :], size.rearrange("o (r m) -> (o r) m", r=SIZE_ROWS))
-        for h in range(HALVES):
-            nc.sync.dma_start(halves[h][:], vals_rows[2][:, parts[h]])
-        nc.sync.dma_start(val_pool[1][:], vals_rows[1])
-        nc.sync.dma_start(val_pool[3][:], vals_rows[3])
+        for j in range(1, PACK):
+            nc.sync.dma_start(val_pool[j][:], vals_rows[j])
 
         identity = sb.tile([P, P], F32, name="identity")
         make_identity(nc, identity[:])
@@ -118,7 +116,6 @@ def tile_attend_multitoken_pl_kernel(tc, query, keys_words, keys_scales, c0, c1,
             )
 
         scores = []
-        rooms = []
         mixed = []
         for b in range(BLOCKS):
             score = ps.tile([P, I], F32, name="score%d" % b, tag="block%d" % b)
@@ -132,9 +129,8 @@ def tile_attend_multitoken_pl_kernel(tc, query, keys_words, keys_scales, c0, c1,
                 stop=True,
             )
             scores.append(score)
-            room = sb.tile([P, EARLY // 2 + I], F32, name="room%d" % b, align_bytes=64)
-            rooms.append(room)
-            mixed.append(room[:, EARLY // 2 : EARLY // 2 + I])
+            mix = sb.tile([P, I], F32, name="mixed%d" % b, align_bytes=64)
+            mixed.append(mix[:])
             nc.scalar.activation(mixed[b], score[:], ACT.Copy, scale=first_cols[:, b : b + 1])
 
         later_ps = ps.tile([P, P], F32, name="later_ps", tag="later")
@@ -144,30 +140,32 @@ def tile_attend_multitoken_pl_kernel(tc, query, keys_words, keys_scales, c0, c1,
         size_cols = sb.tile([P, SIZE_ROWS], F32, name="size_cols", align_bytes=64)
         nc.scalar.copy(size_cols[:], size_turned[:, SIZE_AT : SIZE_AT + SIZE_ROWS])
 
-        def turn(rows_bf, tag, target):
+        def turn(rows_bf, tag):
             bank = ps.tile([P, PAIRS, P], F32, name="turned", tag=tag)
             words = rows_bf.bitcast(F32)
             for u in range(PAIRS):
                 nc.tensor.transpose(bank[:, u, :], words[:, u:WORDS:PAIRS], identity[:])
-            nc.scalar.copy(target.rearrange("p (m u) -> p m u", u=PAIRS), bank[:].rearrange("p u m -> p m u"))
+            return bank
 
-        def listed(window, begin, end):
-            return window[:].indirect(offsets[:, begin // PER_COLUMN : end // PER_COLUMN])
+        def weave(copy, target, bank):
+            copy(target.rearrange("p (m u) -> p m u", u=PAIRS), bank[:].rearrange("p u m -> p m u"))
 
-        picked0 = sb.tile([P, I], BF16, name="picked0", align_bytes=64)
-        nc.vector.tensor_copy(picked0[:], listed(val_pool[0], 0, I))
-        pool_bf = sb.tile([P, T], BF16, name="pool_bf", align_bytes=64)
-        for h in range(HALVES):
-            nc.scalar.activation(pool_bf[:, parts[h]], halves[h][:], ACT.Copy)
+        def listed(j, begin, end):
+            return val_pool[j][:].indirect(offsets[:, begin // PER_COLUMN : end // PER_COLUMN])
 
-        after_cast = sb.tile([P, WORDS + SUMS_ROOM], F32, name="after_cast", tag="half1", align_bytes=64)
-        turned0 = after_cast[:, 0:WORDS]
-        turn(picked0[:], "small", turned0)
-        picked2 = rooms[1][:, 0:WORDS].bitcast(BF16)
-        nc.scalar.activation(picked2[:, 0:EARLY], listed(pool_bf, 0, EARLY), ACT.Copy)
-        size_ps = ps.tile([P, SIZE_ROWS, P], F32, name="size_ps", tag="size")
-        for r in range(SIZE_ROWS):
-            nc.tensor.transpose(size_ps[:, r, :], size_cols[:, r : r + 1].to_broadcast([P, P]), identity[:])
+        def quantise(codes, scales, source):
+            nc.vector.quantize_mx(codes.bitcast(FP8X4), scales, source.bitcast(BF16))
+
+        picked = {j: sb.tile([P, I], BF16, name="picked%d" % j, align_bytes=64) for j in (0, 2, 3)}
+        nc.vector.tensor_copy(picked[0][:], listed(0, 0, I))
+        turned01 = sb.tile([P, 2 * WORDS], F32, name="turned01", align_bytes=64)
+        weave(nc.scalar.copy, turned01[:, 0:WORDS], turn(picked[0][:], "small"))
+        size_ps = [ps.tile([P, SIZE_ROWS, P], F32, name="size_ps", tag="size%d" % b) for b in range(BLOCKS)]
+        for b in range(BLOCKS):
+            for r in range(SIZE_ROWS):
+                nc.tensor.transpose(size_ps[b][:, r, :], size_cols[:, r : r + 1].to_broadcast([P, P]), identity[:])
+        picked[1] = sb.tile([P, I], BF16, name="picked1", align_bytes=64)
+        nc.scalar.activation(picked[1][:], listed(1, 0, I), ACT.Copy)
 
         for tap in range(1, TAPS):
             for b in range(BLOCKS):
@@ -180,70 +178,65 @@ def tile_attend_multitoken_pl_kernel(tc, query, keys_words, keys_scales, c0, c1,
                     ALU.mult,
                     ALU.add,
                 )
-        probs = []
+        probs = shared.tile([P, BLOCKS, I], F32, name="probs", offset=POOL_BYTES, align_bytes=64)
+        sums = [sb.tile([P, 1], F32, name="sum%d" % b) for b in range(BLOCKS)]
+        neg_maxes = [sb.tile([P, 1], F32, name="neg_max%d" % b) for b in range(BLOCKS)]
         inverses = [sb.tile([P, 1], F32, name="inverse%d" % b) for b in range(BLOCKS)]
         for b in range(BLOCKS):
-            neg_max = sb.tile([P, 1], F32, name="neg_max%d" % b)
+            neg_max = neg_maxes[b]
             nc.vector.tensor_reduce(neg_max[:], mixed[b], mybir.AxisListType.X, ALU.max, negate=True)
-            row_sum = after_cast[:, WORDS + b : WORDS + b + 1]
-            prob = sb.tile([P, I], F32, name="prob%d" % b, tag="prob%d" % b, align_bytes=64)
-            nc.scalar.activation(prob[:], mixed[b], ACT.Exp, bias=neg_max[:], accum_out=row_sum)
-            probs.append(prob)
+            nc.scalar.activation(probs[:, b, :], mixed[b], ACT.Exp, bias=neg_max[:], accum_out=sums[b][:])
 
-        codes0 = sb.tile([P, P], U32, name="codes0", align_bytes=64)
-        scales0 = sb.tile([P, P], U8, name="scales0", align_bytes=64)
-        nc.vector.quantize_mx(codes0[:].bitcast(FP8X4), scales0[:], turned0.bitcast(BF16))
-        picked1 = sb.tile([P, I], BF16, name="picked1", align_bytes=64)
-        for h in range(HALVES):
-            begin, end = h * I // HALVES, (h + 1) * I // HALVES
-            nc.vector.tensor_copy(picked1[:, begin:end], listed(val_pool[1], begin, end))
-            nc.vector.reciprocal(inverses[h][:], after_cast[:, WORDS + h : WORDS + h + 1])
-        nc.scalar.activation(picked2[:, EARLY:I], listed(pool_bf, EARLY, I), ACT.Copy)
+        weave(nc.vector.tensor_copy, turned01[:, WORDS : 2 * WORDS], turn(picked[1][:], "mid"))
+        nc.scalar.activation(picked[2][:], listed(2, 0, I), ACT.Copy)
 
-        trio = sb.tile([P, 3 * WORDS], F32, name="trio", align_bytes=64)
-        turn(picked1[:], "later", trio[:, WORDS : 2 * WORDS])
-        weights1 = sb.tile([P, I], BF16, name="weights1", align_bytes=64)
-        weights = [rooms[1][:, EARLY // 2 + WORDS : EARLY // 2 + I].bitcast(BF16), weights1[:]]
+        codes01 = sb.tile([P, 2 * P], U32, name="codes01", align_bytes=64)
+        scales01 = sb.tile([P, 2 * P], U8, name="scales01", align_bytes=64)
+        weights = []
         for b in range(BLOCKS):
+            nc.vector.reciprocal(inverses[b][:], sums[b][:])
+            quantise(codes01[:, block_cols(b)], scales01[:, block_cols(b)], turned01[:, b * WORDS : (b + 1) * WORDS])
+            weight = sb.tile([P, I], BF16, name="weights%d" % b, align_bytes=64)
             nc.vector.scalar_tensor_tensor(
-                weights[b],
-                probs[b][:],
+                weight[:],
+                probs[:, b, :],
                 inverses[b][:],
-                size_ps[:].rearrange("p r m -> p (r m)"),
+                size_ps[b][:].rearrange("p r m -> p (r m)"),
                 ALU.mult,
                 ALU.mult,
             )
-            turn(weights[b], "block%d" % b, trio[:, 2 * b * WORDS : (2 * b + 1) * WORDS])
-        picked3 = sb.tile([P, I], BF16, name="picked3", tag="prob0", align_bytes=64)
-        nc.vector.tensor_copy(picked3[:], listed(val_pool[3], 0, I))
-        turned2 = sb.tile([P, WORDS], F32, name="turned2", align_bytes=64)
-        turned3 = sb.tile([P, WORDS], F32, name="turned3", align_bytes=64)
-        turn(picked2, "size", turned2[:])
-        turn(picked3[:], "last", turned3[:])
+            weights.append(weight)
+        early = sb.tile([P, 2 * WORDS], F32, name="early", align_bytes=64)
+        turned_w0, turned2 = early[:, 0:WORDS], early[:, WORDS : 2 * WORDS]
+        bank_w0 = turn(weights[0][:], "block0")
+        bank2 = turn(picked[2][:], "size0")
+        bank_w1 = turn(weights[1][:], "block1")
+        weave(nc.vector.tensor_copy, turned_w0, bank_w0)
+        weave(nc.vector.tensor_copy, turned2, bank2)
+        nc.scalar.activation(picked[3][:], listed(3, 0, I), ACT.Copy)
+        late = shared.tile([P, 2 * WORDS], F32, name="late", offset=3 * POOL_BYTES, align_bytes=64)
+        turned_w1, turned3 = late[:, 0:WORDS], late[:, WORDS : 2 * WORDS]
+        late_codes = shared.tile([P, PACK * P], U32, name="late_codes", offset=3 * POOL_BYTES + 2048, align_bytes=64)
+        late_scales = sb.tile([P, PACK * P], U8, name="late_scales", align_bytes=64)
+        weave(nc.scalar.copy, turned_w1, bank_w1)
+        bank3 = turn(picked[3][:], "size1")
+        weave(nc.scalar.copy, turned3, bank3)
+        for n, source in ((0, turned_w0), (2, turned2), (1, turned_w1), (3, turned3)):
+            quantise(late_codes[:, block_cols(n)], late_scales[:, block_cols(n)], source)
+        weight_cols = [block_cols(0), block_cols(1)]
+        value_codes = [codes01[:, block_cols(0)], codes01[:, block_cols(1)], late_codes[:, block_cols(2)], late_codes[:, block_cols(3)]]
+        value_scales = [scales01[:, block_cols(0)], scales01[:, block_cols(1)], late_scales[:, block_cols(2)], late_scales[:, block_cols(3)]]
 
-        sources = (trio[:, 0:WORDS], trio[:, WORDS : 3 * WORDS], turned2[:], turned3[:])
-        widths = (1, 2, 1, 1)
-        joint_codes = sb.tile([P, sum(widths) * P], U32, name="joint_codes", tag="pool3", align_bytes=64)
-        joint_scales = sb.tile([P, sum(widths) * P], U8, name="joint_scales", align_bytes=64)
-        for n, source in enumerate(sources):
-            cols = slice(sum(widths[:n]) * P, sum(widths[: n + 1]) * P)
-            nc.vector.quantize_mx(joint_codes[:, cols].bitcast(FP8X4), joint_scales[:, cols], source.bitcast(BF16))
-        weight_cols = [block_cols(0), block_cols(2)]
-        value_cols = [block_cols(1), block_cols(3), block_cols(4)]
-        value_codes = [codes0[:]] + [joint_codes[:, cols] for cols in value_cols]
-        value_scales = [scales0[:]] + [joint_scales[:, cols] for cols in value_cols]
-
-        bank_tags = (("small", "result1"), ("later", "result3"))
+        bank_tags = (("small", "mid"), ("later", "result3"))
         result = [[ps.tile([P, PAIRS, P], F32, name="result", tag=bank_tags[u][b]) for b in range(BLOCKS)] for u in range(PAIRS)]
-        first_pair = [(j, b) for b in range(BLOCKS) for j in range(PAIRS)]
-        second_pair = [(j, b) for j in range(PAIRS, PACK) for b in range(BLOCKS)]
-        for j, b in first_pair + second_pair:
+        order = [(j, b) for b in range(BLOCKS) for j in range(PACK - 1)] + [(PACK - 1, b) for b in range(BLOCKS)]
+        for j, b in order:
             nc.tensor.matmul_mx(
                 result[j // PAIRS][b][:, j % PAIRS, :],
                 lhsT=value_codes[j].bitcast(FP8X4),
                 lhsT_scale=value_scales[j],
-                rhs=joint_codes[:, weight_cols[b]].bitcast(FP8X4),
-                rhs_scale=joint_scales[:, weight_cols[b]],
+                rhs=late_codes[:, weight_cols[b]].bitcast(FP8X4),
+                rhs_scale=late_scales[:, weight_cols[b]],
                 start=True,
                 stop=True,
             )

@@ -31,6 +31,7 @@ SIZE_ROWS = I // P
 SUMS_ROOM = 16
 HALVES = 2
 EARLY = 64
+SHARE3 = 96
 POOL_BYTES = 4 * T
 FIRST_AT, LATER_AT, SIZE_AT = 4, 8, 12
 SYNC_SCALE_STORES = 1
@@ -140,11 +141,11 @@ def tile_attend_multitoken_pl_kernel(tc, query, keys_words, keys_scales, c0, c1,
         size_cols = sb.tile([P, SIZE_ROWS], F32, name="size_cols", align_bytes=64)
         nc.scalar.copy(size_cols[:], size_turned[:, SIZE_AT : SIZE_AT + SIZE_ROWS])
 
-        def turn(rows_bf, tag):
+        def turn(rows_bf, tag, dealt=False):
             bank = ps.tile([P, PAIRS, P], F32, name="turned", tag=tag)
             words = rows_bf.bitcast(F32)
             for u in range(PAIRS):
-                nc.tensor.transpose(bank[:, u, :], words[:, u:WORDS:PAIRS], identity[:])
+                nc.tensor.transpose(bank[:, u, :], words[:, block_cols(u)] if dealt else words[:, u:WORDS:PAIRS], identity[:])
             return bank
 
         def weave(copy, target, bank):
@@ -192,36 +193,44 @@ def tile_attend_multitoken_pl_kernel(tc, query, keys_words, keys_scales, c0, c1,
 
         codes01 = sb.tile([P, 2 * P], U32, name="codes01", align_bytes=64)
         scales01 = sb.tile([P, 2 * P], U8, name="scales01", align_bytes=64)
-        weights = []
-        for b in range(BLOCKS):
-            nc.vector.reciprocal(inverses[b][:], sums[b][:])
-            quantise(codes01[:, block_cols(b)], scales01[:, block_cols(b)], turned01[:, b * WORDS : (b + 1) * WORDS])
-            weight = sb.tile([P, I], BF16, name="weights%d" % b, align_bytes=64)
+        weights = [sb.tile([P, I], BF16, name="weights%d" % b, align_bytes=64) for b in range(BLOCKS)]
+
+        def weigh(b, u):
+            pair = slice(2 * u, 2 * u + 2)
             nc.vector.scalar_tensor_tensor(
-                weight[:],
-                probs[:, b, :],
+                weights[b][:, u * WORDS : (u + 1) * WORDS].rearrange("p (m e) -> p m e", e=2),
+                probs[:, b, :].rearrange("p (m t) -> p m t", t=PACK)[:, :, pair],
                 inverses[b][:],
-                size_ps[b][:].rearrange("p r m -> p (r m)"),
+                size_ps[b][:].rearrange("p r (m t) -> p (r m) t", t=PACK)[:, :, pair],
                 ALU.mult,
                 ALU.mult,
             )
-            weights.append(weight)
-        early = sb.tile([P, 2 * WORDS], F32, name="early", align_bytes=64)
-        turned_w0, turned2 = early[:, 0:WORDS], early[:, WORDS : 2 * WORDS]
-        bank_w0 = turn(weights[0][:], "block0")
+
+        nc.vector.reciprocal(inverses[0][:], sums[0][:])
+        quantise(codes01[:, block_cols(0)], scales01[:, block_cols(0)], turned01[:, 0:WORDS])
+        weigh(0, 0)
+        nc.vector.reciprocal(inverses[1][:], sums[1][:])
+        weigh(0, 1)
+        weigh(1, 0)
+        weigh(1, 1)
+        turned_w0 = sb.tile([P, WORDS], F32, name="turned_w0", align_bytes=64)
+        bank_w0 = turn(weights[0][:], "block0", dealt=True)
         bank2 = turn(picked[2][:], "size0")
-        bank_w1 = turn(weights[1][:], "block1")
-        weave(nc.vector.tensor_copy, turned_w0, bank_w0)
-        weave(nc.vector.tensor_copy, turned2, bank2)
-        nc.scalar.activation(picked[3][:], listed(3, 0, I), ACT.Copy)
-        late = shared.tile([P, 2 * WORDS], F32, name="late", offset=3 * POOL_BYTES, align_bytes=64)
-        turned_w1, turned3 = late[:, 0:WORDS], late[:, WORDS : 2 * WORDS]
-        late_codes = shared.tile([P, PACK * P], U32, name="late_codes", offset=3 * POOL_BYTES + 2048, align_bytes=64)
-        late_scales = sb.tile([P, PACK * P], U8, name="late_scales", align_bytes=64)
-        weave(nc.scalar.copy, turned_w1, bank_w1)
+        bank_w1 = turn(weights[1][:], "block1", dealt=True)
+        quantise(codes01[:, block_cols(1)], scales01[:, block_cols(1)], turned01[:, WORDS : 2 * WORDS])
+        weave(nc.vector.tensor_copy, turned_w0[:], bank_w0)
+        nc.vector.tensor_copy(picked[3][:, 0:SHARE3], listed(3, 0, SHARE3))
+        nc.scalar.activation(picked[3][:, SHARE3:I], listed(3, SHARE3, I), ACT.Copy)
         bank3 = turn(picked[3][:], "size1")
+        late = shared.tile([P, 3 * WORDS], F32, name="late", offset=3 * POOL_BYTES, align_bytes=64)
+        turned2, turned_w1, turned3 = (late[:, n * WORDS : (n + 1) * WORDS] for n in range(3))
+        late_codes = shared.tile([P, PACK * P], U32, name="late_codes", offset=3 * POOL_BYTES + 3072, align_bytes=64)
+        late_scales = sb.tile([P, PACK * P], U8, name="late_scales", align_bytes=64)
+        quantise(late_codes[:, block_cols(0)], late_scales[:, block_cols(0)], turned_w0[:])
+        weave(nc.vector.tensor_copy, turned2, bank2)
+        weave(nc.scalar.copy, turned_w1, bank_w1)
         weave(nc.scalar.copy, turned3, bank3)
-        for n, source in ((0, turned_w0), (2, turned2), (1, turned_w1), (3, turned3)):
+        for n, source in ((1, turned_w1), (2, turned2), (3, turned3)):
             quantise(late_codes[:, block_cols(n)], late_scales[:, block_cols(n)], source)
         weight_cols = [block_cols(0), block_cols(1)]
         value_codes = [codes01[:, block_cols(0)], codes01[:, block_cols(1)], late_codes[:, block_cols(2)], late_codes[:, block_cols(3)]]
@@ -229,7 +238,7 @@ def tile_attend_multitoken_pl_kernel(tc, query, keys_words, keys_scales, c0, c1,
 
         bank_tags = (("small", "mid"), ("later", "result3"))
         result = [[ps.tile([P, PAIRS, P], F32, name="result", tag=bank_tags[u][b]) for b in range(BLOCKS)] for u in range(PAIRS)]
-        order = [(j, b) for b in range(BLOCKS) for j in range(PACK - 1)] + [(PACK - 1, b) for b in range(BLOCKS)]
+        order = [(j, b) for b in range(BLOCKS) for j in range(PAIRS)] + [(j, b) for j in range(PAIRS, PACK) for b in range(BLOCKS)]
         for j, b in order:
             nc.tensor.matmul_mx(
                 result[j // PAIRS][b][:, j % PAIRS, :],

@@ -28,11 +28,10 @@ SCALE_ROWS = 4
 PER_COLUMN = 16
 WORDS = I // 2
 SIZE_ROWS = I // P
-SUMS_ROOM = 16
-HALVES = 2
-EARLY = 64
-SHARE3 = 96
-POOL_BYTES = 4 * T
+WORD_BYTES = 4
+POOL_BYTES = WORD_BYTES * T
+SHARE0 = I // 2
+SHARE3 = 192
 FIRST_AT, LATER_AT, SIZE_AT = 4, 8, 12
 SYNC_SCALE_STORES = 1
 
@@ -72,7 +71,9 @@ def tile_attend_multitoken_pl_kernel(tc, query, keys_words, keys_scales, c0, c1,
         nc.sync.dma_start(query_raw[:], query.rearrange("(p t) q -> p t q", t=PACK))
 
         vals_rows = vals.rearrange("(m j) t -> j m t", j=PACK)
-        val_pool = [shared.tile([P, T], F32, name="val_pool%d" % j, offset=j * POOL_BYTES, align_bytes=64) for j in range(PACK)]
+        val_pool = [
+            shared.tile([P, T], F32, name="val_pool%d" % j, offset=j * POOL_BYTES, align_bytes=64) for j in range(PACK)
+        ]
 
         first_rows = sb.tile([P, P], F32, name="first_rows", tag="first", align_bytes=64)
         later_rows = sb.tile([P, P], F32, name="later_rows", align_bytes=64)
@@ -93,8 +94,9 @@ def tile_attend_multitoken_pl_kernel(tc, query, keys_words, keys_scales, c0, c1,
 
         first_ps = ps.tile([P, P], F32, name="first_ps", tag="block0")
         nc.tensor.transpose(first_ps[:], first_rows[:], identity[:])
-        first_cols = sb.tile([P, BLOCKS], F32, name="first_cols", align_bytes=64)
-        nc.scalar.copy(first_cols[:], first_ps[:, FIRST_AT : FIRST_AT + BLOCKS])
+        room0 = sb.tile([P, WORDS], F32, name="room0", align_bytes=64)
+        first_cols = room0[:, WORDS - BLOCKS : WORDS]
+        nc.scalar.copy(first_cols, first_ps[:, FIRST_AT : FIRST_AT + BLOCKS])
 
         listed_words = sb.tile([P, I], U16, name="listed_words", align_bytes=64)
         nc.vector.tensor_copy(listed_words[:], key_words[:].indirect(offsets[:]))
@@ -130,9 +132,8 @@ def tile_attend_multitoken_pl_kernel(tc, query, keys_words, keys_scales, c0, c1,
                 stop=True,
             )
             scores.append(score)
-            mix = sb.tile([P, I], F32, name="mixed%d" % b, align_bytes=64)
-            mixed.append(mix[:])
-            nc.scalar.activation(mixed[b], score[:], ACT.Copy, scale=first_cols[:, b : b + 1])
+            mixed.append(sb.tile([P, I], F32, name="mixed%d" % b, align_bytes=64))
+            nc.scalar.activation(mixed[b][:], score[:], ACT.Copy, scale=first_cols[:, b : b + 1])
 
         later_ps = ps.tile([P, P], F32, name="later_ps", tag="later")
         nc.tensor.transpose(later_ps[:], later_rows[:], identity[:])
@@ -141,12 +142,14 @@ def tile_attend_multitoken_pl_kernel(tc, query, keys_words, keys_scales, c0, c1,
         size_cols = sb.tile([P, SIZE_ROWS], F32, name="size_cols", align_bytes=64)
         nc.scalar.copy(size_cols[:], size_turned[:, SIZE_AT : SIZE_AT + SIZE_ROWS])
 
-        def turn(rows_bf, tag, dealt=False):
+        def turn(halves, tag):
             bank = ps.tile([P, PAIRS, P], F32, name="turned", tag=tag)
-            words = rows_bf.bitcast(F32)
             for u in range(PAIRS):
-                nc.tensor.transpose(bank[:, u, :], words[:, block_cols(u)] if dealt else words[:, u:WORDS:PAIRS], identity[:])
+                nc.tensor.transpose(bank[:, u, :], halves[u], identity[:])
             return bank
+
+        def alternate(rows_bf):
+            return [rows_bf.bitcast(F32)[:, u:WORDS:PAIRS] for u in range(PAIRS)]
 
         def weave(copy, target, bank):
             copy(target.rearrange("p (m u) -> p m u", u=PAIRS), bank[:].rearrange("p u m -> p m u"))
@@ -154,19 +157,22 @@ def tile_attend_multitoken_pl_kernel(tc, query, keys_words, keys_scales, c0, c1,
         def listed(j, begin, end):
             return val_pool[j][:].indirect(offsets[:, begin // PER_COLUMN : end // PER_COLUMN])
 
-        def quantise(codes, scales, source):
-            nc.vector.quantize_mx(codes.bitcast(FP8X4), scales, source.bitcast(BF16))
+        def quantise(codes, scales, woven):
+            nc.vector.quantize_mx(codes.bitcast(FP8X4), scales, woven.bitcast(BF16))
 
-        picked = {j: sb.tile([P, I], BF16, name="picked%d" % j, align_bytes=64) for j in (0, 2, 3)}
-        nc.vector.tensor_copy(picked[0][:], listed(0, 0, I))
-        turned01 = sb.tile([P, 2 * WORDS], F32, name="turned01", align_bytes=64)
-        weave(nc.scalar.copy, turned01[:, 0:WORDS], turn(picked[0][:], "small"))
+        picked0 = room0[:].bitcast(BF16)
+        nc.vector.tensor_copy(picked0[:, 0:SHARE0], listed(0, 0, SHARE0))
+        nc.scalar.activation(picked0[:, SHARE0:I], listed(0, SHARE0, I), ACT.Copy)
+        bank0 = turn(alternate(picked0), "small")
         size_ps = [ps.tile([P, SIZE_ROWS, P], F32, name="size_ps", tag="size%d" % b) for b in range(BLOCKS)]
         for b in range(BLOCKS):
             for r in range(SIZE_ROWS):
                 nc.tensor.transpose(size_ps[b][:, r, :], size_cols[:, r : r + 1].to_broadcast([P, P]), identity[:])
-        picked[1] = sb.tile([P, I], BF16, name="picked1", align_bytes=64)
-        nc.scalar.activation(picked[1][:], listed(1, 0, I), ACT.Copy)
+        picked1 = sb.tile([P, I], BF16, name="picked1", align_bytes=64)
+        nc.scalar.activation(picked1[:], listed(1, 0, I), ACT.Copy)
+        woven01 = shared.tile([P, 2 * WORDS], F32, name="woven01", offset=POOL_BYTES + WORD_BYTES * BLOCKS * I, align_bytes=64)
+        woven0, woven1 = woven01[:, 0:WORDS], woven01[:, WORDS : 2 * WORDS]
+        weave(nc.scalar.copy, woven0, bank0)
 
         for tap in range(1, TAPS):
             for b in range(BLOCKS):
@@ -181,24 +187,22 @@ def tile_attend_multitoken_pl_kernel(tc, query, keys_words, keys_scales, c0, c1,
                 )
         probs = shared.tile([P, BLOCKS, I], F32, name="probs", offset=POOL_BYTES, align_bytes=64)
         sums = [sb.tile([P, 1], F32, name="sum%d" % b) for b in range(BLOCKS)]
-        neg_maxes = [sb.tile([P, 1], F32, name="neg_max%d" % b) for b in range(BLOCKS)]
         inverses = [sb.tile([P, 1], F32, name="inverse%d" % b) for b in range(BLOCKS)]
         for b in range(BLOCKS):
-            neg_max = neg_maxes[b]
-            nc.vector.tensor_reduce(neg_max[:], mixed[b], mybir.AxisListType.X, ALU.max, negate=True)
-            nc.scalar.activation(probs[:, b, :], mixed[b], ACT.Exp, bias=neg_max[:], accum_out=sums[b][:])
+            neg_max = sb.tile([P, 1], F32, name="neg_max%d" % b)
+            nc.vector.tensor_reduce(neg_max[:], mixed[b][:], mybir.AxisListType.X, ALU.max, negate=True)
+            nc.scalar.activation(probs[:, b, :], mixed[b][:], ACT.Exp, bias=neg_max[:], accum_out=sums[b][:])
 
-        weave(nc.vector.tensor_copy, turned01[:, WORDS : 2 * WORDS], turn(picked[1][:], "mid"))
-        nc.scalar.activation(picked[2][:], listed(2, 0, I), ACT.Copy)
+        weave(nc.vector.tensor_copy, woven1, turn(alternate(picked1[:]), "mid"))
+        picked2 = sb.tile([P, I], BF16, name="picked2", align_bytes=64)
+        nc.scalar.activation(picked2[:], listed(2, 0, I), ACT.Copy)
 
-        codes01 = sb.tile([P, 2 * P], U32, name="codes01", align_bytes=64)
-        scales01 = sb.tile([P, 2 * P], U8, name="scales01", align_bytes=64)
-        weights = [sb.tile([P, I], BF16, name="weights%d" % b, align_bytes=64) for b in range(BLOCKS)]
+        weights = [sb.tile([P, PAIRS, WORDS], BF16, name="weights%d" % b, align_bytes=64) for b in range(BLOCKS)]
 
         def weigh(b, u):
             pair = slice(2 * u, 2 * u + 2)
             nc.vector.scalar_tensor_tensor(
-                weights[b][:, u * WORDS : (u + 1) * WORDS].rearrange("p (m e) -> p m e", e=2),
+                weights[b][:, u, :].rearrange("p (m e) -> p m e", e=2),
                 probs[:, b, :].rearrange("p (m t) -> p m t", t=PACK)[:, :, pair],
                 inverses[b][:],
                 size_ps[b][:].rearrange("p r (m t) -> p (r m) t", t=PACK)[:, :, pair],
@@ -206,40 +210,51 @@ def tile_attend_multitoken_pl_kernel(tc, query, keys_words, keys_scales, c0, c1,
                 ALU.mult,
             )
 
+        codes0 = sb.tile([P, P], U32, name="codes0", align_bytes=64)
+        scales0 = sb.tile([P, P], U8, name="scales0", align_bytes=64)
         nc.vector.reciprocal(inverses[0][:], sums[0][:])
-        quantise(codes01[:, block_cols(0)], scales01[:, block_cols(0)], turned01[:, 0:WORDS])
+        quantise(codes0[:], scales0[:], woven0)
         weigh(0, 0)
         nc.vector.reciprocal(inverses[1][:], sums[1][:])
         weigh(0, 1)
         weigh(1, 0)
         weigh(1, 1)
-        turned_w0 = sb.tile([P, WORDS], F32, name="turned_w0", align_bytes=64)
-        bank_w0 = turn(weights[0][:], "block0", dealt=True)
-        bank2 = turn(picked[2][:], "size0")
-        bank_w1 = turn(weights[1][:], "block1", dealt=True)
-        quantise(codes01[:, block_cols(1)], scales01[:, block_cols(1)], turned01[:, WORDS : 2 * WORDS])
-        weave(nc.vector.tensor_copy, turned_w0[:], bank_w0)
-        nc.vector.tensor_copy(picked[3][:, 0:SHARE3], listed(3, 0, SHARE3))
-        nc.scalar.activation(picked[3][:, SHARE3:I], listed(3, SHARE3, I), ACT.Copy)
-        bank3 = turn(picked[3][:], "size1")
-        late = shared.tile([P, 3 * WORDS], F32, name="late", offset=3 * POOL_BYTES, align_bytes=64)
-        turned2, turned_w1, turned3 = (late[:, n * WORDS : (n + 1) * WORDS] for n in range(3))
-        late_codes = shared.tile([P, PACK * P], U32, name="late_codes", offset=3 * POOL_BYTES + 3072, align_bytes=64)
-        late_scales = sb.tile([P, PACK * P], U8, name="late_scales", align_bytes=64)
-        quantise(late_codes[:, block_cols(0)], late_scales[:, block_cols(0)], turned_w0[:])
-        weave(nc.vector.tensor_copy, turned2, bank2)
-        weave(nc.scalar.copy, turned_w1, bank_w1)
-        weave(nc.scalar.copy, turned3, bank3)
-        for n, source in ((1, turned_w1), (2, turned2), (3, turned3)):
-            quantise(late_codes[:, block_cols(n)], late_scales[:, block_cols(n)], source)
-        weight_cols = [block_cols(0), block_cols(1)]
-        value_codes = [codes01[:, block_cols(0)], codes01[:, block_cols(1)], late_codes[:, block_cols(2)], late_codes[:, block_cols(3)]]
-        value_scales = [scales01[:, block_cols(0)], scales01[:, block_cols(1)], late_scales[:, block_cols(2)], late_scales[:, block_cols(3)]]
+
+        weight_halves = [[weights[b][:, u, :].bitcast(F32) for u in range(PAIRS)] for b in range(BLOCKS)]
+        bank_w0 = turn(weight_halves[0], "block0")
+        bank2 = turn(alternate(picked2[:]), "size0")
+        bank_w1 = turn(weight_halves[1], "block1")
+        woven_w0 = sb.tile([P, WORDS], F32, name="woven_w0", align_bytes=64)
+        weave(nc.vector.tensor_copy, woven_w0[:], bank_w0)
+        picked3 = sb.tile([P, I], BF16, name="picked3", align_bytes=64)
+        nc.vector.tensor_copy(picked3[:, 0:SHARE3], listed(3, 0, SHARE3))
+        nc.scalar.activation(picked3[:, SHARE3:I], listed(3, SHARE3, I), ACT.Copy)
+        bank3 = turn(alternate(picked3[:]), "size1")
+
+        late_banks = (bank_w1, bank2, bank3)
+        late = shared.tile([P, len(late_banks) * WORDS], F32, name="late", offset=3 * POOL_BYTES, align_bytes=64)
+        late_woven = [late[:, n * WORDS : (n + 1) * WORDS] for n in range(len(late_banks))]
+        ready = [woven_w0[:], woven1]
+        blocks = len(ready) + len(late_banks)
+        codes_at = 3 * POOL_BYTES + WORD_BYTES * len(late_banks) * WORDS
+        late_codes = shared.tile([P, blocks * P], U32, name="late_codes", offset=codes_at, align_bytes=64)
+        late_scales = sb.tile([P, blocks * P], U8, name="late_scales", align_bytes=64)
+        for n, woven in enumerate(ready):
+            quantise(late_codes[:, block_cols(n)], late_scales[:, block_cols(n)], woven)
+        for woven, bank in zip(late_woven, late_banks):
+            weave(nc.scalar.copy, woven, bank)
+        for n, woven in enumerate(late_woven, len(ready)):
+            quantise(late_codes[:, block_cols(n)], late_scales[:, block_cols(n)], woven)
+        weight_cols = [block_cols(0), block_cols(2)]
+        value_cols = [block_cols(1), block_cols(3), block_cols(4)]
+        value_codes = [codes0[:]] + [late_codes[:, cols] for cols in value_cols]
+        value_scales = [scales0[:]] + [late_scales[:, cols] for cols in value_cols]
 
         bank_tags = (("small", "mid"), ("later", "result3"))
         result = [[ps.tile([P, PAIRS, P], F32, name="result", tag=bank_tags[u][b]) for b in range(BLOCKS)] for u in range(PAIRS)]
-        order = [(j, b) for b in range(BLOCKS) for j in range(PAIRS)] + [(j, b) for j in range(PAIRS, PACK) for b in range(BLOCKS)]
-        for j, b in order:
+        first_pair = [(j, b) for b in range(BLOCKS) for j in range(PAIRS)]
+        second_pair = [(j, b) for j in range(PAIRS, PACK) for b in range(BLOCKS)]
+        for j, b in first_pair + second_pair:
             nc.tensor.matmul_mx(
                 result[j // PAIRS][b][:, j % PAIRS, :],
                 lhsT=value_codes[j].bitcast(FP8X4),

@@ -19,162 +19,148 @@ ACT = mybir.ActivationFunctionType
 
 P = 128
 PACK = 4
-PAIRS = PACK // 2
+PAIRS = 2
 BLOCKS = Q // P
-TAPS = 3
 QUADRANT = 32
-QUADRANTS = P // QUADRANT
 SCALE_ROWS = 4
 PER_COLUMN = 16
 WORDS = I // 2
-SIZE_ROWS = I // P
-WORD_BYTES = 4
-POOL_BYTES = WORD_BYTES * T
-SHARE0 = I // 2
-SHARE3 = 192
+POOL_BYTES = 4 * T
+SHARE0 = 256
+SHARE3 = 224
 FIRST_AT, LATER_AT, SIZE_AT = 4, 8, 12
-SYNC_SCALE_STORES = 1
 
 
-def block_cols(b):
+def cols(b):
     return slice(b * P, (b + 1) * P)
-
-
-def scale_partitions(quadrant):
-    return slice(QUADRANT * quadrant, QUADRANT * quadrant + SCALE_ROWS)
-
-
-def scale_rows(quadrant):
-    return slice(SCALE_ROWS * quadrant, SCALE_ROWS * (quadrant + 1))
 
 
 def tile_attend_multitoken_pl_kernel(tc, query, keys_words, keys_scales, c0, c1, c2, size, vals, offs, out_0, out_1, out_2):
     nc = tc.nc
     with ExitStack() as ctx:
         sb = ctx.enter_context(tc.tile_pool(name="sb", bufs=1))
-        shared = ctx.enter_context(tc.tile_pool(name="shared", bufs=1))
+        placed = ctx.enter_context(tc.tile_pool(name="placed", bufs=1))
         ps = ctx.enter_context(tc.psum_pool(name="ps", bufs=1))
+
+        def sbuf(name, shape, dtype, tag=""):
+            return sb.tile(shape, dtype, name=name, tag=tag or name, align_bytes=64)
+
+        def on_pool(name, shape, dtype, j, at):
+            return placed.tile(shape, dtype, name=name, offset=j * POOL_BYTES + at, align_bytes=64)
+
+        def bank(name, shape, tag):
+            return ps.tile(shape, F32, name=name, tag=tag)
 
         offsets = sb.tile([P, I // PER_COLUMN], U16, name="offsets")
         nc.sync.dma_start(offsets[:], offs)
-
-        key_bytes = sb.tile([P, T], U8, name="key_bytes", align_bytes=64)
+        key_bytes = sbuf("key_bytes", [P, T], U8)
         nc.vector.memset(key_bytes[:].bitcast(I32), 0)
-        key_words = sb.tile([P, T], U16, name="key_words", align_bytes=64)
+        key_words = sbuf("key_words", [P, T], U16)
         nc.sync.dma_start(key_words[:].bitcast(I32), keys_words[0].bitcast(I32))
+        scale_rows = keys_scales[0].rearrange("(g r) t -> r g t", r=SCALE_ROWS)
         for r in range(SCALE_ROWS):
-            nc.sync.dma_start(
-                key_bytes[r:P:QUADRANT, :].bitcast(I32),
-                keys_scales[0].rearrange("(g r) t -> r g t", r=SCALE_ROWS)[r].bitcast(I32),
-            )
-        query_raw = sb.tile([P, PACK, Q], F32, name="query_raw", align_bytes=64)
+            nc.sync.dma_start(key_bytes[r:P:QUADRANT, :].bitcast(I32), scale_rows[r].bitcast(I32))
+        query_raw = sbuf("query_raw", [P, PACK, Q], F32)
         nc.sync.dma_start(query_raw[:], query.rearrange("(p t) q -> p t q", t=PACK))
 
-        vals_rows = vals.rearrange("(m j) t -> j m t", j=PACK)
-        val_pool = [
-            shared.tile([P, T], F32, name="val_pool%d" % j, offset=j * POOL_BYTES, align_bytes=64) for j in range(PACK)
-        ]
-
-        first_rows = sb.tile([P, P], F32, name="first_rows", tag="first", align_bytes=64)
-        later_rows = sb.tile([P, P], F32, name="later_rows", align_bytes=64)
-        size_rows = sb.tile([P, P], F32, name="size_rows", align_bytes=64)
+        first_rows = sbuf("first_rows", [P, P], F32, tag="first")
+        later_rows = sbuf("later_rows", [P, P], F32)
+        size_rows = sbuf("size_rows", [P, P], F32)
         for zeroed in (first_rows, later_rows, size_rows):
             nc.gpsimd.memset(zeroed[:], 0.0)
+        vals_rows = vals.rearrange("(m j) t -> j m t", j=PACK)
+        pool = [on_pool("pool%d" % j, [P, T], F32, j, 0) for j in range(PACK)]
         nc.sync.dma_start(first_rows[FIRST_AT : FIRST_AT + BLOCKS, :], c0.rearrange("(b m) o -> b (m o)", b=BLOCKS))
-        nc.sync.dma_start(val_pool[0][:], vals_rows[0])
+        nc.sync.dma_start(pool[0][:], vals_rows[0])
         for k, source in enumerate((c1, c2)):
             row = LATER_AT + k * BLOCKS
             nc.sync.dma_start(later_rows[row : row + BLOCKS, :], source.rearrange("(b m) o -> b (m o)", b=BLOCKS))
-        nc.sync.dma_start(size_rows[SIZE_AT : SIZE_AT + SIZE_ROWS, :], size.rearrange("o (r m) -> (o r) m", r=SIZE_ROWS))
+        nc.sync.dma_start(size_rows[SIZE_AT : SIZE_AT + PACK, :], size.rearrange("o (r m) -> (o r) m", r=PACK))
         for j in range(1, PACK):
-            nc.sync.dma_start(val_pool[j][:], vals_rows[j])
+            nc.sync.dma_start(pool[j][:], vals_rows[j])
 
         identity = sb.tile([P, P], F32, name="identity")
         make_identity(nc, identity[:])
 
-        first_ps = ps.tile([P, P], F32, name="first_ps", tag="block0")
+        def listed(j, begin, end):
+            return pool[j][:].indirect(offsets[:, begin // PER_COLUMN : end // PER_COLUMN])
+
+        def turn(halves, tag):
+            turned = bank("turned", [P, PAIRS, P], tag)
+            for u in range(PAIRS):
+                nc.tensor.transpose(turned[:, u, :], halves[u], identity[:])
+            return turned
+
+        def alternate(rows_bf):
+            return [rows_bf.bitcast(F32)[:, u:WORDS:PAIRS] for u in range(PAIRS)]
+
+        def weave(copy, target, turned):
+            copy(target.rearrange("p (m u) -> p m u", u=PAIRS), turned[:].rearrange("p u m -> p m u"))
+
+        def quantise(codes, scales, values):
+            nc.vector.quantize_mx(codes.bitcast(FP8X4), scales, values)
+
+        first_ps = bank("first_ps", [P, P], "block0")
         nc.tensor.transpose(first_ps[:], first_rows[:], identity[:])
-        room0 = sb.tile([P, WORDS], F32, name="room0", align_bytes=64)
+        room0 = sbuf("room0", [P, WORDS], F32)
         first_cols = room0[:, WORDS - BLOCKS : WORDS]
         nc.scalar.copy(first_cols, first_ps[:, FIRST_AT : FIRST_AT + BLOCKS])
 
-        listed_words = sb.tile([P, I], U16, name="listed_words", align_bytes=64)
+        listed_words = sbuf("listed_words", [P, I], U16)
         nc.vector.tensor_copy(listed_words[:], key_words[:].indirect(offsets[:]))
-        listed_bytes = sb.tile([P, I], U8, name="listed_bytes", align_bytes=64)
+        listed_bytes = sbuf("listed_bytes", [P, I], U8)
         nc.vector.tensor_copy(listed_bytes[:], key_bytes[:].indirect(offsets[:]))
 
-        q_codes = sb.tile([P, Q], U32, name="q_codes", tag="first", align_bytes=64)
-        q_scales = sb.tile([P, Q], U8, name="q_scales", align_bytes=64)
-        query_bf = sb.tile([P, Q, PACK], BF16, name="query_bf", align_bytes=64)
+        q_codes = sbuf("q_codes", [P, Q], U32, tag="first")
+        q_scales = sbuf("q_scales", [P, Q], U8)
+        query_bf = sbuf("query_bf", [P, Q, PACK], BF16)
         for b in range(BLOCKS):
             nc.scalar.activation(
-                query_bf[:, block_cols(b), :].rearrange("p (c i) t -> p c t i", i=PACK),
-                query_raw[:, :, block_cols(b)].rearrange("p t (c i) -> p c t i", i=PACK),
+                query_bf[:, cols(b), :].rearrange("p (c i) t -> p c t i", i=PACK),
+                query_raw[:, :, cols(b)].rearrange("p t (c i) -> p c t i", i=PACK),
                 ACT.Copy,
             )
-            nc.vector.quantize_mx(
-                q_codes[:, block_cols(b)].bitcast(FP8X4),
-                q_scales[:, block_cols(b)],
-                query_bf[:, block_cols(b), :].rearrange("p q t -> p (q t)"),
-            )
+            quantise(q_codes[:, cols(b)], q_scales[:, cols(b)], query_bf[:, cols(b), :].rearrange("p q t -> p (q t)"))
 
-        scores = []
-        mixed = []
+        scores, mixed = [], []
         for b in range(BLOCKS):
-            score = ps.tile([P, I], F32, name="score%d" % b, tag="block%d" % b)
+            scores.append(bank("score%d" % b, [P, I], "block%d" % b))
             nc.tensor.matmul_mx(
-                score[:],
-                lhsT=q_codes[:, block_cols(b)].bitcast(FP8X4),
-                lhsT_scale=q_scales[:, block_cols(b)],
+                scores[b][:],
+                lhsT=q_codes[:, cols(b)].bitcast(FP8X4),
+                lhsT_scale=q_scales[:, cols(b)],
                 rhs=listed_words[:].bitcast(FP4X4),
                 rhs_scale=listed_bytes[:],
                 start=True,
                 stop=True,
             )
-            scores.append(score)
-            mixed.append(sb.tile([P, I], F32, name="mixed%d" % b, align_bytes=64))
-            nc.scalar.activation(mixed[b][:], score[:], ACT.Copy, scale=first_cols[:, b : b + 1])
+            mixed.append(on_pool("mixed%d" % b, [P, I], F32, PACK, b * 4 * I))
+            nc.scalar.activation(mixed[b][:], scores[b][:], ACT.Copy, scale=first_cols[:, b : b + 1])
 
-        later_ps = ps.tile([P, P], F32, name="later_ps", tag="later")
+        later_ps = bank("later_ps", [P, P], "later")
         nc.tensor.transpose(later_ps[:], later_rows[:], identity[:])
-        size_turned = ps.tile([P, P], F32, name="size_turned", tag="small")
+        size_turned = bank("size_turned", [P, P], "small")
         nc.tensor.transpose(size_turned[:], size_rows[:], identity[:])
-        size_cols = sb.tile([P, SIZE_ROWS], F32, name="size_cols", align_bytes=64)
-        nc.scalar.copy(size_cols[:], size_turned[:, SIZE_AT : SIZE_AT + SIZE_ROWS])
-
-        def turn(halves, tag):
-            bank = ps.tile([P, PAIRS, P], F32, name="turned", tag=tag)
-            for u in range(PAIRS):
-                nc.tensor.transpose(bank[:, u, :], halves[u], identity[:])
-            return bank
-
-        def alternate(rows_bf):
-            return [rows_bf.bitcast(F32)[:, u:WORDS:PAIRS] for u in range(PAIRS)]
-
-        def weave(copy, target, bank):
-            copy(target.rearrange("p (m u) -> p m u", u=PAIRS), bank[:].rearrange("p u m -> p m u"))
-
-        def listed(j, begin, end):
-            return val_pool[j][:].indirect(offsets[:, begin // PER_COLUMN : end // PER_COLUMN])
-
-        def quantise(codes, scales, woven):
-            nc.vector.quantize_mx(codes.bitcast(FP8X4), scales, woven.bitcast(BF16))
+        size_cols = sbuf("size_cols", [P, PACK], F32)
+        nc.scalar.copy(size_cols[:], size_turned[:, SIZE_AT : SIZE_AT + PACK])
 
         picked0 = room0[:].bitcast(BF16)
         nc.vector.tensor_copy(picked0[:, 0:SHARE0], listed(0, 0, SHARE0))
         nc.scalar.activation(picked0[:, SHARE0:I], listed(0, SHARE0, I), ACT.Copy)
-        bank0 = turn(alternate(picked0), "small")
-        size_ps = [ps.tile([P, SIZE_ROWS, P], F32, name="size_ps", tag="size%d" % b) for b in range(BLOCKS)]
+        turned0 = turn(alternate(picked0), "small")
+        size_ps = [bank("size_ps", [P, PAIRS, P, 2], "size%d" % b) for b in range(BLOCKS)]
         for b in range(BLOCKS):
-            for r in range(SIZE_ROWS):
-                nc.tensor.transpose(size_ps[b][:, r, :], size_cols[:, r : r + 1].to_broadcast([P, P]), identity[:])
-        picked1 = sb.tile([P, I], BF16, name="picked1", align_bytes=64)
+            for r in range(PACK):
+                dealt = size_ps[b][:].rearrange("p u (r m) e -> p r m u e", r=PACK)[:, r]
+                nc.tensor.transpose(dealt, size_cols[:, r : r + 1].to_broadcast([P, P]), identity[:])
+        picked1 = sbuf("picked1", [P, I], BF16)
         nc.scalar.activation(picked1[:], listed(1, 0, I), ACT.Copy)
-        woven01 = shared.tile([P, 2 * WORDS], F32, name="woven01", offset=POOL_BYTES + WORD_BYTES * BLOCKS * I, align_bytes=64)
+        probs = on_pool("probs", [P, BLOCKS, I], F32, 1, 0)
+        woven01 = on_pool("woven01", [P, 2 * WORDS], F32, 1, 4 * BLOCKS * I)
         woven0, woven1 = woven01[:, 0:WORDS], woven01[:, WORDS : 2 * WORDS]
-        weave(nc.scalar.copy, woven0, bank0)
+        weave(nc.scalar.copy, woven0, turned0)
 
-        for tap in range(1, TAPS):
+        for tap in (1, 2):
             for b in range(BLOCKS):
                 column = LATER_AT + (tap - 1) * BLOCKS + b
                 nc.vector.scalar_tensor_tensor(
@@ -185,73 +171,65 @@ def tile_attend_multitoken_pl_kernel(tc, query, keys_words, keys_scales, c0, c1,
                     ALU.mult,
                     ALU.add,
                 )
-        probs = shared.tile([P, BLOCKS, I], F32, name="probs", offset=POOL_BYTES, align_bytes=64)
+        spent = [on_pool("spent%d" % b, [P, P], U8, PACK, b * 4 * I) for b in range(BLOCKS)]
+        early_scales = [tile[:] for tile in spent]
         sums = [sb.tile([P, 1], F32, name="sum%d" % b) for b in range(BLOCKS)]
         inverses = [sb.tile([P, 1], F32, name="inverse%d" % b) for b in range(BLOCKS)]
         for b in range(BLOCKS):
             neg_max = sb.tile([P, 1], F32, name="neg_max%d" % b)
             nc.vector.tensor_reduce(neg_max[:], mixed[b][:], mybir.AxisListType.X, ALU.max, negate=True)
-            nc.scalar.activation(probs[:, b, :], mixed[b][:], ACT.Exp, bias=neg_max[:], accum_out=sums[b][:])
+            nc.scalar.activation(
+                probs[:, b, :].rearrange("p (u m e) -> p m u e", u=PAIRS, e=2),
+                mixed[b][:].rearrange("p (m u e) -> p m u e", u=PAIRS, e=2),
+                ACT.Exp,
+                bias=neg_max[:],
+                accum_out=sums[b][:],
+            )
 
         weave(nc.vector.tensor_copy, woven1, turn(alternate(picked1[:]), "mid"))
-        picked2 = sb.tile([P, I], BF16, name="picked2", align_bytes=64)
+        picked2 = sbuf("picked2", [P, I], BF16)
         nc.scalar.activation(picked2[:], listed(2, 0, I), ACT.Copy)
 
-        weights = [sb.tile([P, PAIRS, WORDS], BF16, name="weights%d" % b, align_bytes=64) for b in range(BLOCKS)]
+        weights = [sbuf("weights%d" % b, [P, PAIRS, WORDS], BF16) for b in range(BLOCKS)]
 
-        def weigh(b, u):
-            pair = slice(2 * u, 2 * u + 2)
+        early_codes = sbuf("early_codes", [P, BLOCKS * P], U32)
+        for b, woven in enumerate((woven0, woven1)):
+            nc.vector.reciprocal(inverses[b][:], sums[b][:])
+            quantise(early_codes[:, cols(b)], early_scales[b], woven.bitcast(BF16))
             nc.vector.scalar_tensor_tensor(
-                weights[b][:, u, :].rearrange("p (m e) -> p m e", e=2),
-                probs[:, b, :].rearrange("p (m t) -> p m t", t=PACK)[:, :, pair],
+                weights[b][:].rearrange("p u w -> p (u w)"),
+                probs[:, b, :],
                 inverses[b][:],
-                size_ps[b][:].rearrange("p r (m t) -> p (r m) t", t=PACK)[:, :, pair],
+                size_ps[b][:].rearrange("p u m e -> p (u m e)"),
                 ALU.mult,
                 ALU.mult,
             )
 
-        codes0 = sb.tile([P, P], U32, name="codes0", align_bytes=64)
-        scales0 = sb.tile([P, P], U8, name="scales0", align_bytes=64)
-        nc.vector.reciprocal(inverses[0][:], sums[0][:])
-        quantise(codes0[:], scales0[:], woven0)
-        weigh(0, 0)
-        nc.vector.reciprocal(inverses[1][:], sums[1][:])
-        weigh(0, 1)
-        weigh(1, 0)
-        weigh(1, 1)
-
-        weight_halves = [[weights[b][:, u, :].bitcast(F32) for u in range(PAIRS)] for b in range(BLOCKS)]
-        bank_w0 = turn(weight_halves[0], "block0")
-        bank2 = turn(alternate(picked2[:]), "size0")
-        bank_w1 = turn(weight_halves[1], "block1")
-        woven_w0 = sb.tile([P, WORDS], F32, name="woven_w0", align_bytes=64)
-        weave(nc.vector.tensor_copy, woven_w0[:], bank_w0)
-        picked3 = sb.tile([P, I], BF16, name="picked3", align_bytes=64)
+        halves = [[weights[b][:, u, :].bitcast(F32) for u in range(PAIRS)] for b in range(BLOCKS)]
+        turned_w0 = turn(halves[0], "block0")
+        turned2 = turn(alternate(picked2[:]), "size0")
+        turned_w1 = turn(halves[1], "block1")
+        picked3 = sbuf("picked3", [P, I], BF16)
         nc.vector.tensor_copy(picked3[:, 0:SHARE3], listed(3, 0, SHARE3))
         nc.scalar.activation(picked3[:, SHARE3:I], listed(3, SHARE3, I), ACT.Copy)
-        bank3 = turn(alternate(picked3[:]), "size1")
+        turned3 = turn(alternate(picked3[:]), "size1")
 
-        late_banks = (bank_w1, bank2, bank3)
-        late = shared.tile([P, len(late_banks) * WORDS], F32, name="late", offset=3 * POOL_BYTES, align_bytes=64)
-        late_woven = [late[:, n * WORDS : (n + 1) * WORDS] for n in range(len(late_banks))]
-        ready = [woven_w0[:], woven1]
-        blocks = len(ready) + len(late_banks)
-        codes_at = 3 * POOL_BYTES + WORD_BYTES * len(late_banks) * WORDS
-        late_codes = shared.tile([P, blocks * P], U32, name="late_codes", offset=codes_at, align_bytes=64)
-        late_scales = sb.tile([P, blocks * P], U8, name="late_scales", align_bytes=64)
-        for n, woven in enumerate(ready):
-            quantise(late_codes[:, block_cols(n)], late_scales[:, block_cols(n)], woven)
-        for woven, bank in zip(late_woven, late_banks):
-            weave(nc.scalar.copy, woven, bank)
-        for n, woven in enumerate(late_woven, len(ready)):
-            quantise(late_codes[:, block_cols(n)], late_scales[:, block_cols(n)], woven)
-        weight_cols = [block_cols(0), block_cols(2)]
-        value_cols = [block_cols(1), block_cols(3), block_cols(4)]
-        value_codes = [codes0[:]] + [late_codes[:, cols] for cols in value_cols]
-        value_scales = [scales0[:]] + [late_scales[:, cols] for cols in value_cols]
+        late_turned = (turned_w0, turned_w1, turned2, turned3)
+        late = on_pool("late", [P, 4 * WORDS], F32, 3, 0)
+        late_woven = [late[:, n * WORDS : (n + 1) * WORDS] for n in range(4)]
+        late_codes = on_pool("late_codes", [P, 4 * P], U32, 3, 4 * 4 * WORDS)
+        late_scales = sbuf("late_scales", [P, 4 * P], U8)
+        for woven, turned in zip(late_woven, late_turned):
+            weave(nc.scalar.copy, woven, turned)
+        for n, woven in enumerate(late_woven):
+            quantise(late_codes[:, cols(n)], late_scales[:, cols(n)], woven.bitcast(BF16))
+        weight_codes = [late_codes[:, cols(n)] for n in (0, 1)]
+        weight_scales = [late_scales[:, cols(n)] for n in (0, 1)]
+        value_codes = [early_codes[:, cols(n)] for n in (0, 1)] + [late_codes[:, cols(n)] for n in (2, 3)]
+        value_scales = early_scales + [late_scales[:, cols(n)] for n in (2, 3)]
 
-        bank_tags = (("small", "mid"), ("later", "result3"))
-        result = [[ps.tile([P, PAIRS, P], F32, name="result", tag=bank_tags[u][b]) for b in range(BLOCKS)] for u in range(PAIRS)]
+        tags = (("small", "mid"), ("later", "result3"))
+        result = [[bank("result", [P, PAIRS, P], tags[u][b]) for b in range(BLOCKS)] for u in range(PAIRS)]
         first_pair = [(j, b) for b in range(BLOCKS) for j in range(PAIRS)]
         second_pair = [(j, b) for j in range(PAIRS, PACK) for b in range(BLOCKS)]
         for j, b in first_pair + second_pair:
@@ -259,36 +237,32 @@ def tile_attend_multitoken_pl_kernel(tc, query, keys_words, keys_scales, c0, c1,
                 result[j // PAIRS][b][:, j % PAIRS, :],
                 lhsT=value_codes[j].bitcast(FP8X4),
                 lhsT_scale=value_scales[j],
-                rhs=late_codes[:, weight_cols[b]].bitcast(FP8X4),
-                rhs_scale=late_scales[:, weight_cols[b]],
+                rhs=weight_codes[b].bitcast(FP8X4),
+                rhs_scale=weight_scales[b],
                 start=True,
                 stop=True,
             )
 
         copies = (nc.scalar.copy, nc.vector.tensor_copy)
         out_rows = out_0.rearrange("(p j) q -> p j q", j=PACK)
-        out_bf = sb.tile([P, Q, PACK], BF16, name="out_bf", align_bytes=64)
-        rows = [sb.tile([P, PAIRS, Q], F32, name="rows%d" % u, align_bytes=64) for u in range(PAIRS)]
+        out_bf = sbuf("out_bf", [P, Q, PACK], BF16)
+        rows = [sbuf("rows%d" % u, [P, PAIRS, Q], F32) for u in range(PAIRS)]
         for u in range(PAIRS):
             places = slice(PAIRS * u, PAIRS * (u + 1))
             for b in range(BLOCKS):
-                copies[b](rows[u][:, :, block_cols(b)], result[u][b][:])
+                copies[b](rows[u][:, :, cols(b)], result[u][b][:])
             nc.sync.dma_start(out_rows[:, places, :], rows[u][:])
             for b in range(BLOCKS):
-                copies[b](out_bf[:, block_cols(b), places], result[u][b][:].rearrange("p j n -> p n j"))
+                copies[b](out_bf[:, cols(b), places], result[u][b][:].rearrange("p j n -> p n j"))
 
-        out_codes = sb.tile([P, Q], U32, name="out_codes", align_bytes=64)
-        out_scales = sb.tile([P, Q], U8, name="out_scales", align_bytes=64)
+        out_codes = sbuf("out_codes", [P, Q], U32)
+        out_scales = sbuf("out_scales", [P, Q], U8)
         for b in range(BLOCKS):
-            nc.vector.quantize_mx(
-                out_codes[:, block_cols(b)].bitcast(FP8X4),
-                out_scales[:, block_cols(b)],
-                out_bf[:, block_cols(b), :].rearrange("p q j -> p (q j)"),
-            )
+            quantise(out_codes[:, cols(b)], out_scales[:, cols(b)], out_bf[:, cols(b), :].rearrange("p q j -> p (q j)"))
         nc.sync.dma_start(out_1[0].rearrange("p c r -> p (c r)").bitcast(I32), out_codes[:].bitcast(I32))
-        for quadrant in range(QUADRANTS):
-            queue = nc.sync if quadrant < SYNC_SCALE_STORES else nc.scalar
+        for g in range(P // QUADRANT):
+            queue = nc.sync if g < 1 else nc.scalar
             queue.dma_start(
-                out_2[0, scale_rows(quadrant), :].bitcast(I32),
-                out_scales[scale_partitions(quadrant), :].bitcast(I32),
+                out_2[0, SCALE_ROWS * g : SCALE_ROWS * (g + 1), :].bitcast(I32),
+                out_scales[QUADRANT * g : QUADRANT * g + SCALE_ROWS, :].bitcast(I32),
             )

@@ -27,7 +27,7 @@ PER_COLUMN = 16
 WORDS = I // 2
 POOL_BYTES = 4 * T
 SHARE0 = 256
-SHARE3 = 224
+SHARE3 = 256
 FIRST_AT, LATER_AT, SIZE_AT = 4, 8, 12
 
 
@@ -148,11 +148,10 @@ def tile_attend_multitoken_pl_kernel(tc, query, keys_words, keys_scales, c0, c1,
         nc.vector.tensor_copy(picked0[:, 0:SHARE0], listed(0, 0, SHARE0))
         nc.scalar.activation(picked0[:, SHARE0:I], listed(0, SHARE0, I), ACT.Copy)
         turned0 = turn(alternate(picked0), "small")
-        size_ps = [bank("size_ps", [P, PAIRS, P, 2], "size%d" % b) for b in range(BLOCKS)]
-        for b in range(BLOCKS):
-            for r in range(PACK):
-                dealt = size_ps[b][:].rearrange("p u (r m) e -> p r m u e", r=PACK)[:, r]
-                nc.tensor.transpose(dealt, size_cols[:, r : r + 1].to_broadcast([P, P]), identity[:])
+        size_ps = bank("size_ps", [P, PAIRS, P, 2], "size")
+        for r in range(PACK):
+            dealt = size_ps[:].rearrange("p u (r m) e -> p r m u e", r=PACK)[:, r]
+            nc.tensor.transpose(dealt, size_cols[:, r : r + 1].to_broadcast([P, P]), identity[:])
         picked1 = sbuf("picked1", [P, I], BF16)
         nc.scalar.activation(picked1[:], listed(1, 0, I), ACT.Copy)
         probs = on_pool("probs", [P, BLOCKS, I], F32, 1, 0)
@@ -192,27 +191,29 @@ def tile_attend_multitoken_pl_kernel(tc, query, keys_words, keys_scales, c0, c1,
 
         weights = [sbuf("weights%d" % b, [P, PAIRS, WORDS], BF16) for b in range(BLOCKS)]
 
+        pieces = (((0, I),), ((0, WORDS), (WORDS, I)))
         early_codes = sbuf("early_codes", [P, BLOCKS * P], U32)
         for b, woven in enumerate((woven0, woven1)):
             nc.vector.reciprocal(inverses[b][:], sums[b][:])
             quantise(early_codes[:, cols(b)], early_scales[b], woven.bitcast(BF16))
-            nc.vector.scalar_tensor_tensor(
-                weights[b][:].rearrange("p u w -> p (u w)"),
-                probs[:, b, :],
-                inverses[b][:],
-                size_ps[b][:].rearrange("p u m e -> p (u m e)"),
-                ALU.mult,
-                ALU.mult,
-            )
+            for begin, end in pieces[b]:
+                nc.vector.scalar_tensor_tensor(
+                    weights[b][:].rearrange("p u w -> p (u w)")[:, begin:end],
+                    probs[:, b, begin:end],
+                    inverses[b][:],
+                    size_ps[:].rearrange("p u m e -> p (u m e)")[:, begin:end],
+                    ALU.mult,
+                    ALU.mult,
+                )
 
         halves = [[weights[b][:, u, :].bitcast(F32) for u in range(PAIRS)] for b in range(BLOCKS)]
         turned_w0 = turn(halves[0], "block0")
-        turned2 = turn(alternate(picked2[:]), "size0")
         turned_w1 = turn(halves[1], "block1")
+        turned2 = turn(alternate(picked2[:]), "tile2")
         picked3 = sbuf("picked3", [P, I], BF16)
         nc.vector.tensor_copy(picked3[:, 0:SHARE3], listed(3, 0, SHARE3))
         nc.scalar.activation(picked3[:, SHARE3:I], listed(3, SHARE3, I), ACT.Copy)
-        turned3 = turn(alternate(picked3[:]), "size1")
+        turned3 = turn(alternate(picked3[:]), "size")
 
         late_turned = (turned_w0, turned_w1, turned2, turned3)
         late = on_pool("late", [P, 4 * WORDS], F32, 3, 0)
@@ -259,9 +260,9 @@ def tile_attend_multitoken_pl_kernel(tc, query, keys_words, keys_scales, c0, c1,
         out_scales = sbuf("out_scales", [P, Q], U8)
         for b in range(BLOCKS):
             quantise(out_codes[:, cols(b)], out_scales[:, cols(b)], out_bf[:, cols(b), :].rearrange("p q j -> p (q j)"))
-        nc.sync.dma_start(out_1[0].rearrange("p c r -> p (c r)").bitcast(I32), out_codes[:].bitcast(I32))
+            nc.sync.dma_start(out_1[0].rearrange("p c r -> p (c r)").bitcast(I32)[:, cols(b)], out_codes[:, cols(b)].bitcast(I32))
         for g in range(P // QUADRANT):
-            queue = nc.sync if g < 1 else nc.scalar
+            queue = nc.sync if g < 2 else nc.scalar
             queue.dma_start(
                 out_2[0, SCALE_ROWS * g : SCALE_ROWS * (g + 1), :].bitcast(I32),
                 out_scales[QUADRANT * g : QUADRANT * g + SCALE_ROWS, :].bitcast(I32),

@@ -260,7 +260,7 @@ def tile_attend_multitoken_pl_kernel(tc, query, keys_words, keys_scales, c0, c1,
         out_scales = sbuf("out_scales", [P, Q], U8)
         for b in range(BLOCKS):
             quantise(out_codes[:, cols(b)], out_scales[:, cols(b)], out_bf[:, cols(b), :].rearrange("p q j -> p (q j)"))
-            nc.sync.dma_start(out_1[0].rearrange("p c r -> p (c r)").bitcast(I32)[:, cols(b)], out_codes[:, cols(b)].bitcast(I32))
+        nc.sync.dma_start(out_1[0].rearrange("p c r -> p (c r)").bitcast(I32), out_codes[:].bitcast(I32))
         for g in range(P // QUADRANT):
             queue = nc.sync if g < 2 else nc.scalar
             queue.dma_start(

@@ -262,8 +262,7 @@ def tile_attend_multitoken_pl_kernel(tc, query, keys_words, keys_scales, c0, c1,
             quantise(out_codes[:, cols(b)], out_scales[:, cols(b)], out_bf[:, cols(b), :].rearrange("p q j -> p (q j)"))
         nc.sync.dma_start(out_1[0].rearrange("p c r -> p (c r)").bitcast(I32), out_codes[:].bitcast(I32))
         for g in range(P // QUADRANT):
-            queue = nc.sync if g < 2 else nc.scalar
-            queue.dma_start(
+            nc.sync.dma_start(
                 out_2[0, SCALE_ROWS * g : SCALE_ROWS * (g + 1), :].bitcast(I32),
                 out_scales[QUADRANT * g : QUADRANT * g + SCALE_ROWS, :].bitcast(I32),
             )

@@ -52,11 +52,11 @@ def tile_attend_multitoken_pl_kernel(tc, query, keys_words, keys_scales, c0, c1,
             return ps.tile(shape, F32, name=name, tag=tag)
 
         offsets = sb.tile([P, I // PER_COLUMN], U16, name="offsets")
-        nc.sync.dma_start(offsets[:], offs)
         key_bytes = sbuf("key_bytes", [P, T], U8)
         nc.vector.memset(key_bytes[:].bitcast(I32), 0)
         key_words = sbuf("key_words", [P, T], U16)
         nc.sync.dma_start(key_words[:].bitcast(I32), keys_words[0].bitcast(I32))
+        nc.sync.dma_start(offsets[:], offs)
         scale_rows = keys_scales[0].rearrange("(g r) t -> r g t", r=SCALE_ROWS)
         for r in range(SCALE_ROWS):
             nc.sync.dma_start(key_bytes[r:P:QUADRANT, :].bitcast(I32), scale_rows[r].bitcast(I32))

from contextlib import ExitStack

import concourse.mybir as mybir
from concourse.masks import make_identity

D, T, I, Q, E = 512, 2048, 512, 256, 512
FLOPS = 2 * D * Q * I + 2 * I * E * Q

F32 = mybir.dt.float32
BF16 = mybir.dt.bfloat16
I32 = mybir.dt.int32
U32 = mybir.dt.uint32
U16 = mybir.dt.uint16
U8 = mybir.dt.uint8
FP8X4 = mybir.dt.float8_e4m3fn_x4
FP4X4 = mybir.dt.float4_e2m1fn_x4
ALU = mybir.AluOpType
ACT = mybir.ActivationFunctionType

P = 128
PACK = 4
PAIRS = 2
BLOCKS = Q // P
QUADRANT = 32
SCALE_ROWS = 4
PER_COLUMN = 16
WORDS = I // 2
POOL_BYTES = 4 * T
SHARE0 = 256
SHARE3 = 256
FIRST_AT, LATER_AT, SIZE_AT = 4, 8, 12


def cols(b):
    return slice(b * P, (b + 1) * P)


def tile_attend_multitoken_pl_kernel(tc, query, keys_words, keys_scales, c0, c1, c2, size, vals, offs, out_0, out_1, out_2):
    nc = tc.nc
    with ExitStack() as ctx:
        sb = ctx.enter_context(tc.tile_pool(name="sb", bufs=1))
        placed = ctx.enter_context(tc.tile_pool(name="placed", bufs=1))
        ps = ctx.enter_context(tc.psum_pool(name="ps", bufs=1))

        def sbuf(name, shape, dtype, tag=""):
            return sb.tile(shape, dtype, name=name, tag=tag or name, align_bytes=64)

        def on_pool(name, shape, dtype, j, at):
            return placed.tile(shape, dtype, name=name, offset=j * POOL_BYTES + at, align_bytes=64)

        def bank(name, shape, tag):
            return ps.tile(shape, F32, name=name, tag=tag)

        offsets = sb.tile([P, I // PER_COLUMN], U16, name="offsets")
        key_bytes = sbuf("key_bytes", [P, T], U8)
        nc.vector.memset(key_bytes[:].bitcast(I32), 0)
        key_words = sbuf("key_words", [P, T], U16)
        nc.sync.dma_start(key_words[:].bitcast(I32), keys_words[0].bitcast(I32))
        nc.sync.dma_start(offsets[:], offs)
        scale_rows = keys_scales[0].rearrange("(g r) t -> r g t", r=SCALE_ROWS)
        for r in range(SCALE_ROWS):
            nc.sync.dma_start(key_bytes[r:P:QUADRANT, :].bitcast(I32), scale_rows[r].bitcast(I32))
        query_raw = sbuf("query_raw", [P, PACK, Q], F32)
        nc.sync.dma_start(query_raw[:], query.rearrange("(p t) q -> p t q", t=PACK))

        first_rows = sbuf("first_rows", [P, P], F32, tag="first")
        later_rows = sbuf("later_rows", [P, P], F32)
        size_rows = sbuf("size_rows", [P, P], F32)
        for zeroed in (first_rows, later_rows, size_rows):
            nc.gpsimd.memset(zeroed[:], 0.0)
        vals_rows = vals.rearrange("(m j) t -> j m t", j=PACK)
        pool = [on_pool("pool%d" % j, [P, T], F32, j, 0) for j in range(PACK)]
        nc.sync.dma_start(first_rows[FIRST_AT : FIRST_AT + BLOCKS, :], c0.rearrange("(b m) o -> b (m o)", b=BLOCKS))
        nc.sync.dma_start(pool[0][:], vals_rows[0])
        for k, source in enumerate((c1, c2)):
            row = LATER_AT + k * BLOCKS
            nc.sync.dma_start(later_rows[row : row + BLOCKS, :], source.rearrange("(b m) o -> b (m o)", b=BLOCKS))
        nc.sync.dma_start(size_rows[SIZE_AT : SIZE_AT + PACK, :], size.rearrange("o (r m) -> (o r) m", r=PACK))
        for j in range(1, PACK):
            nc.sync.dma_start(pool[j][:], vals_rows[j])

        identity = sb.tile([P, P], F32, name="identity")
        make_identity(nc, identity[:])

        def listed(j, begin, end):
            return pool[j][:].indirect(offsets[:, begin // PER_COLUMN : end // PER_COLUMN])

        def turn(halves, tag):
            turned = bank("turned", [P, PAIRS, P], tag)
            for u in range(PAIRS):
                nc.tensor.transpose(turned[:, u, :], halves[u], identity[:])
            return turned

        def alternate(rows_bf):
            return [rows_bf.bitcast(F32)[:, u:WORDS:PAIRS] for u in range(PAIRS)]

        def weave(copy, target, turned):
            copy(target.rearrange("p (m u) -> p m u", u=PAIRS), turned[:].rearrange("p u m -> p m u"))

        def quantise(codes, scales, values):
            nc.vector.quantize_mx(codes.bitcast(FP8X4), scales, values)

        first_ps = bank("first_ps", [P, P], "block0")
        nc.tensor.transpose(first_ps[:], first_rows[:], identity[:])
        room0 = sbuf("room0", [P, WORDS], F32)
        first_cols = room0[:, WORDS - BLOCKS : WORDS]
        nc.scalar.copy(first_cols, first_ps[:, FIRST_AT : FIRST_AT + BLOCKS])

        listed_words = sbuf("listed_words", [P, I], U16)
        nc.vector.tensor_copy(listed_words[:], key_words[:].indirect(offsets[:]))
        listed_bytes = sbuf("listed_bytes", [P, I], U8)
        nc.vector.tensor_copy(listed_bytes[:], key_bytes[:].indirect(offsets[:]))

        q_codes = sbuf("q_codes", [P, Q], U32, tag="first")
        q_scales = sbuf("q_scales", [P, Q], U8)
        query_bf = sbuf("query_bf", [P, Q, PACK], BF16)
        for b in range(BLOCKS):
            nc.scalar.activation(
                query_bf[:, cols(b), :].rearrange("p (c i) t -> p c t i", i=PACK),
                query_raw[:, :, cols(b)].rearrange("p t (c i) -> p c t i", i=PACK),
                ACT.Copy,
            )
            quantise(q_codes[:, cols(b)], q_scales[:, cols(b)], query_bf[:, cols(b), :].rearrange("p q t -> p (q t)"))

        scores, mixed = [], []
        for b in range(BLOCKS):
            scores.append(bank("score%d" % b, [P, I], "block%d" % b))
            nc.tensor.matmul_mx(
                scores[b][:],
                lhsT=q_codes[:, cols(b)].bitcast(FP8X4),
                lhsT_scale=q_scales[:, cols(b)],
                rhs=listed_words[:].bitcast(FP4X4),
                rhs_scale=listed_bytes[:],
                start=True,
                stop=True,
            )
            mixed.append(on_pool("mixed%d" % b, [P, I], F32, PACK, b * 4 * I))
            nc.scalar.activation(mixed[b][:], scores[b][:], ACT.Copy, scale=first_cols[:, b : b + 1])

        later_ps = bank("later_ps", [P, P], "later")
        nc.tensor.transpose(later_ps[:], later_rows[:], identity[:])
        size_turned = bank("size_turned", [P, P], "small")
        nc.tensor.transpose(size_turned[:], size_rows[:], identity[:])
        size_cols = sbuf("size_cols", [P, PACK], F32)
        nc.scalar.copy(size_cols[:], size_turned[:, SIZE_AT : SIZE_AT + PACK])

        picked0 = room0[:].bitcast(BF16)
        nc.vector.tensor_copy(picked0[:, 0:SHARE0], listed(0, 0, SHARE0))
        nc.scalar.activation(picked0[:, SHARE0:I], listed(0, SHARE0, I), ACT.Copy)
        turned0 = turn(alternate(picked0), "small")
        size_ps = bank("size_ps", [P, PAIRS, P, 2], "size")
        for r in range(PACK):
            dealt = size_ps[:].rearrange("p u (r m) e -> p r m u e", r=PACK)[:, r]
            nc.tensor.transpose(dealt, size_cols[:, r : r + 1].to_broadcast([P, P]), identity[:])
        picked1 = sbuf("picked1", [P, I], BF16)
        nc.scalar.activation(picked1[:], listed(1, 0, I), ACT.Copy)
        probs = on_pool("probs", [P, BLOCKS, I], F32, 1, 0)
        woven01 = on_pool("woven01", [P, 2 * WORDS], F32, 1, 4 * BLOCKS * I)
        woven0, woven1 = woven01[:, 0:WORDS], woven01[:, WORDS : 2 * WORDS]
        weave(nc.scalar.copy, woven0, turned0)

        for tap in (1, 2):
            for b in range(BLOCKS):
                column = LATER_AT + (tap - 1) * BLOCKS + b
                nc.vector.scalar_tensor_tensor(
                    mixed[b][:, tap:I],
                    scores[b][:, 0 : I - tap],
                    later_ps[:, column : column + 1],
                    mixed[b][:, tap:I],
                    ALU.mult,
                    ALU.add,
                )
        spent = [on_pool("spent%d" % b, [P, P], U8, PACK, b * 4 * I) for b in range(BLOCKS)]
        early_scales = [tile[:] for tile in spent]
        sums = [sb.tile([P, 1], F32, name="sum%d" % b) for b in range(BLOCKS)]
        inverses = [sb.tile([P, 1], F32, name="inverse%d" % b) for b in range(BLOCKS)]
        for b in range(BLOCKS):
            neg_max = sb.tile([P, 1], F32, name="neg_max%d" % b)
            nc.vector.tensor_reduce(neg_max[:], mixed[b][:], mybir.AxisListType.X, ALU.max, negate=True)
            nc.scalar.activation(
                probs[:, b, :].rearrange("p (u m e) -> p m u e", u=PAIRS, e=2),
                mixed[b][:].rearrange("p (m u e) -> p m u e", u=PAIRS, e=2),
                ACT.Exp,
                bias=neg_max[:],
                accum_out=sums[b][:],
            )

        weave(nc.vector.tensor_copy, woven1, turn(alternate(picked1[:]), "mid"))
        picked2 = sbuf("picked2", [P, I], BF16)
        nc.scalar.activation(picked2[:], listed(2, 0, I), ACT.Copy)

        weights = [sbuf("weights%d" % b, [P, PAIRS, WORDS], BF16) for b in range(BLOCKS)]

        pieces = (((0, I),), ((0, WORDS), (WORDS, I)))
        early_codes = sbuf("early_codes", [P, BLOCKS * P], U32)
        for b, woven in enumerate((woven0, woven1)):
            nc.vector.reciprocal(inverses[b][:], sums[b][:])
            quantise(early_codes[:, cols(b)], early_scales[b], woven.bitcast(BF16))
            for begin, end in pieces[b]:
                nc.vector.scalar_tensor_tensor(
                    weights[b][:].rearrange("p u w -> p (u w)")[:, begin:end],
                    probs[:, b, begin:end],
                    inverses[b][:],
                    size_ps[:].rearrange("p u m e -> p (u m e)")[:, begin:end],
                    ALU.mult,
                    ALU.mult,
                )

        halves = [[weights[b][:, u, :].bitcast(F32) for u in range(PAIRS)] for b in range(BLOCKS)]
        turned_w0 = turn(halves[0], "block0")
        turned_w1 = turn(halves[1], "block1")
        turned2 = turn(alternate(picked2[:]), "tile2")
        picked3 = sbuf("picked3", [P, I], BF16)
        nc.vector.tensor_copy(picked3[:, 0:SHARE3], listed(3, 0, SHARE3))
        nc.scalar.activation(picked3[:, SHARE3:I], listed(3, SHARE3, I), ACT.Copy)
        turned3 = turn(alternate(picked3[:]), "size")

        late_turned = (turned_w0, turned_w1, turned2, turned3)
        late = on_pool("late", [P, 4 * WORDS], F32, 3, 0)
        late_woven = [late[:, n * WORDS : (n + 1) * WORDS] for n in range(4)]
        late_codes = on_pool("late_codes", [P, 4 * P], U32, 3, 4 * 4 * WORDS)
        late_scales = sbuf("late_scales", [P, 4 * P], U8)
        for woven, turned in zip(late_woven, late_turned):
            weave(nc.scalar.copy, woven, turned)
        for n, woven in enumerate(late_woven):
            quantise(late_codes[:, cols(n)], late_scales[:, cols(n)], woven.bitcast(BF16))
        weight_codes = [late_codes[:, cols(n)] for n in (0, 1)]
        weight_scales = [late_scales[:, cols(n)] for n in (0, 1)]
        value_codes = [early_codes[:, cols(n)] for n in (0, 1)] + [late_codes[:, cols(n)] for n in (2, 3)]
        value_scales = early_scales + [late_scales[:, cols(n)] for n in (2, 3)]

        tags = (("small", "mid"), ("later", "result3"))
        result = [[bank("result", [P, PAIRS, P], tags[u][b]) for b in range(BLOCKS)] for u in range(PAIRS)]
        first_pair = [(j, b) for b in range(BLOCKS) for j in range(PAIRS)]
        second_pair = [(j, b) for j in range(PAIRS, PACK) for b in range(BLOCKS)]
        for j, b in first_pair + second_pair:
            nc.tensor.matmul_mx(
                result[j // PAIRS][b][:, j % PAIRS, :],
                lhsT=value_codes[j].bitcast(FP8X4),
                lhsT_scale=value_scales[j],
                rhs=weight_codes[b].bitcast(FP8X4),
                rhs_scale=weight_scales[b],
                start=True,
                stop=True,
            )

        copies = (nc.scalar.copy, nc.vector.tensor_copy)
        out_rows = out_0.rearrange("(p j) q -> p j q", j=PACK)
        out_bf = sbuf("out_bf", [P, Q, PACK], BF16)
        rows = [sbuf("rows%d" % u, [P, PAIRS, Q], F32) for u in range(PAIRS)]
        for u in range(PAIRS):
            places = slice(PAIRS * u, PAIRS * (u + 1))
            for b in range(BLOCKS):
                copies[b](rows[u][:, :, cols(b)], result[u][b][:])
            nc.sync.dma_start(out_rows[:, places, :], rows[u][:])
            for b in range(BLOCKS):
                copies[b](out_bf[:, cols(b), places], result[u][b][:].rearrange("p j n -> p n j"))

        out_codes = sbuf("out_codes", [P, Q], U32)
        out_scales = sbuf("out_scales", [P, Q], U8)
        for b in range(BLOCKS):
            quantise(out_codes[:, cols(b)], out_scales[:, cols(b)], out_bf[:, cols(b), :].rearrange("p q j -> p (q j)"))
        nc.sync.dma_start(out_1[0].rearrange("p c r -> p (c r)").bitcast(I32), out_codes[:].bitcast(I32))
        for g in range(P // QUADRANT):
            nc.sync.dma_start(
                out_2[0, SCALE_ROWS * g : SCALE_ROWS * (g + 1), :].bitcast(I32),
                out_scales[QUADRANT * g : QUADRANT * g + SCALE_ROWS, :].bitcast(I32),
            )
